import numpy as np, ml_dtypes
CORES = [16,18,20,22]
N = 4
import mx_ref
BF = ml_dtypes.bfloat16
def gcols(t, e):
    v = np.concatenate([t.reshape(8, 16, -1, 4), np.zeros((8, 16, 1, 4), BF)], axis=2)
    return np.ascontiguousarray(np.stack([v[g][:, e[g]] for g in range(8)])).reshape(128, -1)
def gpick(z, e):
    return np.concatenate([z[16 * g:16 * g + 16][:, e[g]] for g in range(8)])
def tile(rs):
    return np.stack(rs, axis=2).reshape(128, -1).astype(BF)
def pick(q, e):
    c = np.concatenate([q[0].reshape(128, -1, 4), np.zeros((128, 1, 4), np.uint8)], axis=1); s = np.concatenate([q[1], np.ones((16, 1), np.uint8)], axis=1)
    return (np.ascontiguousarray(c[:, e].reshape(128, -1)), np.ascontiguousarray(s[:, e]))
def join(*qs):
    return (np.concatenate([q[0] for q in qs], axis=1), np.concatenate([q[1] for q in qs], axis=1))
def put(q, e, v):
    c, s = q[0].reshape(128, -1, 4).copy(), q[1].copy(); c[:, e] = v[0].reshape(128, -1, 4); s[:, e] = v[1]
    return (c.reshape(128, -1), s)
def pk(c, s):
    return (np.ascontiguousarray(c), mx_ref.live(s))
def emit(q):
    return q[0], q[1]
def packed(v, rng):
    q = [mx_ref.quantize(np.ascontiguousarray(v[r])) for r in range(N)]
    return np.stack([a for a, b in q]), np.stack([mx_ref.plane(b, rng) for a, b in q])
def values_of_codes():
    e, c = np.zeros((128, 128, 4), np.float32), np.zeros((128, 2, 4), np.uint8)
    e[np.arange(128), np.arange(128), 0] = 1
    c[:127, :, 0] = np.arange(256).reshape(2, 128).T[:127]
    return mx_ref.matmul(mx_ref.quantize(e.reshape(128, 512).astype(BF)), (c.reshape(128, 8), np.full((16, 2), 127, np.uint8))).T.reshape(-1).astype(np.float64)
CODE_VALUE, SCALE_VALUE = values_of_codes(), 2.0 ** (np.arange(256) - 127.0)
def decode(q):
    return (CODE_VALUE[q[0]].reshape(16, 8, -1, 4) * SCALE_VALUE[q[1]][:, None, :, None] + 0.0).reshape(128, -1).astype(np.float32)
def f(rng, *shape):
    return mx_ref.flush((rng.standard_normal(shape, dtype=np.float32) * np.exp2(rng.integers(-2, 3, shape[:-1] + (1,)))).astype(BF))
def wide(rng, *shape, cols=0):
    v = rng.standard_normal(shape, dtype=np.float32) * np.exp2(rng.integers(-12, 13, shape)).astype(np.float32)
    if cols: v *= np.repeat(np.exp2(rng.integers(-cols, cols + 1, shape[:-2] + (1, shape[-1] // 4))) * (rng.random(shape[:-2] + (1, shape[-1] // 4)) > 0.0625), 4, axis=-1).astype(np.float32)
    return mx_ref.flush(v.astype(BF))
C, H, E, K, J, R = 320, 96, 416, 128, 2, 2
def big(v):
    v = v.astype(np.float32)
    v[np.abs(v) < np.float32(2.0 ** -16)] = 0
    return v.astype(BF)
def numbers_of(rng):
    return {"x": big(f(rng, N, 128, 4 * C)), "u": np.array(f(rng, N, 128, 512)), "v": np.array(f(rng, N, 128, 512))}
def layers(rng):
    return big(f(rng, N, 128, 2048)).reshape(N, 8, 16, 4, 8, 16, 4)
def weights(rng, w):
    c, p = packed(np.ascontiguousarray(w).reshape(N, 128, 2048), rng)
    return {"wc": c, "ws": p}
def setup_inputs(rng):
    return {**numbers_of(rng), **weights(rng, layers(rng))}
def setup_inputs_ties(rng):
    d = numbers_of(rng)
    x = d["x"].reshape(N, 8, 16, C, 4)
    x[:, :, 0] = 0
    x[:, :, 0, :, 0] = rng.integers(0, 3, (N, 8, C)).astype(np.float32).astype(BF)
    u = d["u"].reshape(N, 128, 128, 4)
    u[:, :, ::16] = 0
    o = rng.permutation(N)
    for r in range(N):
        for h in range(0, 128, 16): u[r, h, h, 0] = 0.0 if r == o[0] else -1.0 if r == o[1] else 1.0
    w = layers(rng)
    w[:, :, :, :, :, 0] = 0
    return {"x": x.reshape(N, 128, 4 * C), "u": u.reshape(N, 128, 512), "v": d["v"], **weights(rng, w)}
def setup_inputs_near(rng):
    d = numbers_of(rng)
    x = d["x"].astype(np.float32).reshape(N, 8, 16, C, 4)
    u = d["u"].reshape(N, 128, 128, 4)
    o = rng.permutation(N) % 4
    x[:, :, :2] = 0
    x[:, :, 8:] = 0
    x[:, :, 0, :, 0] = 1
    u[:, :, ::16] = 0
    for r in range(N):
        s = rng.integers(0, 16, (8, C))
        low = rng.permutation(8)[:4]
        if o[r] == 3: s[low] = s[low] % 4
        x[r, :, 8] = ((s[:, :, None] >> np.arange(4)) & 1) * np.exp2(np.arange(4) - (23.0 if o[r] < 2 else 28.0))
        if o[r] == 3: x[r, low, 9] = x[r, low, 8]
        if o[r] < 2: x[r, :, 11, :, 0] = 2.0 ** -10
        for g in rng.permutation(8)[:4]: x[r, g, 1, rng.integers(C), 0] = 2.0 ** 28 * rng.choice([-1.0, 1.0])
        k = (1.0, -2.0 ** -30, 2.0 ** -30, -2.0 ** -30)[o[r]]
        for h in range(0, 128, 16):
            u[r, h + 8, h] = k
            if o[r] < 2:
                u[r, h, h, 0] = k
                u[r, h + 11, h, 0] = k
            if o[r] == 2: u[r, h + 1, h, 0] = 1.0
            if o[r] == 3 and h // 16 in low:
                u[r, h + 8, h] = -k
                u[r, h + 9, h] = 1.125 * k
    w = layers(rng)
    for i in (0, 1, 8, 9, 10, 11, 12, 13, 14, 15):
        w[:, :, i] = 0
        w[:, :, :, :, :, i] = 0
    return {"x": x.reshape(N, 128, 4 * C).astype(BF), "u": u.reshape(N, 128, 512), "v": d["v"], **weights(rng, w)}
def setup_inputs_huge(rng):
    d = numbers_of(rng)
    o = rng.permutation(N)
    c = rng.integers(0, 2, (N, 1, 1, C, 1))
    odd = np.arange(16).reshape(1, 1, 16, 1, 1) % 2
    x = np.where(c == odd, 2.0 ** 30 * (0.7 + 0.05 * rng.random((N, 8, 16, C, 4))), 2.0 ** 28 * (0.9 + 0.1 * rng.random((N, 8, 16, C, 4))))
    x[o == 0] = 2.0 ** 30 * (0.75 + 0.0625 * rng.integers(0, 3, (1, 8, 16, C, 4)))
    a = 2.0 ** 30 * (1.0 - 0.1 * rng.random((N, 8, 16, 8, 4)))
    for r in range(N):
        if o[r] == 0: a[r] = 2.0 ** 30 * (rng.permutation(8) % 2 * 2.0 - 1.0)[None, None, :, None]
        elif o[r] < N // 2: a[r] *= -1.0
        else: a[r] *= (1.0 - 2.0 * odd[0]) * rng.choice([-1.0, 1.0], (1, 1, 8, 1))
    u = d["u"].reshape(N, 128, 128, 4)
    u[:, :, ::16] = a.reshape(N, 128, 8, 4).astype(np.float32).astype(BF)
    w = np.zeros((N, 128, 4, 128, 4), np.float32)
    i = np.arange(128)
    for b in range(4): w[:, i, b, i, b] = -1
    return {"x": x.astype(np.float32).reshape(N, 128, 4 * C).astype(BF), "u": u.reshape(N, 128, 512), "v": d["v"], **weights(rng, w.astype(BF))}
def setup_inputs_long(rng):
    d = numbers_of(rng)
    x = d["x"].astype(np.float32).reshape(N, 8, 16, C, 4)
    x[:, :, 0] = 0
    x[:, :, 0, 1::2, 0] = 1
    s = np.arange(E) % 2
    s[E - 2:] = 1, 0
    m = E // 32
    far = np.concatenate([[m - 1], np.arange(m - 3, 0, -1), [0, m - 2]])
    less = np.concatenate([[m - 1], np.arange(m - 3, 0, -1), [m - 2, 0]])
    t = np.stack([m - 1 - far, m - 1 - less, far[::-1], less[::-1]])[rng.integers(0, 4, (N, 32))].reshape(N, E)
    for r in range(N):
        x[r, :, 0, :, 1 + r % 2] = s[:C]
        x[(r + 1) % N, :, 0, :H, 1 + r % 2] = s[C:]
        x[r, :, 1, :, 1 + r % 2] = t[r, :C]
        x[(r + 1) % N, :, 1, :H, 1 + r % 2] = t[r, C:]
    n = (N, 8, 8, C, 4)
    x[:, :, 8:] = (1.0 + (2 * rng.integers(0, 4, n) + 1) * 0.125) * np.exp2(12.0 - rng.integers(8, 15, n)) * (rng.integers(0, 2, n) * 2.0 - 1.0)
    x[:, :, 8, :, 0] = np.where(rng.random((N, 8, C)) < 0.5, 1.96875, 0.0625) * 2.0 ** 12
    u = d["u"].reshape(N, 128, 128, 4)
    for r in range(N):
        k = rng.permutation(8)
        for g in range(8):
            if k[g] < 7:
                u[r, :, 16 * g] = 0
                u[r, 16 * g + (1 if k[g] == 6 else 0), 16 * g, 0 if k[g] < 5 else 1 + r % 2] = -1.0 if k[g] in (3, 4) else 1.0
    w = layers(rng)
    w[:, :, :9] = 0
    return {"x": x.reshape(N, 128, 4 * C).astype(BF), "u": u.reshape(N, 128, 512), "v": d["v"], **weights(rng, w)}
def setup_inputs_spread(rng):
    d = setup_inputs(rng)
    d["x"] = big(wide(rng, N, 128, 4 * C, cols=6))
    return d
def check_inputs(d):
    b = []
    for k in ("x", "u", "v"):
        a = np.abs(d[k].astype(np.float32))
        if not (np.isfinite(a).all() and ((a == 0) | (a >= 2.0 ** -30) & (a <= 2.0 ** 30)).all()): b.append("a value of " + k)
    none, least, most = [emit(mx_ref.quantize(np.full((128, 16), k, np.float32).astype(BF)))[1][0, 0] for k in (0.0, 2.0 ** -30, 2.0 ** 30)]
    for r in range(N):
        if ((d["wc"][r] == 0x7F) | (d["wc"][r] == 0xFF)).any(): b.append("wc: a code that is no number")
        s = mx_ref.live(d["ws"][r])
        if ((s != none) & ((s < least) | (s > most))).any(): b.append("ws: a scale out of range")
    return b
def reference(x, u, v, wc, ws):
    qu = [mx_ref.quantize(u[r]) for r in range(N)]
    lay = [pk(wc[r], ws[r]) for r in range(N)]
    now = [x[r] for r in range(N)]
    mirror = np.zeros((N, 8, E), np.int64)
    place = np.arange(E)
    for t in range(R):
        q = [mx_ref.quantize(now[r]) for r in range(N)]
        left, away, far = [], [], []
        for r in range(N):
            window = join(q[r], pick(q[(r + 1) % N], np.arange(H)))
            s = mx_ref.matmul(qu[r], window)[::16] + np.float32(0.0)
            full = decode(window).astype(BF)
            standing = np.argsort(np.argsort(-s, axis=1, kind="stable"), axis=1)
            o = np.argsort(place + standing // 32, axis=1, kind="stable")
            end = np.maximum.accumulate(o, axis=1) == place
            b = np.minimum.accumulate(np.where(end, place, E)[:, ::-1], axis=1)[:, ::-1]
            a = np.concatenate([np.zeros((8, 1), np.int64), np.maximum.accumulate(np.where(end, place + 1, 0), axis=1)[:, :-1]], axis=1)
            mirror[r] = np.take_along_axis(o, a + b - place, axis=1)
            z = (gcols(full, o[:, :C]).astype(np.float32) - gcols(full, mirror[r][:, :C]).astype(np.float32) * np.float32(0.5)).astype(BF)
            e = np.argsort(-np.abs(o - place)[:, :C], axis=1, kind="stable")[:, :K]
            left.append(z)
            away.append(e)
            far.append(mx_ref.quantize(gcols(z, e)))
        for r in range(N):
            back = np.full((8, C), K)
            np.put_along_axis(back, away[r], np.arange(K)[None, :], axis=1)
            rows = []
            for b in range(4):
                p = mx_ref.matmul(pick(lay[r], np.arange(128 * b, 128 * b + 128)), far[(r - J) % N]) * np.float32(0.03125)
                p = np.concatenate([p, np.zeros((128, 1), np.float32)], axis=1)
                rows.append(gpick(p, back) + left[r][:, b::4].astype(np.float32))
            now[r] = tile(rows)
    y, lm = np.zeros((N, 128, C), np.float32), np.zeros((N, 8, E), np.float32)
    oc, osc = np.zeros((N, 128, 4 * C), np.uint8), np.zeros((N, 16, C), np.uint8)
    for r in range(N):
        q = mx_ref.quantize(now[r])
        y[r] = mx_ref.matmul(mx_ref.quantize(v[r]), q)
        lm[r] = mirror[r]
        oc[r], osc[r] = emit(q)
    return {"y": y, "lm": lm, "oc": oc, "osc": osc}

@@ -1,0 +1,583 @@
+from concourse.mybir import dt, AluOpType as OP, ActivationFunctionType as AF
+
+C, H, E, K, J, R = 320, 96, 416, 128, 2, 2
+HW, GW, HO, PAD = 232, 240, 184, 16
+HE = E // 2
+BIG = 2.0 ** 96
+P = 2.0 ** 21
+A_N = (12, 11)
+V_EARLY, A_EARLY = (3, 6), (6, 5)
+NT = 7
+
+F32, BF, I32, U16, Q4, U8 = "float32", "bfloat16", "int32", "uint16", "float8_e4m3fn_x4", "uint8"
+
+
+def _sb(n, d):
+    return ("sbuf", [128, n], d)
+
+
+SCRATCH = {
+    "xin": _sb(4 * C, BF), "xst": _sb(4 * C, BF), "uin": _sb(512, BF), "vin": _sb(512, BF),
+    "uq": _sb(128, Q4), "us": _sb(128, U8), "ur": _sb(128, Q4), "urs": _sb(128, U8),
+    "vq": _sb(128, Q4), "vs": _sb(128, U8), "wq": _sb(512, Q4), "wp": _sb(512, U8),
+    "win0": _sb(E, Q4), "wis0": _sb(E, U8), "win1": _sb(E, Q4), "wis1": _sb(E, U8),
+    "fq": _sb(C, Q4), "fs": _sb(C, U8),
+    "aq0": _sb(K, Q4), "as0": _sb(K, U8), "aq1": _sb(K, Q4), "as1": _sb(K, U8),
+    "al0": _sb(K, Q4), "als0": _sb(K, U8), "al1": _sb(K, Q4), "als1": _sb(K, U8),
+    "pi": _sb(4, I32), "pf": _sb(4, F32), "pc": _sb(48, F32), "uli": _sb(8, I32), "ul": _sb(8, U16),
+    "yrow": _sb(E, BF), "m16": _sb(512, BF), "mrow": _sb(128, BF), "mhi": _sb(128, BF), "c16": _sb(32, F32),
+    "irow": _sb(E, F32), "ones": _sb(512, BF), "mk": _sb(E, BF), "rs": _sb(E, BF),
+    "m1": _sb(32, F32), "m2": _sb(32, F32), "mw16": _sb(16, F32), "rl": _sb(26, U16), "mw": _sb(E, F32),
+    "co": _sb(26, F32), "pl": _sb(26, F32), "shl": _sb(48, U16), "cnf": _sb(2, F32), "cnl": _sb(2, U16),
+    "keep": _sb(672, BF), "ctw": _sb(7 * 512, BF), "cwq": _sb(7 * 128, Q4), "cws": _sb(7 * 128, U8),
+    "et": _sb(2048, BF), "eq": _sb(512, Q4), "es": _sb(512, U8),
+    "sa": _sb(E, F32), "sh": _sb(E, F32), "sg": _sb(max(A_N) * E, BF),
+    "ct": _sb(NT * 4 * E, BF), "cq": _sb(NT * E, Q4), "cs": _sb(NT * E, U8),
+    "bw": _sb(272, BF), "bi": _sb(3 * GW, BF), "pw": _sb(272, BF), "ab": _sb(GW, BF),
+    "ot": _sb(8 * GW, BF), "oq": _sb(2 * GW, Q4), "osx": _sb(2 * GW, U8),
+    "sc": _sb(E, F32), "t26": _sb(26, F32), "ow": _sb(26, U16),
+    "xs": _sb(E, F32), "mir": _sb(E, F32), "sc2": _sb(E, F32), "mrw": _sb(26, U16),
+    "ad": _sb(C, F32), "ad2": _sb(C, BF), "acc": _sb(1, F32), "val": _sb(C, BF), "vm": _sb(352, BF),
+    "tb": _sb(672, BF), "tbs": _sb(672, BF), "rkw": _sb(32, U16), "er": _sb(C, F32),
+    "sce": _sb(K, F32), "ew": _sb(8, U16), "mer": _sb(K, F32), "scm": _sb(K, F32), "mew": _sb(8, U16),
+    "rf": _sb(20, F32), "rt": _sb(20, F32), "ru": _sb(20, F32), "rv": _sb(20, F32), "bk": _sb(20, U16),
+    "fp": _sb(4 * E, BF), "gp": _sb(4 * E, BF), "gf": _sb(4 * C, BF), "ge": _sb(4 * K, BF),
+    "at": _sb(4 * K, BF), "a32": _sb(4 * K, BF), "z": _sb(4 * C, BF), "zw": _sb(4 * (K + C), BF),
+    "dsb": _sb(E, F32), "mr": _sb(E, F32), "ysb": _sb(C, F32),
+}
+for _b in range(8):
+    SCRATCH["b%d" % _b] = ("psum", [128, 512], F32)
+
+SEMAPHORES = ["qv", "qa", "qt", "qg", "h0", "h1", "f0", "f1", "sent",
+              "dx", "du", "dv", "dw", "ds", "oy", "ol", "ocs"]
+
+
+def rank_program(g, core, T, topo):
+    rank = T.rank_of(core)
+    if rank is None:
+        return
+    n = len(T.cores)
+    ops = []
+
+    def v(name, a=0, b=None, s=1, p0=0, p1=128):
+        w = SCRATCH[name][1][1]
+        if s > 0:
+            b = w if b is None else b
+            cols = range(a, b, s)
+            b = cols[-1] + 1
+            sl = slice(a, b, s) if s > 1 else slice(a, b)
+        else:
+            cols = range(0, a + 1)
+            sl = slice(a, None, -1)
+        ap = T[name][p0:p1, sl] if (p0, p1) != (0, 128) else T[name][:, sl]
+        return (ap, [(name, frozenset(cols), p0, p1)])
+
+    def ind(win, off, word=False):
+        ap = win[0].bitcast(dt.uint32) if word else win[0]
+        return (ap.indirect(off[0]), win[1] + off[1])
+
+    def col(name, c, p0=0, p1=128):
+        return v(name, c, c + 1, 1, p0, p1)
+
+    def add(q, fn, outs, ins, ext=(), dma=None, acc=None):
+        rd, wr = [], []
+        for x in ins:
+            if isinstance(x, tuple):
+                rd += x[1]
+        for x in outs:
+            wr += x[1]
+        ops.append({"q": q, "fn": fn, "rd": rd, "wr": wr, "ext": list(ext), "dma": dma, "acc": acc})
+
+    def ap(x):
+        return x[0] if isinstance(x, tuple) else x
+
+    def ts(out, a, s1, op0, s2=None, op1=None):
+        if op1 is None:
+            add("v", lambda: g.vector.tensor_scalar(ap(out), ap(a), ap(s1), None, op0), [out], [a, s1])
+        else:
+            add("v", lambda: g.vector.tensor_scalar(ap(out), ap(a), ap(s1), ap(s2), op0, op1), [out], [a, s1, s2])
+
+    def tt(out, a, b, op):
+        add("v", lambda: g.vector.tensor_tensor(ap(out), ap(a), ap(b), op), [out], [a, b])
+
+    def cp(out, a):
+        add("v", lambda: g.vector.tensor_copy(ap(out), ap(a)), [out], [a])
+
+    def scan(out, a, b, init, op0, op1):
+        add("v", lambda: g.vector.tensor_tensor_scan(ap(out), ap(a), ap(b), ap(init), op0, op1), [out], [a, b, init])
+
+    def ms(out, c):
+        add("v", lambda: g.vector.memset(ap(out), c), [out], [])
+
+    def tr(out, a):
+        add("v", lambda: g.vector.transpose(ap(out), ap(a)), [out], [a])
+
+    def qz(q, s, a):
+        add("v", lambda: g.vector.quantize_mx(ap(q), ap(s), ap(a)), [q, s], [a])
+
+    def act(out, a, f, bias=0.0, scale=1.0, accum=None):
+        if accum is None:
+            if f == AF.Copy:
+                add("a", lambda: g.scalar.activation(ap(out), ap(a), f, scale=scale), [out], [a])
+            else:
+                add("a", lambda: g.scalar.activation(ap(out), ap(a), f, bias=ap(bias), scale=scale), [out], [a, bias])
+        else:
+            add("a", lambda: g.scalar.activation(ap(out), ap(a), f, bias=ap(bias), scale=scale, accum_out=ap(accum)),
+                [out, accum], [a, bias])
+
+    def mm(bank, w, ws_, wc0, x, xs_, xc0, cols, start=True, stop=True, ext=(), acc=None):
+        o, a, b = v(bank, 0, cols), v(w, wc0, wc0 + 128), v(ws_, wc0, wc0 + 128)
+        c, d = v(x, xc0, xc0 + cols), v(xs_, xc0, xc0 + cols)
+        add("t", lambda: g.tensor.matmul_mx(o[0], a[0], b[0], c[0], d[0], start, stop), [o], [a, b, c, d], ext, None, acc)
+
+    def iota(out, pat, base, cm, small=True):
+        if small:
+            add("g", lambda: g.iota(ap(out), pat, base, cm, allow_small_or_imprecise_dtypes=True), [out], [])
+        else:
+            add("g", lambda: g.iota(ap(out), pat, base, cm), [out], [])
+
+    def dma(q, out, a, sem):
+        eng = g.sync if q == "s" else g.scalar
+        outs = [out] if isinstance(out, tuple) else []
+        add(q, lambda: eng.dma_start(ap(out), ap(a)), outs, [a], (), sem)
+
+    def bytes_of(x):
+        return (x[0].bitcast(dt.uint8), x[1])
+
+    sent = [0]
+
+    def send(dst, qd, sd, c0, qs, ss, cols, sem):
+        rid, pid, _ = topo.addr(dst)
+        m = topo.mask(core, dst)
+        for src, land in ((bytes_of(v(qs, 0, cols)), bytes_of(v(qd, c0, c0 + cols))), (v(ss, 0, cols), v(sd, c0, c0 + cols))):
+            add("g", lambda src=src, land=land: g.remote_dma(land[0], src[0], T.sem[sem], T.sem.sent, pid, rid, m),
+                [], [src], (), "remote")
+            sent[0] += len(topo.engines(core, dst))
+
+    prev, far = T.cores[(rank - 1) % n], T.cores[(rank + J) % n]
+    n_halo = 2 * len(topo.engines(T.cores[(rank + 1) % n], core))
+    n_far = 2 * len(topo.engines(T.cores[(rank - J) % n], core))
+
+    dma("s", v("xin"), T.x[:], "dx")
+    dma("a", v("uin"), T.u[:], "du")
+    dma("s", bytes_of(v("wq")), T.wc[:], "dw")
+    ops[-1]["rd"] = v("xin")[1]
+    dma("s", v("wp"), T.ws[:], "ds")
+    dma("s", v("vin"), T.v[:], "dv")
+
+    iota(col("pi", 0), [[0, 1]], 0, 1, False)
+    iota(v("uli"), [[16, 8]], 0, 0, False)
+    iota(v("yrow"), [[0, 26], [1, 16]], 0, 0)
+    iota(v("c16"), [[16, 32]], 0, 0)
+    iota(v("m16"), [[0, 8], [1, 16], [0, 4]], 0, 0)
+    ms(v("rs"), 0.0)
+    ms(v("ones"), 1.0)
+    ts(col("pi", 1), col("pi", 0), 15, OP.bitwise_and)
+    ts(col("pi", 2), col("pi", 0), 4, OP.arith_shift_right)
+    cp(v("ul"), v("uli"))
+    ms(v("rs", 0, E, 16), -BIG)
+    tt(col("pi", 3), col("pi", 0), col("pi", 2), OP.add)
+    ms(v("keep"), 1.0)
+    ts(col("pi", 3), col("pi", 3), 1, OP.bitwise_and)
+    ms(v("keep", 0, 672, 16), 0.0)
+    cp(v("pf"), v("pi"))
+    r_, a_, par = col("pf", 1), col("pf", 2), col("pf", 3)
+    ms(v("ct", 6 * 4 * E + 3, 7 * 4 * E, 4), 0.0)
+    ms(v("ctw", 1024 + 3, 7 * 512, 4), 0.0)
+    ms(v("ot", 3, 8 * GW, 4), 0.0)
+    ms(v("bw", 0, PAD), 0.0)
+    ms(v("bw", PAD + HW, 272), 1024.0)
+    ms(v("pw"), 99.0)
+    ms(v("vm"), 0.0)
+    ts(v("mk"), v("yrow"), r_, OP.not_equal, -BIG, OP.mult)
+    ID = AF.Identity
+    pieces = [(0, 0, 128, 1.0, 1.0), (1, 0, 128, -1.0, -1.0), (2, 0, 32, 1.0, 9.0), (2, 32, 64, -11.0, 33.0), (2, 64, 128, -1.0, -5.0)]
+    for s, p0, p1, k, c in pieces:
+        act(col("pc", s, p0, p1), col("pf", 2, p0, p1), ID, c, k)
+        act(col("pc", 8 + s, p0, p1), col("pf", 2, p0, p1), ID, -c + (1.0 if c < 0 else 0.0), -k)
+    act(v("pc", 4, 7), v("pc", 0, 3), AF.Abs)
+    act(v("pc", 12, 15), v("pc", 0, 3), ID, 12.0, -1.0)
+    act(v("pc", 16, 19), v("pc", 0, 3), ID, 0.0, 1024.0)
+    act(col("pc", 23), r_, ID, float(PAD))
+    act(col("pc", 24), col("pc", 2), ID, -12.0)
+    act(col("pc", 25), r_, ID, -512.0, -1024.0)
+    act(col("pc", 26), a_, ID, 8.0)
+    act(col("pc", 27), r_, ID, -8.0)
+    act(col("pc", 28), r_, ID, 0.0, 16.0)
+    act(col("pc", 29), r_, ID, -128.0, 16.0)
+    act(v("pc", 20, 23), v("pc", 0, 3), ID, col("pc", 23))
+    act(v("pc", 32, 35), v("pc", 4, 7), ID, col("pc", 28))
+    act(v("pc", 36, 39), v("pc", 4, 7), ID, col("pc", 29))
+    act(col("pc", 30), r_, ID, 128.0)
+    act(v("pl"), v("c16", 0, 26), ID, col("pc", 30))
+    act(col("pc", 31), par, ID, col("pc", 28), 336.0)
+    act(v("cnf"), v("c16", 0, 32, 16), ID, col("pc", 31))
+    qz(v("uq"), v("us"), v("uin"))
+    ts(v("m1", 0, 17), v("yrow", 0, 17), r_, OP.is_equal, P, OP.mult)
+    ts(v("m2", 0, 17), v("yrow", 0, 17), r_, OP.is_equal, -2 * P, OP.mult)
+    cp((v("ur")[0].bitcast(dt.uint32), v("ur")[1]), ind(v("uq"), v("ul"), True))
+    cp(v("urs"), ind(v("us"), v("ul")))
+    ts(v("rl"), v("c16", 0, 26), 0.0, OP.mult, r_, OP.add)
+    tt(v("mw16"), v("m1", 0, 16), v("m2", 1, 17), OP.add)
+    ts(col("pc", 40), r_, 0.0, OP.is_equal, 2 * P, OP.mult)
+    act(v("mw"), ind(v("mw16"), v("rl")), AF.Copy)
+    act(col("pc", 41), col("pc", 40), ID, -P)
+    act(col("pc", 42), col("pc", 40), ID, -P - 128.0 * 1024)
+    act(v("co"), v("pl"), ID, col("pc", 42), 1024.0)
+    latch = col("pc", 41)
+
+    def count_tiles():
+        for h in range(2):
+            ts(v("ctw", 512 * h, 512 * h + 512), v("m16"), col("pc", 26) if h else a_, OP.is_equal, 1.0 / 32, OP.mult)
+        for s in range(3):
+            ts(v("ctw", 1024 + s, 1536, 4), v("yrow", 0, 128), r_, OP.is_equal)
+            ts(v("shl", 16 * s, 16 * s + 16), v("c16", 0, 16), col("pc", 20 + s), OP.add)
+        qz(v("cwq", 0, 384), v("cws", 0, 384), v("ctw", 0, 1536))
+
+    def move_tiles():
+        for s in range(3):
+            for h in range(2):
+                ts(v("ctw", 1536 + 512 * h + s, 2048 + 512 * h, 4), v("mhi"), col("pc", 27) if h else r_, OP.is_equal,
+                   col("pc", 16 + s), OP.mult)
+
+    def far_tiles():
+        for s in range(3):
+            for h in range(2):
+                ts(v("ctw", 2560 + 512 * h + s, 3072 + 512 * h, 4), v("mrow"), col("pc", 32 + 4 * h + s), OP.is_equal,
+                   2.0, OP.mult)
+        ts(v("cnl"), v("cnf"), 15.0, OP.add, 671.0, OP.min)
+        qz(v("cwq", 640, 896), v("cws", 640, 896), v("ctw", 2560, 3584))
+
+    def latch_row(out, row, w):
+        scan(out, row, v("mw", 0, w), -2 * P, OP.max, OP.add)
+
+    def offsets(out, buf, w):
+        ts(v(out, 0, w // 16), v(buf, 15, w, 16), latch, OP.add)
+
+    for t in range(R):
+        last = t == R - 1
+        win, wis, xt = "win%d" % t, "wis%d" % t, "xin" if t == 0 else "xst"
+        qz(v(win, 0, C), v(wis, 0, C), v(xt))
+        send(prev, win, wis, C, win, wis, H, "h%d" % t)
+        mm("b0", "ur", "urs", 0, win, wis, 0, C)
+        mm("b2", "ur", "urs", 0, win, wis, 0, C)
+        if t == 0:
+            for b in range(4):
+                o = v("et", 512 * b, 512 * b + 512)
+                add("g", lambda o=o, b=b: g.affine_select(o[0], T.ones[:], [[1, 512]], OP.is_equal, 0.0, -b, -4), [o], [v("ones")])
+            iota(v("mhi"), [[1, 8], [0, 16]], 0, 0)
+            iota(v("mrow"), [[1, 128]], 0, 0)
+            iota(v("irow"), [[1, E]], 0, 0)
+
+        A_C = list(range(8, 8 + A_N[t]))
+        V_C = [c for c in range(26) if c not in A_C]
+        ES = len(V_C)
+        A0 = ES + 1
+        ve, ae = V_EARLY[t], A_EARLY[t]
+
+        def slot(k, a, b):
+            base = (k // 4) * 4 * E + k % 4
+            return v("ct", base + 4 * a, base + 4 * b, 4)
+
+        def mask_scores(bank, a, b):
+            tt(v("sa", a, b), v(bank, a, b), v("mk", a, b), OP.add)
+
+        def latch_scores(a, b):
+            scan(v("sh", a, b), v("rs", a, b), v("sa", a, b), -BIG, OP.add, OP.max)
+
+        def sj(c):
+            return col("sh", 16 * c + 15)
+
+        started = [False]
+
+        def count(u, end=False):
+            for a, b, hs in ((0, HW, (0,)), (HW, E, (1,))) if end else ((0, E, (0, 1)),):
+                qz(v("cq", u * E + a, u * E + b), v("cs", u * E + a, u * E + b), v("ct", 4 * (u * E + a), 4 * (u * E + b)))
+                for h in hs:
+                    mm("b4", "cwq", "cws", 128 * h, "cq", "cs", u * E + HO * h, HW, not started[0], end and h == 1, (), ("st", t))
+                    started[0] = True
+
+        def sg(k, a, b):
+            return v("sg", k * E + a, k * E + b)
+
+        def p1(k, bank, a, b):
+            act(sg(k, a, b), v(bank, a, b), AF.Sign, sj(A_C[k]), -1.0)
+
+        def p2gt(k):
+            act(slot(A0 + k, 0, 16 * A_C[k] + 16), sg(k, 0, 16 * A_C[k] + 16), AF.Relu)
+
+        def p2ge(k):
+            act(slot(A0 + k, 16 * A_C[k] + 16, E), sg(k, 16 * A_C[k] + 16, E), AF.Sign, 1.0)
+
+        mask_scores("b0", 128, 224)
+        mask_scores("b0", 0, 128)
+        latch_scores(128, 224)
+        mask_scores("b0", 224, C)
+        latch_scores(0, 128)
+        latch_scores(224, C)
+        if t == 0:
+            count_tiles()
+        for k in range(ae):
+            p1(k, "b2", 0, C)
+            if k:
+                p2gt(k - 1)
+        p2gt(ae - 1)
+        for k in range(8):
+            ts(slot(k, 0, 16 * k + 16), v("b0", 0, 16 * k + 16), sj(k), OP.is_lt)
+        tt(slot(ES, 0, C), v("b0", 0, C), v("sh", 0, C), OP.is_equal)
+        for k in range(ve):
+            ts(slot(k, 16 * k + 16, C), v("b0", 16 * k + 16, C), sj(k), OP.is_le)
+        mm("b1", "ur", "urs", 0, win, wis, 0, E, ext=[("h%d" % t, n_halo)])
+        mm("b3", "ur", "urs", 0, win, wis, 0, E)
+        mask_scores("b1", C, E)
+        ts(slot(0, C, E), v("b1", C, E), sj(0), OP.is_le)
+        latch_scores(C, E)
+        for k in range(1, ve):
+            ts(slot(k, C, E), v("b1", C, E), sj(k), OP.is_le)
+        tt(slot(ES, C, E), v("b1", C, E), v("sh", C, E), OP.is_equal)
+        for k in range(ae):
+            p1(k, "b3", C, E)
+        p1(ae, "b3", 0, E)
+        for k in range(ae):
+            p2ge(k)
+        for k in range(ae, len(A_C)):
+            if k + 1 < len(A_C):
+                p1(k + 1, "b3", 0, E)
+            p2gt(k)
+            p2ge(k)
+
+        def vblock(k):
+            c = V_C[k]
+            if c >= 8:
+                ts(slot(k, 0, 16 * c + 16), v("b1", 0, 16 * c + 16), sj(c), OP.is_lt)
+            if 16 * c + 16 < E:
+                ts(slot(k, 16 * c + 16, E), v("b1", 16 * c + 16, E), sj(c), OP.is_le)
+
+        for k in range(ve, 7):
+            vblock(k)
+        count(0)
+        vblock(7)
+        if t == 0:
+            qz(v("eq"), v("es"), v("et"))
+        vblock(8)
+        count(1)
+        for b in range(3):
+            mm("b%d" % (5 + b), "eq", "es", 128 * b, win, wis, 0, E)
+        vblock(9)
+        vblock(10)
+        count(4)
+        vblock(11)
+        vblock(12)
+        count(2)
+        vblock(13)
+        if ES > 14:
+            vblock(14)
+        count(5)
+        if t == 0:
+            qz(v("vq"), v("vs"), v("vin"))
+        count(3)
+        count(6, True)
+        if t == 0:
+            move_tiles()
+        mm("b0", "eq", "es", 384, win, wis, 0, E)
+
+        def shifts(s):
+            return v("shl", 16 * s, 16 * s + 15)
+
+        ts(v("bw", PAD, PAD + HW), v("b4", 0, HW), 192.0 - 16.5 / 32, OP.add)
+        ts(v("bi", 0, GW), v("bw", PAD, PAD + GW), col("pc", 8), OP.add)
+        for s in (1, 2):
+            act(v("bi", s * GW, s * GW + GW), v("bw", PAD, PAD + GW), ID, col("pc", 8 + s))
+        for s in range(3):
+            tt(v("ot", s, 4 * GW, 4), ind(v("bw"), shifts(s)), v("bi", s * GW, s * GW + GW), OP.is_lt)
+
+        def unpack(b):
+            act(v("fp", b * E, b * E + E), v("b%d" % ((5 + b) % 8), 0, E), AF.Copy)
+
+        for b in range(3):
+            unpack(b)
+        qz(v("oq", 0, GW), v("osx", 0, GW), v("ot", 0, 4 * GW))
+        mm("b4", "cwq", "cws", 256, "oq", "osx", 0, HW)
+        if t == 0:
+            qz(v("cwq", 384, 640), v("cws", 384, 640), v("ctw", 1536, 2560))
+        cp(v("pw", PAD, PAD + HW), v("b4", 0, HW))
+        act(v("ab"), ind(v("pw"), shifts(2)), AF.Abs, col("pc", 24))
+        for s in range(2):
+            ts(v("ot", 4 * GW + s, 8 * GW, 4), ind(v("pw"), shifts(s)), col("pc", 12 + s), OP.is_equal)
+        act(v("ot", 4 * GW + 2, 8 * GW, 4), v("ab"), AF.Relu, 1.0, -1.0)
+        unpack(3)
+        qz(v("oq", GW, 2 * GW), v("osx", GW, 2 * GW), v("ot", 4 * GW, 8 * GW))
+        mm("b1", "cwq", "cws", 384, "oq", "osx", GW, HE)
+        mm("b4", "cwq", "cws", 512, "oq", "osx", GW + HE - HO, HE)
+        mm("b2", "cwq", "cws", 512, "oq", "osx", GW - HO, E)
+        mm("b2", "cwq", "cws", 384, "oq", "osx", GW, HE)
+        if t == 0:
+            far_tiles()
+        mm("b3", "cwq", "cws", 768, "oq", "osx", GW - HO, C)
+        mm("b3", "cwq", "cws", 640, "oq", "osx", GW, HE)
+
+        scan(v("xs", 0, HE), v("irow", 0, HE), v("b1", 0, HE), 0.0, OP.max, OP.add)
+        latch_row(v("sc", 0, HE), v("b1", 0, HE), HE)
+        latch_row(v("sc", HE, E), v("b4", 0, HE), HE)
+        scan(v("xs", HE, E), v("irow", HE, E), v("b4", 0, HE), col("xs", HE - 1), OP.max, OP.add)
+        tt(v("t26"), v("sc", 15, E, 16), v("co"), OP.add)
+        scan(v("mir", E - 1, None, -1), v("ones", 0, E), v("xs", E - 1, None, -1), 1000.0, OP.add, OP.min)
+        ts(v("ow"), v("t26"), 1.0 / 1024, OP.mult)
+        act(v("ad"), v("b2", 0, C), AF.Abs)
+        act(v("ad2"), v("ad"), AF.Sign, col("pc", 25), 1.0, v("acc"))
+        for b in range(4):
+            act(v("gp", b * E, b * E + E), ind(v("fp", b * E, b * E + E), v("ow")), AF.Copy, 0.0, -0.5)
+
+        def plane(b):
+            return v("gp", b * E, b * E + E)
+
+        def whole(b):
+            act(v("gf", b * C, b * C + C), v("gp", b * E, b * E + C), AF.Copy, 0.0, -2.0)
+
+        scan(v("val"), v("b3", 0, C), v("ones", 0, C), v("acc"), OP.add, OP.mult)
+        tt(v("vm", 16, 16 + C), v("b3", 0, C), v("val"), OP.mult)
+        tr(v("tb", 0, C), v("vm", 16, 16 + C))
+        tr(v("tb", C, 672), v("vm"))
+        scan(v("tbs", 0, C), v("keep", 0, C), v("tb", 0, C), 0.0, OP.mult, OP.add)
+        scan(v("tbs", C, 672), v("keep", C, 672), v("tb", C, 672), 0.0, OP.mult, OP.add)
+        ts(v("rkw"), ind(v("tbs"), v("cnl")), 0.25, OP.mult, 159.0, OP.add)
+        cp(ind(v("er"), v("rkw", 0, 20)), v("irow", 0, C))
+        ops[-1]["wr"], ops[-1]["rd"] = v("er")[1], v("rkw", 0, 20)[1] + v("irow", 0, C)[1]
+        cp(v("rf"), v("rkw", 0, 20))
+        latch_row(v("sce"), v("er", 0, K), K)
+        ts(v("rt"), v("rf"), 128.0, OP.is_ge, 1024.0, OP.mult)
+        offsets("ew", "sce", K)
+        whole(0)
+        whole(1)
+        act(v("mer"), ind(v("mir"), v("ew")), AF.Copy)
+        mw_ = E if last else C
+        latch_row(v("sc2", 0, mw_), v("mir", 0, mw_), mw_)
+        latch_row(v("scm"), v("mer"), K)
+        tt(v("ru"), v("rt"), v("rf"), OP.add)
+        offsets("mew", "scm", K)
+        offsets("mrw", "sc2", mw_)
+        for b in range(4):
+            act(v("ge", b * K, b * K + K), ind(plane(b), v("ew")), AF.Copy, 0.0, -2.0)
+        for b in range(4):
+            tt(v("at", b, 4 * K, 4), ind(plane(b), v("mew")), v("ge", b * K, b * K + K), OP.add)
+        tt(v("rv"), v("ru"), v("pl", 0, 20), OP.min)
+        qz(v("aq%d" % t), v("as%d" % t), v("at"))
+        send(far, "al%d" % t, "als%d" % t, 0, "aq%d" % t, "as%d" % t, K, "f%d" % t)
+
+        cp(v("bk"), v("rv"))
+        for b in range(2, 4):
+            whole(b)
+        for b in range(4):
+            act(v("a32", b * K, b * K + K), v("at", b, 4 * K, 4), AF.Copy, 0.0, 32.0)
+        W = K + C
+        for b in range(4):
+            tt(v("z", b * C, b * C + C), ind(plane(b), v("mrw", 0, 20)), v("gf", b * C, b * C + C), OP.add)
+            act(v("zw", b * W + K, b * W + W), v("z", b * C, b * C + C), AF.Copy, 0.0, 32.0)
+        if last:
+            act(v("dsb"), v("b2", 0, E), AF.Copy, 0.0, 1.0 / 1024)
+
+        for b in range(4):
+            mm("b%d" % ((5 + b) % 8), "wq", "wp", 128 * b, "al%d" % t, "als%d" % t, 0, K,
+               ext=[("f%d" % t, n_far)] if b == 0 else ())
+        for b in range(4):
+            tt(v("zw", b * W, b * W + K), v("b%d" % ((5 + b) % 8), 0, K), v("a32", b * K, b * K + K), OP.add)
+        for b, lo, hi, on_scalar in ((0, 0, C, 1), (1, 0, C, 1), (2, C // 2, C, 0), (3, 0, C, 0), (2, 0, C // 2, 1)):
+            src = ind(v("zw", b * W, b * W + W), v("bk", lo // 16, hi // 16))
+            if on_scalar:
+                act(v("xst", 4 * lo + b, 4 * hi, 4), src, AF.Copy, 0.0, 1.0 / 32)
+            else:
+                ts(v("xst", 4 * lo + b, 4 * hi, 4), src, 1.0 / 32, OP.mult)
+
+    qz(v("fq"), v("fs"), v("xst"))
+    mm("b1", "vq", "vs", 0, "fq", "fs", 0, C)
+    tt(v("mr"), ind(v("dsb"), v("mrw")), v("mir"), OP.add)
+    act(v("ysb"), v("b1", 0, C), AF.Copy)
+    dma("s", T.oc[:], bytes_of(v("fq")), "ocs")
+    for k in range(4):
+        dma("s", T.osc[4 * k:4 * k + 4, :], v("fs", 0, C, 1, 32 * k, 32 * k + 4), "ocs")
+    dma("a", T.y[:], v("ysb"), "oy")
+    dma("s", T.lm[:], (T.mr[0:128:16, :], v("mr")[1]), "ol")
+
+    emit(g, T, ops, sent[0])
+
+
+def meets(a, b):
+    if a[0] != b[0] or a[3] <= b[2] or b[3] <= a[2]:
+        return False
+    return SCRATCH[a[0]][0] == "psum" or not a[1].isdisjoint(b[1])
+
+
+def emit(g, T, ops, sent):
+    eng = {"v": g.vector, "a": g.scalar, "t": g.tensor, "g": g, "s": g.sync}
+    deps = []
+    by_buf = {}
+    for i, o in enumerate(ops):
+        d = set()
+        for kind, regs in (("r", o["rd"]), ("w", o["wr"])):
+            for reg in regs:
+                psum = SCRATCH[reg[0]][0] == "psum"
+                for j, k2, r2 in by_buf.get(reg[0], []):
+                    if j in d or not meets(reg, r2):
+                        continue
+                    if kind == "r" and k2 == "r" and not (psum and ops[j]["q"] != o["q"]):
+                        continue
+                    if o["acc"] is not None and ops[j]["acc"] == o["acc"]:
+                        continue
+                    if ops[j]["dma"] == "remote":
+                        continue
+                    d.add(j)
+        deps.append(d)
+        for kind, regs in (("r", o["rd"]), ("w", o["wr"])):
+            for reg in regs:
+                by_buf.setdefault(reg[0], []).append((i, kind, reg))
+    known_q = {q: ({}, set()) for q in eng}
+    done = []
+    waits = []
+    needed = set()
+    for i, o in enumerate(ops):
+        last, dm = known_q[o["q"]]
+        last, dm = dict(last), set(dm)
+        w = []
+        for j in sorted(deps[i], reverse=True):
+            oj = ops[j]
+            if oj["dma"]:
+                if j in dm:
+                    continue
+            elif last.get(oj["q"], -1) >= j:
+                continue
+            w.append(j)
+            needed.add(j)
+            l2, d2 = done[j]
+            for q, x in l2.items():
+                last[q] = max(last.get(q, -1), x)
+            dm |= d2
+        waits.append(w)
+        known_q[o["q"]] = (last, dm)
+        l3, d3 = dict(last), set(dm)
+        if o["dma"]:
+            d3.add(i)
+        else:
+            l3[o["q"]] = i
+        done.append((l3, d3))
+    count, total = {}, {}
+    for i, o in enumerate(ops):
+        if o["dma"] and o["dma"] != "remote":
+            total[o["dma"]] = total.get(o["dma"], 0) + 16
+            count[i] = (o["dma"], total[o["dma"]])
+        elif i in needed:
+            s = "q" + o["q"]
+            total[s] = total.get(s, 0) + 1
+            count[i] = (s, total[s])
+    waited = {}
+    for i, o in enumerate(ops):
+        e = eng[o["q"]]
+        for s, c in [count[j] for j in waits[i]] + o["ext"]:
+            e.wait_ge(T.sem[s], c)
+            waited[s] = max(waited.get(s, 0), c)
+        ins = o["fn"]()
+        if i in count:
+            ins.then_inc(T.sem[count[i][0]], 16 if o["dma"] else 1)
+    g.wait_ge(T.sem.sent, sent)
+    for s, c in total.items():
+        if waited.get(s, 0) < c:
+            g.sync.wait_ge(T.sem[s], c)

@@ -3,11 +3,22 @@ from concourse.mybir import dt, AluOpType as OP, ActivationFunctionType as AF
 C, H, E, K, J, R = 320, 96, 416, 128, 2, 2
 HW, GW, HO, PAD = 232, 240, 184, 16
 HE = E // 2
+CH = 192
+NB, OWN = E // 16, C // 16
 BIG = 2.0 ** 96
 P = 2.0 ** 21
-A_N = (12, 11)
-V_EARLY, A_EARLY = (3, 6), (6, 5)
+DIG = 6144.0
+ON_VECTOR = (14, 16)
+SHARED = ((25, 24, 23, 22), (25, 24))
+XS = 128
+SN = 256
 NT = 7
+TW = [128, 128, 192, 256, 320, 384, E]
+TP = [128, 128, HO + 128, HO + 128, 320, 384, E]
+CYCLE = 0.9
+HOP, LOAD = 170.0, 2000.0
+TRAVEL, FIRST = 1500.0, 2000.0
+PASSES = 2
 
 F32, BF, I32, U16, Q4, U8 = "float32", "bfloat16", "int32", "uint16", "float8_e4m3fn_x4", "uint8"
 
@@ -24,25 +35,27 @@ SCRATCH = {
     "fq": _sb(C, Q4), "fs": _sb(C, U8),
     "aq0": _sb(K, Q4), "as0": _sb(K, U8), "aq1": _sb(K, Q4), "as1": _sb(K, U8),
     "al0": _sb(K, Q4), "als0": _sb(K, U8), "al1": _sb(K, Q4), "als1": _sb(K, U8),
-    "pi": _sb(4, I32), "pf": _sb(4, F32), "pc": _sb(48, F32), "uli": _sb(8, I32), "ul": _sb(8, U16),
-    "yrow": _sb(E, BF), "m16": _sb(512, BF), "mrow": _sb(128, BF), "mhi": _sb(128, BF), "c16": _sb(32, F32),
-    "irow": _sb(E, F32), "ones": _sb(512, BF), "mk": _sb(E, BF), "rs": _sb(E, BF),
-    "m1": _sb(32, F32), "m2": _sb(32, F32), "mw16": _sb(16, F32), "rl": _sb(26, U16), "mw": _sb(E, F32),
-    "co": _sb(26, F32), "pl": _sb(26, F32), "shl": _sb(48, U16), "cnf": _sb(2, F32), "cnl": _sb(2, U16),
-    "keep": _sb(672, BF), "ctw": _sb(7 * 512, BF), "cwq": _sb(7 * 128, Q4), "cws": _sb(7 * 128, U8),
-    "et": _sb(2048, BF), "eq": _sb(512, Q4), "es": _sb(512, U8),
-    "sa": _sb(E, F32), "sh": _sb(E, F32), "sg": _sb(max(A_N) * E, BF),
+    "pi": _sb(8, I32), "pf": _sb(8, F32), "pc": _sb(64, F32), "ul": _sb(8, U16),
+    "yrow": _sb(128, BF), "m16": _sb(512, BF), "mrow": _sb(128, BF), "mhi": _sb(128, BF), "c16": _sb(32, F32),
+    "irow": _sb(HW, F32), "irc": _sb(E, BF), "ones": _sb(516, BF), "hb": _sb(HW, F32),
+    "pvl": _sb(6, U16), "pm": _sb(48, F32), "ibl": _sb(NB, U16), "exl": _sb(NB, U16), "dul": _sb(4, U16), "dm": _sb(64, F32),
+    "m1": _sb(32, F32), "m2": _sb(32, F32), "mw16": _sb(16, F32), "rl": _sb(26, U16), "mw": _sb(HE, F32),
+    "co": _sb(26, F32), "pl": _sb(26, F32), "shl": _sb(48, U16), "cnf": _sb(2, F32), "cnl": _sb(4, U16),
+    "keep": _sb(E, BF), "ctw": _sb(9 * 512, BF), "cwq": _sb(9 * 128, Q4), "cws": _sb(9 * 128, U8),
+    "et": _sb(516, BF), "eq": _sb(512, Q4), "es": _sb(512, U8),
+    "sb": _sb(E, F32), "pt": _sb(64, F32), "pv": _sb(32, F32), "sg": _sb(8 * NB * NB, BF), "jk": _sb(8 * NB * NB, BF),
+    "rs": _sb(32, F32), "sn": _sb(SN * 17, BF), "seg": _sb(E, BF),
+    "y0": _sb(32, F32), "y1": _sb(64, F32), "hi": _sb(64, BF), "lo": _sb(64, F32),
     "ct": _sb(NT * 4 * E, BF), "cq": _sb(NT * E, Q4), "cs": _sb(NT * E, U8),
-    "bw": _sb(272, BF), "bi": _sb(3 * GW, BF), "pw": _sb(272, BF), "ab": _sb(GW, BF),
+    "kw": _sb(272, BF), "bi": _sb(3 * GW, BF), "pw": _sb(272, BF), "ab": _sb(GW, BF),
     "ot": _sb(8 * GW, BF), "oq": _sb(2 * GW, Q4), "osx": _sb(2 * GW, U8),
-    "sc": _sb(E, F32), "t26": _sb(26, F32), "ow": _sb(26, U16),
-    "xs": _sb(E, F32), "mir": _sb(E, F32), "sc2": _sb(E, F32), "mrw": _sb(26, U16),
-    "ad": _sb(C, F32), "ad2": _sb(C, BF), "acc": _sb(1, F32), "val": _sb(C, BF), "vm": _sb(352, BF),
-    "tb": _sb(672, BF), "tbs": _sb(672, BF), "rkw": _sb(32, U16), "er": _sb(C, F32),
-    "sce": _sb(K, F32), "ew": _sb(8, U16), "mer": _sb(K, F32), "scm": _sb(K, F32), "mew": _sb(8, U16),
-    "rf": _sb(20, F32), "rt": _sb(20, F32), "ru": _sb(20, F32), "rv": _sb(20, F32), "bk": _sb(20, U16),
-    "fp": _sb(4 * E, BF), "gp": _sb(4 * E, BF), "gf": _sb(4 * C, BF), "ge": _sb(4 * K, BF),
-    "at": _sb(4 * K, BF), "a32": _sb(4 * K, BF), "z": _sb(4 * C, BF), "zw": _sb(4 * (K + C), BF),
+    "sc": _sb(E, F32), "t26": _sb(26, F32), "ow": _sb(26, U16), "dl": _sb(E, BF),
+    "xs": _sb(E, BF), "mir": _sb(E + 32, BF), "tm": _sb(2 * E + 32, BF), "mrw": _sb(32, U16),
+    "ad2": _sb(C, BF), "acc": _sb(1, F32), "val": _sb(C, BF), "vm": _sb(C + 32, BF),
+    "tb": _sb(2 * E + 32, BF), "tbs": _sb(2 * E + 32, BF), "rkw": _sb(32, U16), "er": _sb(C + 32, BF),
+    "ew": _sb(48, U16), "mew": _sb(48, U16), "ik": _sb(E, F32),
+    "fp": _sb(4 * E, BF), "gp": _sb(4 * E, BF), "ge": _sb(4 * C, BF),
+    "at": _sb(4 * K, BF), "z": _sb(4 * C, BF), "zw": _sb(4 * C, BF),
     "dsb": _sb(E, F32), "mr": _sb(E, F32), "ysb": _sb(C, F32),
 }
 for _b in range(8):
@@ -70,7 +83,7 @@ def rank_program(g, core, T, topo):
             cols = range(0, a + 1)
             sl = slice(a, None, -1)
         ap = T[name][p0:p1, sl] if (p0, p1) != (0, 128) else T[name][:, sl]
-        return (ap, [(name, frozenset(cols), p0, p1)])
+        return (ap, [(name, bits(cols), p0, p1, len(cols))])
 
     def ind(win, off, word=False):
         ap = win[0].bitcast(dt.uint32) if word else win[0]
@@ -79,14 +92,10 @@ def rank_program(g, core, T, topo):
     def col(name, c, p0=0, p1=128):
         return v(name, c, c + 1, 1, p0, p1)
 
-    def add(q, fn, outs, ins, ext=(), dma=None, acc=None):
-        rd, wr = [], []
-        for x in ins:
-            if isinstance(x, tuple):
-                rd += x[1]
-        for x in outs:
-            wr += x[1]
-        ops.append({"q": q, "fn": fn, "rd": rd, "wr": wr, "ext": list(ext), "dma": dma, "acc": acc})
+    def add(q, fn, outs, ins, ext=(), dma=None, acc=None, rate=None):
+        ins = [x for x in ins if isinstance(x, tuple)]
+        ops.append({"q": q, "fn": fn, "rd": [r for x in ins for r in x[1]], "wr": [r for x in outs for r in x[1]],
+                    "ext": list(ext), "dma": dma, "acc": acc, "time": length(q, outs, ins, dma, rate)})
 
     def ap(x):
         return x[0] if isinstance(x, tuple) else x
@@ -98,7 +107,7 @@ def rank_program(g, core, T, topo):
             add("v", lambda: g.vector.tensor_scalar(ap(out), ap(a), ap(s1), ap(s2), op0, op1), [out], [a, s1, s2])
 
     def tt(out, a, b, op):
-        add("v", lambda: g.vector.tensor_tensor(ap(out), ap(a), ap(b), op), [out], [a, b])
+        add("v", lambda: g.vector.tensor_tensor(ap(out), ap(a), ap(b), op), [out], [a, b], rate=2.0)
 
     def cp(out, a):
         add("v", lambda: g.vector.tensor_copy(ap(out), ap(a)), [out], [a])
@@ -113,17 +122,18 @@ def rank_program(g, core, T, topo):
         add("v", lambda: g.vector.transpose(ap(out), ap(a)), [out], [a])
 
     def qz(q, s, a):
-        add("v", lambda: g.vector.quantize_mx(ap(q), ap(s), ap(a)), [q, s], [a])
+        add("v", lambda: g.vector.quantize_mx(ap(q), ap(s), ap(a)), [q, s], [a], rate=1.0)
 
     def act(out, a, f, bias=0.0, scale=1.0, accum=None):
-        if accum is None:
-            if f == AF.Copy:
-                add("a", lambda: g.scalar.activation(ap(out), ap(a), f, scale=scale), [out], [a])
-            else:
-                add("a", lambda: g.scalar.activation(ap(out), ap(a), f, bias=ap(bias), scale=scale), [out], [a, bias])
-        else:
+        if accum is not None:
             add("a", lambda: g.scalar.activation(ap(out), ap(a), f, bias=ap(bias), scale=scale, accum_out=ap(accum)),
                 [out, accum], [a, bias])
+        elif f != AF.Copy:
+            add("a", lambda: g.scalar.activation(ap(out), ap(a), f, bias=ap(bias), scale=ap(scale)), [out], [a, bias, scale])
+        elif scale != 1.0:
+            add("a", lambda: g.scalar.activation(ap(out), ap(a), f, scale=scale), [out], [a])
+        else:
+            add("a", lambda: g.scalar.activation(ap(out), ap(a), f), [out], [a])
 
     def mm(bank, w, ws_, wc0, x, xs_, xc0, cols, start=True, stop=True, ext=(), acc=None):
         o, a, b = v(bank, 0, cols), v(w, wc0, wc0 + 128), v(ws_, wc0, wc0 + 128)
@@ -135,6 +145,13 @@ def rank_program(g, core, T, topo):
             add("g", lambda: g.iota(ap(out), pat, base, cm, allow_small_or_imprecise_dtypes=True), [out], [])
         else:
             add("g", lambda: g.iota(ap(out), pat, base, cm), [out], [])
+
+    def fill(out, c):
+        iota(out, [[0, out[1][0][4]]], c, 0, SCRATCH[out[1][0][0]][2] != I32)
+
+    def select(out, pat, op, base, cm):
+        src = v("ones", 0, out[1][0][4])
+        add("g", lambda: g.affine_select(out[0], src[0], pat, op, 0.0, base, cm), [out], [src])
 
     def dma(q, out, a, sem):
         eng = g.sync if q == "s" else g.scalar
@@ -152,6 +169,7 @@ def rank_program(g, core, T, topo):
         for src, land in ((bytes_of(v(qs, 0, cols)), bytes_of(v(qd, c0, c0 + cols))), (v(ss, 0, cols), v(sd, c0, c0 + cols))):
             add("g", lambda src=src, land=land: g.remote_dma(land[0], src[0], T.sem[sem], T.sem.sent, pid, rid, m),
                 [], [src], (), "remote")
+            ops[-1]["raises"] = sem
             sent[0] += len(topo.engines(core, dst))
 
     prev, far = T.cores[(rank - 1) % n], T.cores[(rank + J) % n]
@@ -160,329 +178,271 @@ def rank_program(g, core, T, topo):
 
     dma("s", v("xin"), T.x[:], "dx")
     dma("a", v("uin"), T.u[:], "du")
-    dma("s", bytes_of(v("wq")), T.wc[:], "dw")
-    ops[-1]["rd"] = v("xin")[1]
-    dma("s", v("wp"), T.ws[:], "ds")
-    dma("s", v("vin"), T.v[:], "dv")
+    for out, src, sem in ((bytes_of(v("wq")), T.wc[:], "dw"), (v("wp"), T.ws[:], "ds"), (v("vin"), T.v[:], "dv")):
+        dma("s", out, src, sem)
+        ops[-1]["rd"] = v("xin")[1]
+
+    ID = AF.Identity
+    r_, a_, par, g_, h_, rh, rl_ = [col("pf", k) for k in range(1, 8)]
+
+    def pc(k, p0=0, p1=128):
+        return col("pc", k, p0, p1)
 
     iota(col("pi", 0), [[0, 1]], 0, 1, False)
-    iota(v("uli"), [[16, 8]], 0, 0, False)
-    iota(v("yrow"), [[0, 26], [1, 16]], 0, 0)
     iota(v("c16"), [[16, 32]], 0, 0)
     iota(v("m16"), [[0, 8], [1, 16], [0, 4]], 0, 0)
-    ms(v("rs"), 0.0)
-    ms(v("ones"), 1.0)
-    ts(col("pi", 1), col("pi", 0), 15, OP.bitwise_and)
-    ts(col("pi", 2), col("pi", 0), 4, OP.arith_shift_right)
-    cp(v("ul"), v("uli"))
-    ms(v("rs", 0, E, 16), -BIG)
-    tt(col("pi", 3), col("pi", 0), col("pi", 2), OP.add)
-    ms(v("keep"), 1.0)
+    iota(v("yrow"), [[0, 8], [1, 16]], 0, 0)
+    iota(v("irow"), [[1, HW]], 0, 0)
+    iota(v("irc"), [[1, E]], -HE, 0)
+    iota(v("mhi"), [[1, 8], [0, 16]], 0, 0)
+    iota(v("mrow"), [[1, 128]], 0, 0)
+    for name, c in (("rs", 0.0), ("y0", 0.0), ("pv", -BIG), ("ones", 1.0)):
+        ms(v(name), c)
+    ms(col("sn", SN - 1), 0.0)
+    for u in range(NT):
+        (ms if u < 4 else fill)(v("ct", 4 * (u * E + 16 * (4 * u + 1)), 4 * (u * E + TP[u])), 0)
+    select(v("et"), [[1, 516]], OP.is_equal, -3, -4)
+    select(v("keep"), [[0, NB], [1, 16]], OP.not_equal, 0, 0)
+    fill(v("ctw", 1024 + 3, 1536, 4), 0)
+    fill(v("ctw", 1536 + 3, 9 * 512, 4), 0)
+    fill(v("ot", 3, 8 * GW, 4), 0)
+    for name, c in (("kw", 1024), ("pw", 99)):
+        fill(v(name, 0, PAD), c)
+        fill(v(name, PAD + HW, 272), c)
+    for name, w in (("vm", C), ("er", C), ("mir", E)):
+        fill(v(name, 0, 16), 0)
+        fill(v(name, 16 + w, 32 + w), 0)
+    iota(v("ik"), [[1024, E]], 0, 0)
+    for name in ("tb", "tbs"):
+        fill(v(name, C, E), 0)
+        fill(v(name, E + C + 32, 2 * E + 32), 0)
+    p_ = col("pi", 0)
+    ts(col("pi", 4), p_, 7, OP.bitwise_and)
+    ts(col("pi", 1), p_, 15, OP.bitwise_and)
+    ts(col("pi", 2), p_, 4, OP.arith_shift_right)
+    ts(col("pi", 5), p_, 3, OP.arith_shift_right, 1, OP.bitwise_and)
+    ts(col("pi", 6), p_, 1, OP.arith_shift_right, 7, OP.bitwise_and)
+    ts(col("pi", 7), p_, 1, OP.bitwise_and)
+    tt(col("pi", 3), p_, col("pi", 2), OP.add)
     ts(col("pi", 3), col("pi", 3), 1, OP.bitwise_and)
-    ms(v("keep", 0, 672, 16), 0.0)
     cp(v("pf"), v("pi"))
-    r_, a_, par = col("pf", 1), col("pf", 2), col("pf", 3)
-    ms(v("ct", 6 * 4 * E + 3, 7 * 4 * E, 4), 0.0)
-    ms(v("ctw", 1024 + 3, 7 * 512, 4), 0.0)
-    ms(v("ot", 3, 8 * GW, 4), 0.0)
-    ms(v("bw", 0, PAD), 0.0)
-    ms(v("bw", PAD + HW, 272), 1024.0)
-    ms(v("pw"), 99.0)
-    ms(v("vm"), 0.0)
-    ts(v("mk"), v("yrow"), r_, OP.not_equal, -BIG, OP.mult)
-    ID = AF.Identity
-    pieces = [(0, 0, 128, 1.0, 1.0), (1, 0, 128, -1.0, -1.0), (2, 0, 32, 1.0, 9.0), (2, 32, 64, -11.0, 33.0), (2, 64, 128, -1.0, -5.0)]
-    for s, p0, p1, k, c in pieces:
-        act(col("pc", s, p0, p1), col("pf", 2, p0, p1), ID, c, k)
-        act(col("pc", 8 + s, p0, p1), col("pf", 2, p0, p1), ID, -c + (1.0 if c < 0 else 0.0), -k)
-    act(v("pc", 4, 7), v("pc", 0, 3), AF.Abs)
-    act(v("pc", 12, 15), v("pc", 0, 3), ID, 12.0, -1.0)
-    act(v("pc", 16, 19), v("pc", 0, 3), ID, 0.0, 1024.0)
-    act(col("pc", 23), r_, ID, float(PAD))
-    act(col("pc", 24), col("pc", 2), ID, -12.0)
-    act(col("pc", 25), r_, ID, -512.0, -1024.0)
-    act(col("pc", 26), a_, ID, 8.0)
-    act(col("pc", 27), r_, ID, -8.0)
-    act(col("pc", 28), r_, ID, 0.0, 16.0)
-    act(col("pc", 29), r_, ID, -128.0, 16.0)
-    act(v("pc", 20, 23), v("pc", 0, 3), ID, col("pc", 23))
-    act(v("pc", 32, 35), v("pc", 4, 7), ID, col("pc", 28))
-    act(v("pc", 36, 39), v("pc", 4, 7), ID, col("pc", 29))
-    act(col("pc", 30), r_, ID, 128.0)
-    act(v("pl"), v("c16", 0, 26), ID, col("pc", 30))
-    act(col("pc", 31), par, ID, col("pc", 28), 336.0)
-    act(v("cnf"), v("c16", 0, 32, 16), ID, col("pc", 31))
+    ts(v("ul"), v("rs", 0, 8), g_, OP.add, 16.0, OP.mult)
     qz(v("uq"), v("us"), v("uin"))
+    cp((v("ur")[0].bitcast(dt.uint32), v("ur")[1]), ind(v("uq"), v("ul"), True))
+    act(v("urs"), ind(v("us"), v("ul")), AF.Copy)
+    qz(v("vq"), v("vs"), v("vin"))
+    act(pc(45), h_, ID, 0.0, -BIG)
+    act(pc(46), h_, ID, -BIG, BIG)
+    act(pc(43), a_, ID, rl_, 2.0)
+    act(pc(44), rh, ID, pc(43), 16.0)
+    act(pc(47), h_, ID, -1.0, 1.0)
+    act(pc(48), h_, ID, 0.0, -1.0)
+    for k in range(2):
+        act(v("pm", k, 48, 2), v("c16", 0, 24), ID, pc(45 + k), 0.0)
+        act(v("dm", k, 64, 2), v("c16"), ID, pc(47 + k), 0.0)
+    ts(v("pvl", 0, 3), v("c16", 0, 24, 8), pc(44), OP.add, C - 1.0, OP.min)
+    ts(v("pvl", 4, 5), v("c16", 0, 1), pc(44), OP.add, H - 1.0, OP.min)
+    act(pc(50), a_, ID, 0.0, 2.0)
+    act(pc(54), rl_, ID, -8.0 * 63, 8.0)
+    ts(pc(51), r_, pc(50), OP.is_le, 1.0 / 16, OP.mult)
+    ts(pc(53), rh, a_, OP.is_equal, 1.0 / 8, OP.mult)
+    act(pc(52), pc(51), ID, 31.0, -496.0)
+    act(pc(55), pc(53), ID, 63.0, pc(54))
+    ts(v("dul"), v("c16", 0, 4), 0.5, OP.mult, rh, OP.add)
+    ts(v("ibl"), v("c16", 0, NB), pc(51), OP.mult, pc(52), OP.add)
+    ts(v("exl"), v("c16", 0, NB), pc(53), OP.mult, pc(55), OP.add)
+    for p0, p1, sg_, c in ((0, 64, 1.0, 0.0), (64, 128, -1.0, 11.0)):
+        act(pc(9, p0, p1), col("pf", 2, p0, p1), ID, c, 3.0 * sg_)
+        act(v("pc", 0, 3, 1, p0, p1), v("c16", 0, 3, 1, p0, p1), ID, pc(9, p0, p1), sg_ / 16)
+        act(pc(8, p0, p1), col("pf", 2, p0, p1), ID, sg_, 0.0)
+        act(pc(56, p0, p1), col("pf", 5, p0, p1), ID, (192 - 15.5 / 32) * sg_, HO / 32 * sg_)
+        act(v("hb", 0, HW, 1, p0, p1), v("irow", 0, HW, 1, p0, p1), ID, pc(56, p0, p1), sg_ / 32)
+    act(v("pc", 4, 7), v("pc", 0, 3), AF.Abs)
+    act(v("pc", 57, 60), v("pc", 4, 7), ID, 0.0, -1.0)
+    act(v("pc", 12, 15), v("pc", 0, 3), ID, 0.0, -1.0)
+    act(v("pc", 16, 19), v("pc", 0, 3), ID, 0.0, 1024.0)
+    act(pc(23), r_, ID, float(PAD))
+    act(pc(25), r_, ID, -512.0, -1024.0)
+    act(pc(27), r_, ID, -8.0)
+    act(pc(28), r_, ID, 0.0, 16.0)
+    act(pc(29), r_, ID, -128.0, 16.0)
+    act(pc(49), g_, ID, 8.0)
+    act(v("pc", 20, 23), v("pc", 0, 3), ID, pc(23))
+    act(v("pc", 32, 35), v("pc", 4, 7), ID, pc(28))
+    act(v("pc", 36, 39), v("pc", 4, 7), ID, pc(29))
+    act(pc(30), r_, ID, 128.0)
+    act(v("pl"), v("c16", 0, 26), ID, pc(30))
+    act(pc(31), par, ID, pc(28), E + 16.0)
+    act(v("cnf"), v("c16", 0, 32, 16), ID, pc(31))
+    ts(v("cnl", 0, 2), v("cnf"), 15.0, OP.add, 2 * E + 31.0, OP.min)
+    ts(v("cnl", 2, 4), v("cnf"), 14.0, OP.add, 2 * E + 31.0, OP.min)
     ts(v("m1", 0, 17), v("yrow", 0, 17), r_, OP.is_equal, P, OP.mult)
     ts(v("m2", 0, 17), v("yrow", 0, 17), r_, OP.is_equal, -2 * P, OP.mult)
-    cp((v("ur")[0].bitcast(dt.uint32), v("ur")[1]), ind(v("uq"), v("ul"), True))
-    cp(v("urs"), ind(v("us"), v("ul")))
     ts(v("rl"), v("c16", 0, 26), 0.0, OP.mult, r_, OP.add)
+    ts(pc(40), r_, 0.0, OP.is_equal, 2 * P, OP.mult)
     tt(v("mw16"), v("m1", 0, 16), v("m2", 1, 17), OP.add)
-    ts(col("pc", 40), r_, 0.0, OP.is_equal, 2 * P, OP.mult)
-    act(v("mw"), ind(v("mw16"), v("rl")), AF.Copy)
-    act(col("pc", 41), col("pc", 40), ID, -P)
-    act(col("pc", 42), col("pc", 40), ID, -P - 128.0 * 1024)
-    act(v("co"), v("pl"), ID, col("pc", 42), 1024.0)
-    latch = col("pc", 41)
-
-    def count_tiles():
+    act(pc(42), pc(40), ID, -P - 128.0 * 1024)
+    act(v("mw"), ind(v("mw16"), v("rl", 0, HE // 16)), AF.Copy)
+    act(v("co"), v("pl"), ID, pc(42), 1024.0)
+    for h in range(2):
+        for k in range(2):
+            ts(v("ctw", 512 * h + 256 * k, 512 * h + 256 * k + 256), v("m16", 0, 256), pc(49) if h else g_, OP.is_equal,
+               (1.0 - 2 * k) / 32, OP.mult)
+    qz(v("cwq", 0, 256), v("cws", 0, 256), v("ctw", 0, 1024))
+    for s in range(3):
+        ts(v("ctw", 1024 + s, 1536, 4), v("yrow"), r_, OP.is_equal, pc(8), OP.mult)
+        ts(v("shl", 16 * s, 16 * s + 16), v("c16", 0, 16), pc(20 + s), OP.add)
         for h in range(2):
-            ts(v("ctw", 512 * h, 512 * h + 512), v("m16"), col("pc", 26) if h else a_, OP.is_equal, 1.0 / 32, OP.mult)
-        for s in range(3):
-            ts(v("ctw", 1024 + s, 1536, 4), v("yrow", 0, 128), r_, OP.is_equal)
-            ts(v("shl", 16 * s, 16 * s + 16), v("c16", 0, 16), col("pc", 20 + s), OP.add)
-        qz(v("cwq", 0, 384), v("cws", 0, 384), v("ctw", 0, 1536))
+            ts(v("ctw", 1536 + 512 * h + s, 2048 + 512 * h, 4), v("mhi"), pc(27) if h else r_, OP.is_equal, pc(16 + s), OP.mult)
+            ts(v("ctw", 2560 + 512 * h + s, 3072 + 512 * h, 4), v("mrow"), pc(32 + 4 * h + s), OP.is_equal, 2.0, OP.mult)
+            act(v("ctw", 3584 + 512 * h + s, 4096 + 512 * h, 4), v("ctw", 1536 + 512 * h + s, 2048 + 512 * h, 4), AF.Abs)
+    for a, b in ((2, 3), (3, 5), (5, 7), (7, 9)):
+        qz(v("cwq", 128 * a, 128 * b), v("cws", 128 * a, 128 * b), v("ctw", 512 * a, 512 * b))
+    for b in range(4):
+        qz(v("eq", 128 * b, 128 * b + 128), v("es", 128 * b, 128 * b + 128), v("et", 3 - b, 515 - b))
 
-    def move_tiles():
-        for s in range(3):
-            for h in range(2):
-                ts(v("ctw", 1536 + 512 * h + s, 2048 + 512 * h, 4), v("mhi"), col("pc", 27) if h else r_, OP.is_equal,
-                   col("pc", 16 + s), OP.mult)
+    def back(name, a, b):
+        return (T[name][:, b - 1:a - 1:-1] if a else T[name][:, b - 1::-1], v(name, a, b)[1])
 
-    def far_tiles():
-        for s in range(3):
-            for h in range(2):
-                ts(v("ctw", 2560 + 512 * h + s, 3072 + 512 * h, 4), v("mrow"), col("pc", 32 + 4 * h + s), OP.is_equal,
-                   2.0, OP.mult)
-        ts(v("cnl"), v("cnf"), 15.0, OP.add, 671.0, OP.min)
-        qz(v("cwq", 640, 896), v("cws", 640, 896), v("ctw", 2560, 3584))
+    def slot(k, a, b):
+        base = (k // 4) * 4 * E + k % 4
+        return v("ct", base + 4 * a, base + 4 * b, 4)
 
-    def latch_row(out, row, w):
-        scan(out, row, v("mw", 0, w), -2 * P, OP.max, OP.add)
+    def tri(name, c):
+        return v(name, 8 * c * (c - 1), 8 * c * (c + 1))
 
-    def offsets(out, buf, w):
-        ts(v(out, 0, w // 16), v(buf, 15, w, 16), latch, OP.add)
+    def shifts(s):
+        return v("shl", 16 * s, 16 * s + 15)
+
+    def plane(b):
+        return v("gp", b * E, b * E + E)
+
+    def bank(b):
+        return "b%d" % ((5 + b) % 8)
 
     for t in range(R):
-        last = t == R - 1
-        win, wis, xt = "win%d" % t, "wis%d" % t, "xin" if t == 0 else "xst"
-        qz(v(win, 0, C), v(wis, 0, C), v(xt))
+        first, last = t == 0, t == R - 1
+        win, wis, xt = "win%d" % t, "wis%d" % t, "xin" if first else "xst"
+        halo = [("h%d" % t, n_halo)]
+        qz(v(win, 0, CH), v(wis, 0, CH), v(xt, 0, 4 * CH))
         send(prev, win, wis, C, win, wis, H, "h%d" % t)
-        mm("b0", "ur", "urs", 0, win, wis, 0, C)
-        mm("b2", "ur", "urs", 0, win, wis, 0, C)
-        if t == 0:
-            for b in range(4):
-                o = v("et", 512 * b, 512 * b + 512)
-                add("g", lambda o=o, b=b: g.affine_select(o[0], T.ones[:], [[1, 512]], OP.is_equal, 0.0, -b, -4), [o], [v("ones")])
-            iota(v("mhi"), [[1, 8], [0, 16]], 0, 0)
-            iota(v("mrow"), [[1, 128]], 0, 0)
-            iota(v("irow"), [[1, E]], 0, 0)
+        qz(v(win, CH, C), v(wis, CH, C), v(xt, 4 * CH, 4 * C))
 
-        A_C = list(range(8, 8 + A_N[t]))
-        V_C = [c for c in range(26) if c not in A_C]
-        ES = len(V_C)
-        A0 = ES + 1
-        ve, ae = V_EARLY[t], A_EARLY[t]
+        mm("b0", "ur", "urs", 0, win, wis, 0, CH)
+        mm("b2", "ur", "urs", 0, win, wis, CH, C - CH)
+        mm("b1", "ur", "urs", 0, win, wis, E - 128, 128, ext=halo)
+        act(v("sb", 0, CH), v("b0", 0, CH), AF.Copy)
+        cp(v("sb", CH, C), v("b2", 0, C - CH))
+        act(v("sb", C, E), v("b1", 128 - H, 128), AF.Copy)
+        for l0, l1, o, c0, c1 in ((0, 3, 0, 0, OWN), (4, 5, 48, OWN, NB)):
+            w, k = 16 * (l1 - l0), 2 * (c1 - c0)
+            tt(v("pt", o, o + w), ind(v("sb", 16 * c0, 16 * c1), v("pvl", l0, l1)), v("pm", 0, w), OP.add)
+            tt(v("pv", c0, c1), v("pt", o, o + k, 2), v("pt", o + 1, o + k, 2), OP.max)
+            tt(slot(NB - 1, 16 * c0, 16 * c1), ind(v("pv", 0 if c0 else 0, 32), v("ibl", c0, c1)), v("sb", 16 * c0, 16 * c1), OP.is_gt)
+        for b in range(4):
+            mm(bank(b), "eq", "es", 128 * b, win, wis, 0, E, ext=halo)
+            act(v("fp", b * E, b * E + E), v(bank(b), 0, E), AF.Copy)
 
-        def slot(k, a, b):
-            base = (k // 4) * 4 * E + k % 4
-            return v("ct", base + 4 * a, base + 4 * b, 4)
-
-        def mask_scores(bank, a, b):
-            tt(v("sa", a, b), v(bank, a, b), v("mk", a, b), OP.add)
-
-        def latch_scores(a, b):
-            scan(v("sh", a, b), v("rs", a, b), v("sa", a, b), -BIG, OP.add, OP.max)
-
-        def sj(c):
-            return col("sh", 16 * c + 15)
-
-        started = [False]
-
-        def count(u, end=False):
-            for a, b, hs in ((0, HW, (0,)), (HW, E, (1,))) if end else ((0, E, (0, 1)),):
+        nv = ON_VECTOR[t]
+        for c in range(1, NB):
+            x, below, pivot = slot(c - 1, 0, 16 * c), v("sb", 0, 16 * c), col("pv", c)
+            if c <= nv or c in SHARED[t]:
+                ts(x, below, pivot, OP.is_lt)
+            if c <= nv:
+                scan(v("sn", SN * (c + 1) - 16 * c, SN * (c + 1)), x, x, 0.0, OP.add, OP.max)
+            elif c in SHARED[t]:
+                act(tri("jk", c), x, ID, 0.0, 1.0, col("rs", c))
+            else:
+                act(tri("sg", c), below, AF.Sign, pivot, -1.0)
+                act(x, tri("sg", c), AF.Relu, 0.0, 1.0, col("rs", c))
+        scan(v("seg"), v("keep", 0, E), slot(NB - 1, 0, E), 0.0, OP.mult, OP.add)
+        tt(v("y0", 0, nv + 1), v("sn", SN - 1, SN * (nv + 1), SN), v("seg", 15, 16 * nv + 16, 16), OP.add)
+        tt(v("y0", nv + 1, NB), v("rs", nv + 1, NB), v("seg", 16 * nv + 31, E, 16), OP.add)
+        tt(v("y1"), ind(v("y0"), v("dul")), v("dm"), OP.mult)
+        ts(v("hi"), v("y1"), DIG, OP.add)
+        tt(v("lo"), v("y1"), v("hi"), OP.subtract)
+        act(slot(NB, 0, 256), ind(v("hi"), v("exl", 0, 16)), ID, -DIG)
+        ts(slot(NB + 1, 0, 256), ind(v("lo"), v("exl", 0, 16)), DIG, OP.add)
+        act(slot(NB, 256, E), ind(v("hi"), v("exl", 16, NB)), ID, -DIG)
+        act(slot(NB + 1, 256, E), ind(v("lo"), v("exl", 16, NB)), ID, DIG)
+        for u in (3, 2, 1, 0, 4, 5, 6):
+            w = TP[u] if first else TW[u]
+            for a, b, hs in ((0, HW, (0,)), (HW, E, (1,))) if u == 6 else ((0, w, (0, 1) if TW[u] > HO else (0,)),):
                 qz(v("cq", u * E + a, u * E + b), v("cs", u * E + a, u * E + b), v("ct", 4 * (u * E + a), 4 * (u * E + b)))
                 for h in hs:
-                    mm("b4", "cwq", "cws", 128 * h, "cq", "cs", u * E + HO * h, HW, not started[0], end and h == 1, (), ("st", t))
-                    started[0] = True
+                    mm("b4", "cwq", "cws", 128 * h, "cq", "cs", u * E + HO * h, max(128, min(HW, TW[u] - HO * h)),
+                       (u, h) == (3, 0), (u, h) == (6, 1), (), ("st", t))
 
-        def sg(k, a, b):
-            return v("sg", k * E + a, k * E + b)
-
-        def p1(k, bank, a, b):
-            act(sg(k, a, b), v(bank, a, b), AF.Sign, sj(A_C[k]), -1.0)
-
-        def p2gt(k):
-            act(slot(A0 + k, 0, 16 * A_C[k] + 16), sg(k, 0, 16 * A_C[k] + 16), AF.Relu)
-
-        def p2ge(k):
-            act(slot(A0 + k, 16 * A_C[k] + 16, E), sg(k, 16 * A_C[k] + 16, E), AF.Sign, 1.0)
-
-        mask_scores("b0", 128, 224)
-        mask_scores("b0", 0, 128)
-        latch_scores(128, 224)
-        mask_scores("b0", 224, C)
-        latch_scores(0, 128)
-        latch_scores(224, C)
-        if t == 0:
-            count_tiles()
-        for k in range(ae):
-            p1(k, "b2", 0, C)
-            if k:
-                p2gt(k - 1)
-        p2gt(ae - 1)
-        for k in range(8):
-            ts(slot(k, 0, 16 * k + 16), v("b0", 0, 16 * k + 16), sj(k), OP.is_lt)
-        tt(slot(ES, 0, C), v("b0", 0, C), v("sh", 0, C), OP.is_equal)
-        for k in range(ve):
-            ts(slot(k, 16 * k + 16, C), v("b0", 16 * k + 16, C), sj(k), OP.is_le)
-        mm("b1", "ur", "urs", 0, win, wis, 0, E, ext=[("h%d" % t, n_halo)])
-        mm("b3", "ur", "urs", 0, win, wis, 0, E)
-        mask_scores("b1", C, E)
-        ts(slot(0, C, E), v("b1", C, E), sj(0), OP.is_le)
-        latch_scores(C, E)
-        for k in range(1, ve):
-            ts(slot(k, C, E), v("b1", C, E), sj(k), OP.is_le)
-        tt(slot(ES, C, E), v("b1", C, E), v("sh", C, E), OP.is_equal)
-        for k in range(ae):
-            p1(k, "b3", C, E)
-        p1(ae, "b3", 0, E)
-        for k in range(ae):
-            p2ge(k)
-        for k in range(ae, len(A_C)):
-            if k + 1 < len(A_C):
-                p1(k + 1, "b3", 0, E)
-            p2gt(k)
-            p2ge(k)
-
-        def vblock(k):
-            c = V_C[k]
-            if c >= 8:
-                ts(slot(k, 0, 16 * c + 16), v("b1", 0, 16 * c + 16), sj(c), OP.is_lt)
-            if 16 * c + 16 < E:
-                ts(slot(k, 16 * c + 16, E), v("b1", 16 * c + 16, E), sj(c), OP.is_le)
-
-        for k in range(ve, 7):
-            vblock(k)
-        count(0)
-        vblock(7)
-        if t == 0:
-            qz(v("eq"), v("es"), v("et"))
-        vblock(8)
-        count(1)
-        for b in range(3):
-            mm("b%d" % (5 + b), "eq", "es", 128 * b, win, wis, 0, E)
-        vblock(9)
-        vblock(10)
-        count(4)
-        vblock(11)
-        vblock(12)
-        count(2)
-        vblock(13)
-        if ES > 14:
-            vblock(14)
-        count(5)
-        if t == 0:
-            qz(v("vq"), v("vs"), v("vin"))
-        count(3)
-        count(6, True)
-        if t == 0:
-            move_tiles()
-        mm("b0", "eq", "es", 384, win, wis, 0, E)
-
-        def shifts(s):
-            return v("shl", 16 * s, 16 * s + 15)
-
-        ts(v("bw", PAD, PAD + HW), v("b4", 0, HW), 192.0 - 16.5 / 32, OP.add)
-        ts(v("bi", 0, GW), v("bw", PAD, PAD + GW), col("pc", 8), OP.add)
+        tt(v("kw", PAD, PAD + HW), v("b4", 0, HW), v("hb"), OP.add)
+        ts(v("bi", 0, GW), v("kw", PAD, PAD + GW), pc(4), OP.subtract)
         for s in (1, 2):
-            act(v("bi", s * GW, s * GW + GW), v("bw", PAD, PAD + GW), ID, col("pc", 8 + s))
+            act(v("bi", s * GW, s * GW + GW), v("kw", PAD, PAD + GW), ID, pc(57 + s))
         for s in range(3):
-            tt(v("ot", s, 4 * GW, 4), ind(v("bw"), shifts(s)), v("bi", s * GW, s * GW + GW), OP.is_lt)
-
-        def unpack(b):
-            act(v("fp", b * E, b * E + E), v("b%d" % ((5 + b) % 8), 0, E), AF.Copy)
-
-        for b in range(3):
-            unpack(b)
+            tt(v("ot", s, 4 * GW, 4), ind(v("kw"), shifts(s)), v("bi", s * GW, s * GW + GW), OP.is_lt)
         qz(v("oq", 0, GW), v("osx", 0, GW), v("ot", 0, 4 * GW))
         mm("b4", "cwq", "cws", 256, "oq", "osx", 0, HW)
-        if t == 0:
-            qz(v("cwq", 384, 640), v("cws", 384, 640), v("ctw", 1536, 2560))
         cp(v("pw", PAD, PAD + HW), v("b4", 0, HW))
-        act(v("ab"), ind(v("pw"), shifts(2)), AF.Abs, col("pc", 24))
+        act(v("ab"), ind(v("pw"), shifts(2)), AF.Abs, pc(2))
         for s in range(2):
-            ts(v("ot", 4 * GW + s, 8 * GW, 4), ind(v("pw"), shifts(s)), col("pc", 12 + s), OP.is_equal)
+            ts(v("ot", 4 * GW + s, 8 * GW, 4), ind(v("pw"), shifts(s)), pc(12 + s), OP.is_equal)
         act(v("ot", 4 * GW + 2, 8 * GW, 4), v("ab"), AF.Relu, 1.0, -1.0)
-        unpack(3)
         qz(v("oq", GW, 2 * GW), v("osx", GW, 2 * GW), v("ot", 4 * GW, 8 * GW))
         mm("b1", "cwq", "cws", 384, "oq", "osx", GW, HE)
         mm("b4", "cwq", "cws", 512, "oq", "osx", GW + HE - HO, HE)
         mm("b2", "cwq", "cws", 512, "oq", "osx", GW - HO, E)
         mm("b2", "cwq", "cws", 384, "oq", "osx", GW, HE)
-        if t == 0:
-            far_tiles()
-        mm("b3", "cwq", "cws", 768, "oq", "osx", GW - HO, C)
-        mm("b3", "cwq", "cws", 640, "oq", "osx", GW, HE)
+        for bk_, w0 in (("b0", 896), ("b3", 640)):
+            mm(bk_, "cwq", "cws", w0 + 128, "oq", "osx", GW - HO, C)
+            mm(bk_, "cwq", "cws", w0, "oq", "osx", GW, HE)
 
-        scan(v("xs", 0, HE), v("irow", 0, HE), v("b1", 0, HE), 0.0, OP.max, OP.add)
-        latch_row(v("sc", 0, HE), v("b1", 0, HE), HE)
-        latch_row(v("sc", HE, E), v("b4", 0, HE), HE)
-        scan(v("xs", HE, E), v("irow", HE, E), v("b4", 0, HE), col("xs", HE - 1), OP.max, OP.add)
+        for k, bk_ in enumerate(("b1", "b4")):
+            scan(v("sc", k * HE, k * HE + HE), v(bk_, 0, HE), v("mw", 0, HE), -2 * P, OP.max, OP.add)
         tt(v("t26"), v("sc", 15, E, 16), v("co"), OP.add)
-        scan(v("mir", E - 1, None, -1), v("ones", 0, E), v("xs", E - 1, None, -1), 1000.0, OP.add, OP.min)
         ts(v("ow"), v("t26"), 1.0 / 1024, OP.mult)
-        act(v("ad"), v("b2", 0, C), AF.Abs)
-        act(v("ad2"), v("ad"), AF.Sign, col("pc", 25), 1.0, v("acc"))
+        act(v("ad2"), v("b0", 0, C), AF.Sign, pc(25), 1.0, v("acc"))
+        act(v("dl"), v("b2", 0, E), ID, 0.0, rl_)
+        scan(v("xs"), v("irc"), v("dl"), -float(HE), OP.max, OP.add)
+        scan(back("mir", 16, 16 + E), v("ones", 0, E), back("xs", 0, E), 500.0, OP.add, OP.min)
         for b in range(4):
-            act(v("gp", b * E, b * E + E), ind(v("fp", b * E, b * E + E), v("ow")), AF.Copy, 0.0, -0.5)
-
-        def plane(b):
-            return v("gp", b * E, b * E + E)
-
-        def whole(b):
-            act(v("gf", b * C, b * C + C), v("gp", b * E, b * E + C), AF.Copy, 0.0, -2.0)
+            act(plane(b), ind(v("fp", b * E, b * E + E), v("ow")), AF.Copy, 0.0, -0.5)
 
         scan(v("val"), v("b3", 0, C), v("ones", 0, C), v("acc"), OP.add, OP.mult)
         tt(v("vm", 16, 16 + C), v("b3", 0, C), v("val"), OP.mult)
         tr(v("tb", 0, C), v("vm", 16, 16 + C))
-        tr(v("tb", C, 672), v("vm"))
+        tr(v("tb", E, E + C + 32), v("vm"))
         scan(v("tbs", 0, C), v("keep", 0, C), v("tb", 0, C), 0.0, OP.mult, OP.add)
-        scan(v("tbs", C, 672), v("keep", C, 672), v("tb", C, 672), 0.0, OP.mult, OP.add)
-        ts(v("rkw"), ind(v("tbs"), v("cnl")), 0.25, OP.mult, 159.0, OP.add)
-        cp(ind(v("er"), v("rkw", 0, 20)), v("irow", 0, C))
-        ops[-1]["wr"], ops[-1]["rd"] = v("er")[1], v("rkw", 0, 20)[1] + v("irow", 0, C)[1]
-        cp(v("rf"), v("rkw", 0, 20))
-        latch_row(v("sce"), v("er", 0, K), K)
-        ts(v("rt"), v("rf"), 128.0, OP.is_ge, 1024.0, OP.mult)
-        offsets("ew", "sce", K)
-        whole(0)
-        whole(1)
-        act(v("mer"), ind(v("mir"), v("ew")), AF.Copy)
-        mw_ = E if last else C
-        latch_row(v("sc2", 0, mw_), v("mir", 0, mw_), mw_)
-        latch_row(v("scm"), v("mer"), K)
-        tt(v("ru"), v("rt"), v("rf"), OP.add)
-        offsets("mew", "scm", K)
-        offsets("mrw", "sc2", mw_)
-        for b in range(4):
-            act(v("ge", b * K, b * K + K), ind(plane(b), v("ew")), AF.Copy, 0.0, -2.0)
-        for b in range(4):
-            tt(v("at", b, 4 * K, 4), ind(plane(b), v("mew")), v("ge", b * K, b * K + K), OP.add)
-        tt(v("rv"), v("ru"), v("pl", 0, 20), OP.min)
-        qz(v("aq%d" % t), v("as%d" % t), v("at"))
-        send(far, "al%d" % t, "als%d" % t, 0, "aq%d" % t, "as%d" % t, K, "f%d" % t)
-
-        cp(v("bk"), v("rv"))
-        for b in range(2, 4):
-            whole(b)
-        for b in range(4):
-            act(v("a32", b * K, b * K + K), v("at", b, 4 * K, 4), AF.Copy, 0.0, 32.0)
-        W = K + C
-        for b in range(4):
-            tt(v("z", b * C, b * C + C), ind(plane(b), v("mrw", 0, 20)), v("gf", b * C, b * C + C), OP.add)
-            act(v("zw", b * W + K, b * W + W), v("z", b * C, b * C + C), AF.Copy, 0.0, 32.0)
+        scan(v("tbs", E, E + C + 32), v("keep", 0, C + 32), v("tb", E, E + C + 32), 0.0, OP.mult, OP.add)
+        ts(v("rkw"), ind(v("tbs"), v("cnl", 0, 2)), 0.25, OP.mult, 159.0, OP.add)
+        cp(ind(v("er", 16, 16 + C), v("rkw", 0, 20)), v("mir", 16, 16 + C))
+        ops[-1]["wr"], ops[-1]["rd"] = v("er", 16, 16 + C)[1], v("rkw", 0, 20)[1] + v("mir", 16, 16 + C)[1]
+        for k0, k1, o0, wide in ((0, K, 0, 1), (K, C, 16, 2)):
+            tr(v("tb", k0, k1), v("er", 16 + k0, 16 + k1))
+            tr(v("tb", E + k0 + (32 if k0 else 0), E + k1 + 32), v("er", k0 + (32 if k0 else 0), k1 + 32))
+            ts(v("ew", o0, o0 + 16 * wide), ind(v("tb"), v("cnl", 2, 2 + wide)), float(HE), OP.add)
+            ts(v("mew", o0, o0 + 16 * wide), ind(v("tb"), v("cnl", 0, wide)), float(HE), OP.add)
+            e_, m_ = [v(name, o0 + k0 // 16, o0 + k1 // 16) for name in ("ew", "mew")]
+            for b in range(4):
+                gb = v("ge", b * C + k0, b * C + k1)
+                zb = v("z", b * C + k0, b * C + k1) if k0 else v("at", b, 4 * K, 4)
+                act(gb, ind(plane(b), e_), AF.Copy, 0.0, -2.0)
+                tt(zb, ind(plane(b), m_), gb, OP.add)
+                act(v("zw", b * C + k0, b * C + k1), zb, AF.Copy, 0.0, 32.0)
+            if k0 == 0:
+                qz(v("aq%d" % t), v("as%d" % t), v("at"))
+                send(far, "al%d" % t, "als%d" % t, 0, "aq%d" % t, "as%d" % t, K, "f%d" % t)
         if last:
-            act(v("dsb"), v("b2", 0, E), AF.Copy, 0.0, 1.0 / 1024)
+            tr(v("tm", 0, E), v("mir", 16, 16 + E))
+            tr(v("tm", E, 2 * E + 32), v("mir"))
+            ts(v("mrw"), ind(v("tm"), v("cnl", 0, 2)), float(HE), OP.add)
+            tt(v("dsb"), v("b2", 0, E), v("ik"), OP.add)
+            act(v("mr"), ind(v("dsb"), v("mrw", 0, NB)), AF.Copy, 0.0, 1.0 / 1024)
+            dma("s", T.lm[:], (T.mr[0:128:16, :], v("mr")[1]), "ol")
 
         for b in range(4):
-            mm("b%d" % ((5 + b) % 8), "wq", "wp", 128 * b, "al%d" % t, "als%d" % t, 0, K,
-               ext=[("f%d" % t, n_far)] if b == 0 else ())
-        for b in range(4):
-            tt(v("zw", b * W, b * W + K), v("b%d" % ((5 + b) % 8), 0, K), v("a32", b * K, b * K + K), OP.add)
-        for b, lo, hi, on_scalar in ((0, 0, C, 1), (1, 0, C, 1), (2, C // 2, C, 0), (3, 0, C, 0), (2, 0, C // 2, 1)):
-            src = ind(v("zw", b * W, b * W + W), v("bk", lo // 16, hi // 16))
+            mm(bank(b), "wq", "wp", 128 * b, "al%d" % t, "als%d" % t, 0, K, ext=[("f%d" % t, n_far)])
+            tt(v("zw", b * C, b * C + K), v(bank(b), 0, K), v("zw", b * C, b * C + K), OP.add)
+        for b, lo, hi, on_scalar in ((0, 0, C, 1), (1, 0, C, 1), (2, XS, C, 0), (3, 0, C, 0), (2, 0, XS, 1)):
+            src = ind(v("zw", b * C, b * C + C), v("rkw", lo // 16, hi // 16))
             if on_scalar:
                 act(v("xst", 4 * lo + b, 4 * hi, 4), src, AF.Copy, 0.0, 1.0 / 32)
             else:
@@ -490,25 +450,46 @@ def rank_program(g, core, T, topo):
 
     qz(v("fq"), v("fs"), v("xst"))
     mm("b1", "vq", "vs", 0, "fq", "fs", 0, C)
-    tt(v("mr"), ind(v("dsb"), v("mrw")), v("mir"), OP.add)
     act(v("ysb"), v("b1", 0, C), AF.Copy)
     dma("s", T.oc[:], bytes_of(v("fq")), "ocs")
     for k in range(4):
         dma("s", T.osc[4 * k:4 * k + 4, :], v("fs", 0, C, 1, 32 * k, 32 * k + 4), "ocs")
     dma("a", T.y[:], v("ysb"), "oy")
-    dma("s", T.lm[:], (T.mr[0:128:16, :], v("mr")[1]), "ol")
 
-    emit(g, T, ops, sent[0])
+    emit(g, T, arrange(ops), sent[0])
+
+
+def bits(cols):
+    return ((1 << len(cols) * cols.step) - 1) // ((1 << cols.step) - 1) << cols.start
 
 
 def meets(a, b):
     if a[0] != b[0] or a[3] <= b[2] or b[3] <= a[2]:
         return False
-    return SCRATCH[a[0]][0] == "psum" or not a[1].isdisjoint(b[1])
+    return SCRATCH[a[0]][0] == "psum" or a[1] & b[1] != 0
 
 
-def emit(g, T, ops, sent):
-    eng = {"v": g.vector, "a": g.scalar, "t": g.tensor, "g": g, "s": g.sync}
+def length(q, outs, ins, dma, rate):
+    if dma:
+        return 300.0 if dma == "remote" else 60.0
+    n = outs[0][1][0][4]
+    full = [x[1][0][0] for x in outs[:1] + ins if x[1][0][4] == n]
+    if q == "t":
+        return 0.6 * (n + 16)
+    if q == "g":
+        return 150 + 2.0 * CYCLE * n
+    if len(outs[0][1]) > 1:
+        return 50 + 3.8 * CYCLE * n
+    if any(len(x[1]) > 1 for x in ins):
+        return 60 + 1.56 * CYCLE * n
+    if rate == 2.0 and any(SCRATCH[b][0] == "psum" for b in full):
+        rate = 1.0
+    if rate is None:
+        rate = 0.5 if q == "v" and all(SCRATCH[b][2] in (BF, U16) for b in full) else 1.0
+    return (30 if q == "v" else 60) + CYCLE * max(32.0, rate * n)
+
+
+def depends(ops):
     deps = []
     by_buf = {}
     for i, o in enumerate(ops):
@@ -530,6 +511,78 @@ def emit(g, T, ops, sent):
         for kind, regs in (("r", o["rd"]), ("w", o["wr"])):
             for reg in regs:
                 by_buf.setdefault(reg[0], []).append((i, kind, reg))
+    return deps
+
+
+def arrange(ops):
+    deps = [{j: HOP + (LOAD if ops[j]["dma"] else 0.0) for j in d} for d in depends(ops)]
+    groups, sends = {}, {}
+    for i, o in enumerate(ops):
+        if o["acc"] is not None:
+            groups.setdefault(o["acc"], []).append(i)
+        if o["dma"] == "remote":
+            if sends:
+                deps[i][max(sends.values())] = 0.0
+            sends[o["raises"]] = i
+        for sem, _ in o["ext"]:
+            deps[i][sends[sem]] = TRAVEL
+    for members in groups.values():
+        for i in members[1:]:
+            deps[i][members[0]] = 0.0
+        for i in members[:-1]:
+            deps[members[-1]][i] = 0.0
+    time = [o["time"] for o in ops]
+    time[min(i for i, o in enumerate(ops) if o["dma"] == "remote")] += FIRST
+    back = [{} for _ in ops]
+    for i, d in enumerate(deps):
+        for j, gap in d.items():
+            back[j][i] = gap
+    tail = [LOAD if o["dma"] and o["dma"] != "remote" else 0.0 for o in ops]
+    after, below = list(tail), [set() for _ in ops]
+    for i in reversed(range(len(ops))):
+        for j, gap in back[i].items():
+            after[i] = max(after[i], gap + time[j] + after[j])
+            below[i] |= below[j] | {j}
+        load = {}
+        for j in sorted(below[i], key=lambda k: -after[k]):
+            load[ops[j]["q"]] = load.get(ops[j]["q"], 0.0) + time[j]
+            after[i] = max(after[i], load[ops[j]["q"]] + after[j])
+    free, start, left = {}, {}, [len(d) for d in deps]
+    ready = {i: 0.0 for i, d in enumerate(deps) if not d}
+    while ready:
+        at = {i: max(x, free.get(ops[i]["q"], 0.0)) for i, x in ready.items()}
+        i = min(at, key=lambda k: (at[k], -time[k] - after[k], k))
+        start[i] = at[i]
+        free[ops[i]["q"]] = at[i] + time[i]
+        del ready[i]
+        for j in back[i]:
+            left[j] -= 1
+            if not left[j]:
+                ready[j] = max(start[m] + time[m] + gap for m, gap in deps[j].items())
+
+    def place(order, before, least):
+        busy, begin = {}, {}
+        for i in order:
+            at = max([begin[j] + time[j] + gap for j, gap in before[i].items()] + [least[i]])
+            line = busy.setdefault(ops[i]["q"], [])
+            k = 0
+            while k < len(line) and at + time[i] > line[k][0]:
+                at = max(at, line[k][1])
+                k += 1
+            line.insert(k, (at, at + time[i]))
+            begin[i] = at
+        return begin
+
+    every, zero = range(len(ops)), [0.0] * len(ops)
+    for _ in range(PASSES):
+        late = place(sorted(every, key=lambda k: (-start[k] - time[k], -k)), back, tail)
+        start = place(sorted(every, key=lambda k: (-late[k] - time[k], k)), deps, zero)
+    return [ops[i] for i in sorted(every, key=lambda k: (start[k], k))]
+
+
+def emit(g, T, ops, sent):
+    eng = {"v": g.vector, "a": g.scalar, "t": g.tensor, "g": g, "s": g.sync}
+    deps = depends(ops)
     known_q = {q: ({}, set()) for q in eng}
     done = []
     waits = []
@@ -568,11 +621,12 @@ def emit(g, T, ops, sent):
             s = "q" + o["q"]
             total[s] = total.get(s, 0) + 1
             count[i] = (s, total[s])
-    waited = {}
+    waited, landed = {}, set()
     for i, o in enumerate(ops):
         e = eng[o["q"]]
-        for s, c in [count[j] for j in waits[i]] + o["ext"]:
+        for s, c in [count[j] for j in waits[i]] + [x for x in o["ext"] if x not in landed]:
             e.wait_ge(T.sem[s], c)
+            landed.add((s, c))
             waited[s] = max(waited.get(s, 0), c)
         ins = o["fn"]()
         if i in count:

@@ -3,20 +3,21 @@ from concourse.mybir import dt, AluOpType as OP, ActivationFunctionType as AF
 C, H, E, K, J, R = 320, 96, 416, 128, 2, 2
 HW, GW, HO, PAD = 232, 240, 184, 16
 HE = E // 2
-CH = 192
-NB, OWN = E // 16, C // 16
+NB = E // 16
+PIECES = ((0, 128), (128, C), (C, E))
+EDGE = C - 16
 BIG = 2.0 ** 96
-P = 2.0 ** 21
+P = 1024.0
 DIG = 6144.0
 ON_VECTOR = (14, 16)
 SHARED = ((25, 24, 23, 22), (25, 24))
-XS = 128
 SN = 256
+AW = 160
+GATHERS = [(b, 0, 128, b < 1) for b in range(4)] + [(b, 128, C, b < 3) for b in range(4)]
 NT = 7
 TW = [128, 128, 192, 256, 320, 384, E]
 TP = [128, 128, HO + 128, HO + 128, 320, 384, E]
-CYCLE = 0.9
-HOP, LOAD = 170.0, 2000.0
+CYCLE, HOP, LOAD = 0.9, 170.0, 2000.0
 TRAVEL, FIRST = 1500.0, 2000.0
 PASSES = 2
 
@@ -36,33 +37,33 @@ SCRATCH = {
     "aq0": _sb(K, Q4), "as0": _sb(K, U8), "aq1": _sb(K, Q4), "as1": _sb(K, U8),
     "al0": _sb(K, Q4), "als0": _sb(K, U8), "al1": _sb(K, Q4), "als1": _sb(K, U8),
     "pi": _sb(8, I32), "pf": _sb(8, F32), "pc": _sb(64, F32), "ul": _sb(8, U16),
-    "yrow": _sb(128, BF), "m16": _sb(512, BF), "mrow": _sb(128, BF), "mhi": _sb(128, BF), "c16": _sb(32, F32),
-    "irow": _sb(HW, F32), "irc": _sb(E, BF), "ones": _sb(516, BF), "hb": _sb(HW, F32),
-    "pvl": _sb(6, U16), "pm": _sb(48, F32), "ibl": _sb(NB, U16), "exl": _sb(NB, U16), "dul": _sb(4, U16), "dm": _sb(64, F32),
-    "m1": _sb(32, F32), "m2": _sb(32, F32), "mw16": _sb(16, F32), "rl": _sb(26, U16), "mw": _sb(HE, F32),
-    "co": _sb(26, F32), "pl": _sb(26, F32), "shl": _sb(48, U16), "cnf": _sb(2, F32), "cnl": _sb(4, U16),
+    "yrow": _sb(128, BF), "m16": _sb(320, BF), "mrow": _sb(256, BF), "mhi": _sb(256, BF), "c16": _sb(32, F32),
+    "irow": _sb(HW, F32), "irc": _sb(E, BF), "ones": _sb(516, BF), "hb": _sb(2 * HW, F32),
+    "pvl": _sb(4, U16), "pm": _sb(32, F32), "ibl": _sb(12, U16), "exl": _sb(NB, U16), "dul": _sb(4, U16), "dm": _sb(64, F32),
+    "m0": _sb(16, F32), "m1": _sb(16, F32), "m2": _sb(32, F32), "mw16": _sb(16, F32), "mw": _sb(E, F32),
+    "shl": _sb(48, U16), "cnf": _sb(2, F32), "cnl": _sb(4, U16),
     "keep": _sb(E, BF), "ctw": _sb(9 * 512, BF), "cwq": _sb(9 * 128, Q4), "cws": _sb(9 * 128, U8),
     "et": _sb(516, BF), "eq": _sb(512, Q4), "es": _sb(512, U8),
-    "sb": _sb(E, F32), "pt": _sb(64, F32), "pv": _sb(32, F32), "sg": _sb(8 * NB * NB, BF), "jk": _sb(8 * NB * NB, BF),
+    "sb": _sb(E, F32), "pt": _sb(96, F32), "pv": _sb(48, F32), "sg": _sb(8 * NB * NB, BF), "jk": _sb(8 * NB * NB, BF),
     "rs": _sb(32, F32), "sn": _sb(SN * 17, BF), "seg": _sb(E, BF),
     "y0": _sb(32, F32), "y1": _sb(64, F32), "hi": _sb(64, BF), "lo": _sb(64, F32),
-    "ct": _sb(NT * 4 * E, BF), "cq": _sb(NT * E, Q4), "cs": _sb(NT * E, U8),
+    "ct": _sb(NT * 4 * E, BF), "cq": _sb(NT * E + 2 * GW, Q4), "cs": _sb(NT * E + 2 * GW, U8),
     "kw": _sb(272, BF), "bi": _sb(3 * GW, BF), "pw": _sb(272, BF), "ab": _sb(GW, BF),
-    "ot": _sb(8 * GW, BF), "oq": _sb(2 * GW, Q4), "osx": _sb(2 * GW, U8),
-    "sc": _sb(E, F32), "t26": _sb(26, F32), "ow": _sb(26, U16), "dl": _sb(E, BF),
+    "ot": _sb(8 * GW, BF), "eg": _sb(96, F32),
+    "sc": _sb(E, F32), "ow": _sb(NB, U16), "dl": _sb(E, BF),
     "xs": _sb(E, BF), "mir": _sb(E + 32, BF), "tm": _sb(2 * E + 32, BF), "mrw": _sb(32, U16),
-    "ad2": _sb(C, BF), "acc": _sb(1, F32), "val": _sb(C, BF), "vm": _sb(C + 32, BF),
+    "ad": _sb(EDGE + 32, BF), "ad2": _sb(EDGE + 32, BF), "acc": _sb(1, F32), "val": _sb(C, BF), "vm": _sb(C + 32, BF),
     "tb": _sb(2 * E + 32, BF), "tbs": _sb(2 * E + 32, BF), "rkw": _sb(32, U16), "er": _sb(C + 32, BF),
-    "ew": _sb(48, U16), "mew": _sb(48, U16), "ik": _sb(E, F32),
+    "ew": _sb(48, U16), "mew": _sb(48, U16),
     "fp": _sb(4 * E, BF), "gp": _sb(4 * E, BF), "ge": _sb(4 * C, BF),
     "at": _sb(4 * K, BF), "z": _sb(4 * C, BF), "zw": _sb(4 * C, BF),
-    "dsb": _sb(E, F32), "mr": _sb(E, F32), "ysb": _sb(C, F32),
+    "orow": _sb(E, BF), "mr": _sb(E, F32), "ysb": _sb(C, F32),
 }
 for _b in range(8):
     SCRATCH["b%d" % _b] = ("psum", [128, 512], F32)
 
 SEMAPHORES = ["qv", "qa", "qt", "qg", "h0", "h1", "f0", "f1", "sent",
-              "dx", "du", "dv", "dw", "ds", "oy", "ol", "ocs"]
+              "dx", "dy", "du", "dv", "dw", "ds", "oy", "ol", "ocs"]
 
 
 def rank_program(g, core, T, topo):
@@ -73,17 +74,13 @@ def rank_program(g, core, T, topo):
     ops = []
 
     def v(name, a=0, b=None, s=1, p0=0, p1=128):
-        w = SCRATCH[name][1][1]
-        if s > 0:
-            b = w if b is None else b
-            cols = range(a, b, s)
-            b = cols[-1] + 1
-            sl = slice(a, b, s) if s > 1 else slice(a, b)
-        else:
-            cols = range(0, a + 1)
-            sl = slice(a, None, -1)
+        cols = range(a, SCRATCH[name][1][1] if b is None else b, s)
+        sl = slice(a, cols[-1] + 1, s) if s > 1 else slice(a, cols[-1] + 1)
         ap = T[name][p0:p1, sl] if (p0, p1) != (0, 128) else T[name][:, sl]
         return (ap, [(name, bits(cols), p0, p1, len(cols))])
+
+    def back(name, a, b):
+        return (T[name][:, b - 1:a - 1:-1] if a else T[name][:, b - 1::-1], v(name, a, b)[1])
 
     def ind(win, off, word=False):
         ap = win[0].bitcast(dt.uint32) if word else win[0]
@@ -147,7 +144,7 @@ def rank_program(g, core, T, topo):
             add("g", lambda: g.iota(ap(out), pat, base, cm), [out], [])
 
     def fill(out, c):
-        iota(out, [[0, out[1][0][4]]], c, 0, SCRATCH[out[1][0][0]][2] != I32)
+        iota(out, [[0, out[1][0][4]]], c, 0)
 
     def select(out, pat, op, base, cm):
         src = v("ones", 0, out[1][0][4])
@@ -176,8 +173,9 @@ def rank_program(g, core, T, topo):
     n_halo = 2 * len(topo.engines(T.cores[(rank + 1) % n], core))
     n_far = 2 * len(topo.engines(T.cores[(rank - J) % n], core))
 
-    dma("s", v("xin"), T.x[:], "dx")
+    dma("s", v("xin", 0, 512), T.x[:, 0:512], "dx")
     dma("a", v("uin"), T.u[:], "du")
+    dma("s", v("xin", 512, 4 * C), T.x[:, 512:4 * C], "dy")
     for out, src, sem in ((bytes_of(v("wq")), T.wc[:], "dw"), (v("wp"), T.ws[:], "ds"), (v("vin"), T.v[:], "dv")):
         dma("s", out, src, sem)
         ops[-1]["rd"] = v("xin")[1]
@@ -190,12 +188,13 @@ def rank_program(g, core, T, topo):
 
     iota(col("pi", 0), [[0, 1]], 0, 1, False)
     iota(v("c16"), [[16, 32]], 0, 0)
-    iota(v("m16"), [[0, 8], [1, 16], [0, 4]], 0, 0)
+    iota(v("m16"), [[0, 5], [1, 16], [0, 4]], 0, 0)
     iota(v("yrow"), [[0, 8], [1, 16]], 0, 0)
     iota(v("irow"), [[1, HW]], 0, 0)
     iota(v("irc"), [[1, E]], -HE, 0)
-    iota(v("mhi"), [[1, 8], [0, 16]], 0, 0)
-    iota(v("mrow"), [[1, 128]], 0, 0)
+    iota(v("mhi"), [[1, 16], [0, 16]], 0, 0)
+    iota(v("mrow"), [[1, 256]], 0, 0)
+    iota(v("eg", 64, 96), [[-1, 32]], C - EDGE, 0)
     for name, c in (("rs", 0.0), ("y0", 0.0), ("pv", -BIG), ("ones", 1.0)):
         ms(v(name), c)
     ms(col("sn", SN - 1), 0.0)
@@ -206,13 +205,13 @@ def rank_program(g, core, T, topo):
     fill(v("ctw", 1024 + 3, 1536, 4), 0)
     fill(v("ctw", 1536 + 3, 9 * 512, 4), 0)
     fill(v("ot", 3, 8 * GW, 4), 0)
+    fill(v("bi", HW, GW), 0)
     for name, c in (("kw", 1024), ("pw", 99)):
         fill(v(name, 0, PAD), c)
         fill(v(name, PAD + HW, 272), c)
     for name, w in (("vm", C), ("er", C), ("mir", E)):
         fill(v(name, 0, 16), 0)
         fill(v(name, 16 + w, 32 + w), 0)
-    iota(v("ik"), [[1024, E]], 0, 0)
     for name in ("tb", "tbs"):
         fill(v(name, C, E), 0)
         fill(v(name, E + C + 32, 2 * E + 32), 0)
@@ -238,18 +237,18 @@ def rank_program(g, core, T, topo):
     act(pc(47), h_, ID, -1.0, 1.0)
     act(pc(48), h_, ID, 0.0, -1.0)
     for k in range(2):
-        act(v("pm", k, 48, 2), v("c16", 0, 24), ID, pc(45 + k), 0.0)
+        act(v("pm", k, 32, 2), v("c16", 0, 16), ID, pc(45 + k), 0.0)
         act(v("dm", k, 64, 2), v("c16"), ID, pc(47 + k), 0.0)
-    ts(v("pvl", 0, 3), v("c16", 0, 24, 8), pc(44), OP.add, C - 1.0, OP.min)
-    ts(v("pvl", 4, 5), v("c16", 0, 1), pc(44), OP.add, H - 1.0, OP.min)
+    ts(v("pvl", 0, 2), v("c16", 0, 16, 8), pc(44), OP.add, C - 129.0, OP.min)
+    ts(v("pvl", 2, 3), v("c16", 0, 1), pc(44), OP.add, H - 1.0, OP.min)
     act(pc(50), a_, ID, 0.0, 2.0)
     act(pc(54), rl_, ID, -8.0 * 63, 8.0)
     ts(pc(51), r_, pc(50), OP.is_le, 1.0 / 16, OP.mult)
     ts(pc(53), rh, a_, OP.is_equal, 1.0 / 8, OP.mult)
-    act(pc(52), pc(51), ID, 31.0, -496.0)
+    act(pc(52), pc(51), ID, 12.0, -192.0)
     act(pc(55), pc(53), ID, 63.0, pc(54))
     ts(v("dul"), v("c16", 0, 4), 0.5, OP.mult, rh, OP.add)
-    ts(v("ibl"), v("c16", 0, NB), pc(51), OP.mult, pc(52), OP.add)
+    ts(v("ibl"), v("c16", 0, 12), pc(51), OP.mult, pc(52), OP.add)
     ts(v("exl"), v("c16", 0, NB), pc(53), OP.mult, pc(55), OP.add)
     for p0, p1, sg_, c in ((0, 64, 1.0, 0.0), (64, 128, -1.0, 11.0)):
         act(pc(9, p0, p1), col("pf", 2, p0, p1), ID, c, 3.0 * sg_)
@@ -259,50 +258,40 @@ def rank_program(g, core, T, topo):
         act(v("hb", 0, HW, 1, p0, p1), v("irow", 0, HW, 1, p0, p1), ID, pc(56, p0, p1), sg_ / 32)
     act(v("pc", 4, 7), v("pc", 0, 3), AF.Abs)
     act(v("pc", 57, 60), v("pc", 4, 7), ID, 0.0, -1.0)
+    act(v("hb", HW, 2 * HW), v("hb", 0, HW), ID, pc(57))
     act(v("pc", 12, 15), v("pc", 0, 3), ID, 0.0, -1.0)
-    act(v("pc", 16, 19), v("pc", 0, 3), ID, 0.0, 1024.0)
     act(pc(23), r_, ID, float(PAD))
-    act(pc(25), r_, ID, -512.0, -1024.0)
-    act(pc(27), r_, ID, -8.0)
+    act(pc(25), r_, ID, -0.5, -1.0)
+    act(pc(24), rl_, ID, 0.0, 1024.0)
     act(pc(28), r_, ID, 0.0, 16.0)
-    act(pc(29), r_, ID, -128.0, 16.0)
     act(pc(49), g_, ID, 8.0)
     act(v("pc", 20, 23), v("pc", 0, 3), ID, pc(23))
     act(v("pc", 32, 35), v("pc", 4, 7), ID, pc(28))
-    act(v("pc", 36, 39), v("pc", 4, 7), ID, pc(29))
-    act(pc(30), r_, ID, 128.0)
-    act(v("pl"), v("c16", 0, 26), ID, pc(30))
     act(pc(31), par, ID, pc(28), E + 16.0)
     act(v("cnf"), v("c16", 0, 32, 16), ID, pc(31))
     ts(v("cnl", 0, 2), v("cnf"), 15.0, OP.add, 2 * E + 31.0, OP.min)
     ts(v("cnl", 2, 4), v("cnf"), 14.0, OP.add, 2 * E + 31.0, OP.min)
-    ts(v("m1", 0, 17), v("yrow", 0, 17), r_, OP.is_equal, P, OP.mult)
+    act(pc(30), r_, ID, P)
+    ts(v("m0"), v("yrow", 0, 16), r_, OP.is_equal)
+    ts(v("m1"), v("yrow", 0, 16), r_, OP.is_equal, pc(30), OP.mult)
     ts(v("m2", 0, 17), v("yrow", 0, 17), r_, OP.is_equal, -2 * P, OP.mult)
-    ts(v("rl"), v("c16", 0, 26), 0.0, OP.mult, r_, OP.add)
-    ts(pc(40), r_, 0.0, OP.is_equal, 2 * P, OP.mult)
-    tt(v("mw16"), v("m1", 0, 16), v("m2", 1, 17), OP.add)
-    act(pc(42), pc(40), ID, -P - 128.0 * 1024)
-    act(v("mw"), ind(v("mw16"), v("rl", 0, HE // 16)), AF.Copy)
-    act(v("co"), v("pl"), ID, pc(42), 1024.0)
-    for h in range(2):
-        for k in range(2):
-            ts(v("ctw", 512 * h + 256 * k, 512 * h + 256 * k + 256), v("m16", 0, 256), pc(49) if h else g_, OP.is_equal,
-               (1.0 - 2 * k) / 32, OP.mult)
-    qz(v("cwq", 0, 256), v("cws", 0, 256), v("ctw", 0, 1024))
+    tt(v("mw16"), v("m1"), v("m2", 1, 17), OP.add)
+    act(pc(42), col("m2", 0), ID, -P, -1.0)
+    for x in range(16):
+        act(v("mw", x, E, 16), v("c16", 0, NB), ID, col("mw16", x), col("m0", x))
+    for a, b, c in ((0, 64, 1.0), (64, 136, -1.0)):
+        ts(v("ctw", 4 * a, 4 * b), v("m16", 0, 4 * (b - a)), pc(49), OP.is_equal, c / 32, OP.mult)
+    qz(v("cwq", 0, 136), v("cws", 0, 136), v("ctw", 0, 544))
     for s in range(3):
         ts(v("ctw", 1024 + s, 1536, 4), v("yrow"), r_, OP.is_equal, pc(8), OP.mult)
         ts(v("shl", 16 * s, 16 * s + 16), v("c16", 0, 16), pc(20 + s), OP.add)
-        for h in range(2):
-            ts(v("ctw", 1536 + 512 * h + s, 2048 + 512 * h, 4), v("mhi"), pc(27) if h else r_, OP.is_equal, pc(16 + s), OP.mult)
-            ts(v("ctw", 2560 + 512 * h + s, 3072 + 512 * h, 4), v("mrow"), pc(32 + 4 * h + s), OP.is_equal, 2.0, OP.mult)
-            act(v("ctw", 3584 + 512 * h + s, 4096 + 512 * h, 4), v("ctw", 1536 + 512 * h + s, 2048 + 512 * h, 4), AF.Abs)
+        ts(v("ctw", 1536 + s, 2560, 4), v("mhi"), r_, OP.is_equal, pc(s), OP.mult)
+        ts(v("ctw", 2560 + s, 3584, 4), v("mrow"), pc(32 + s), OP.is_equal, 2.0, OP.mult)
+        act(v("ctw", 3584 + s, 4608, 4), v("ctw", 1536 + s, 2560, 4), AF.Sign)
     for a, b in ((2, 3), (3, 5), (5, 7), (7, 9)):
         qz(v("cwq", 128 * a, 128 * b), v("cws", 128 * a, 128 * b), v("ctw", 512 * a, 512 * b))
     for b in range(4):
         qz(v("eq", 128 * b, 128 * b + 128), v("es", 128 * b, 128 * b + 128), v("et", 3 - b, 515 - b))
-
-    def back(name, a, b):
-        return (T[name][:, b - 1:a - 1:-1] if a else T[name][:, b - 1::-1], v(name, a, b)[1])
 
     def slot(k, a, b):
         base = (k // 4) * 4 * E + k % 4
@@ -311,8 +300,8 @@ def rank_program(g, core, T, topo):
     def tri(name, c):
         return v(name, 8 * c * (c - 1), 8 * c * (c + 1))
 
-    def shifts(s):
-        return v("shl", 16 * s, 16 * s + 15)
+    def shifts(s, a=0, b=GW):
+        return v("shl", 16 * s + a // 16, 16 * s + b // 16)
 
     def plane(b):
         return v("gp", b * E, b * E + E)
@@ -320,32 +309,39 @@ def rank_program(g, core, T, topo):
     def bank(b):
         return "b%d" % ((5 + b) % 8)
 
+    def const(bk_, tile, o, w):
+        mm(bk_, "cwq", "cws", 128 * tile, "cq", "cs", o, w)
+
     for t in range(R):
         first, last = t == 0, t == R - 1
         win, wis, xt = "win%d" % t, "wis%d" % t, "xin" if first else "xst"
         halo = [("h%d" % t, n_halo)]
-        qz(v(win, 0, CH), v(wis, 0, CH), v(xt, 0, 4 * CH))
-        send(prev, win, wis, C, win, wis, H, "h%d" % t)
-        qz(v(win, CH, C), v(wis, CH, C), v(xt, 4 * CH, 4 * C))
 
-        mm("b0", "ur", "urs", 0, win, wis, 0, CH)
-        mm("b2", "ur", "urs", 0, win, wis, CH, C - CH)
-        mm("b1", "ur", "urs", 0, win, wis, E - 128, 128, ext=halo)
-        act(v("sb", 0, CH), v("b0", 0, CH), AF.Copy)
-        cp(v("sb", CH, C), v("b2", 0, C - CH))
-        act(v("sb", C, E), v("b1", 128 - H, 128), AF.Copy)
-        for l0, l1, o, c0, c1 in ((0, 3, 0, 0, OWN), (4, 5, 48, OWN, NB)):
-            w, k = 16 * (l1 - l0), 2 * (c1 - c0)
-            tt(v("pt", o, o + w), ind(v("sb", 16 * c0, 16 * c1), v("pvl", l0, l1)), v("pm", 0, w), OP.add)
-            tt(v("pv", c0, c1), v("pt", o, o + k, 2), v("pt", o + 1, o + k, 2), OP.max)
-            tt(slot(NB - 1, 16 * c0, 16 * c1), ind(v("pv", 0 if c0 else 0, 32), v("ibl", c0, c1)), v("sb", 16 * c0, 16 * c1), OP.is_gt)
+        for k, (a, b) in enumerate(PIECES):
+            w, bk_ = b - a, "b%d" % k
+            if b <= C:
+                qz(v(win, a, b), v(wis, a, b), v(xt, 4 * a, 4 * b))
+                mm(bk_, "ur", "urs", 0, win, wis, a, w)
+            else:
+                mm(bk_, "ur", "urs", 0, win, wis, b - 128, 128, ext=halo)
+            src = v(bk_, max(0, 128 - w), max(128, w))
+            if k == 0:
+                send(prev, win, wis, C, win, wis, H, "h%d" % t)
+                cp(v("sb", a, b), src)
+            else:
+                act(v("sb", a, b), src, AF.Copy)
+            l0, wide = (0, -(-w // 128)) if b <= C else (2, 1)
+            tt(v("pt", 32 * k, 32 * k + 16 * wide), ind(v("sb", a, b), v("pvl", l0, l0 + wide)), v("pm", 0, 16 * wide), OP.add)
+            tt(v("pv", 16 * k, 16 * k + w // 16), v("pt", 32 * k, 32 * k + w // 8, 2), v("pt", 32 * k + 1, 32 * k + w // 8, 2), OP.max)
+            tt(slot(NB - 1, a, b), ind(v("pv", 16 * k, 16 * k + 16), v("ibl", 0, w // 16)), v("sb", a, b), OP.is_gt)
         for b in range(4):
             mm(bank(b), "eq", "es", 128 * b, win, wis, 0, E, ext=halo)
             act(v("fp", b * E, b * E + E), v(bank(b), 0, E), AF.Copy)
 
         nv = ON_VECTOR[t]
         for c in range(1, NB):
-            x, below, pivot = slot(c - 1, 0, 16 * c), v("sb", 0, 16 * c), col("pv", c)
+            k = max(k for k, (a, b) in enumerate(PIECES) if a <= 16 * c)
+            x, below, pivot = slot(c - 1, 0, 16 * c), v("sb", 0, 16 * c), col("pv", 16 * k + c - PIECES[k][0] // 16)
             if c <= nv or c in SHARED[t]:
                 ts(x, below, pivot, OP.is_lt)
             if c <= nv:
@@ -355,7 +351,7 @@ def rank_program(g, core, T, topo):
             else:
                 act(tri("sg", c), below, AF.Sign, pivot, -1.0)
                 act(x, tri("sg", c), AF.Relu, 0.0, 1.0, col("rs", c))
-        scan(v("seg"), v("keep", 0, E), slot(NB - 1, 0, E), 0.0, OP.mult, OP.add)
+        scan(v("seg"), v("keep"), slot(NB - 1, 0, E), 0.0, OP.mult, OP.add)
         tt(v("y0", 0, nv + 1), v("sn", SN - 1, SN * (nv + 1), SN), v("seg", 15, 16 * nv + 16, 16), OP.add)
         tt(v("y0", nv + 1, NB), v("rs", nv + 1, NB), v("seg", 16 * nv + 31, E, 16), OP.add)
         tt(v("y1"), ind(v("y0"), v("dul")), v("dm"), OP.mult)
@@ -370,49 +366,55 @@ def rank_program(g, core, T, topo):
             for a, b, hs in ((0, HW, (0,)), (HW, E, (1,))) if u == 6 else ((0, w, (0, 1) if TW[u] > HO else (0,)),):
                 qz(v("cq", u * E + a, u * E + b), v("cs", u * E + a, u * E + b), v("ct", 4 * (u * E + a), 4 * (u * E + b)))
                 for h in hs:
-                    mm("b4", "cwq", "cws", 128 * h, "cq", "cs", u * E + HO * h, max(128, min(HW, TW[u] - HO * h)),
+                    mm("b4", "cwq", "cws", 8 - 8 * h, "cq", "cs", u * E + HO * h, max(128, min(HW, TW[u] - HO * h)),
                        (u, h) == (3, 0), (u, h) == (6, 1), (), ("st", t))
 
-        tt(v("kw", PAD, PAD + HW), v("b4", 0, HW), v("hb"), OP.add)
-        ts(v("bi", 0, GW), v("kw", PAD, PAD + GW), pc(4), OP.subtract)
+        o1, o2 = NT * E, NT * E + GW
+        tt(v("kw", PAD, PAD + HW), v("b4", 0, HW), v("hb", 0, HW), OP.add)
+        tt(v("bi", 0, HW), v("b4", 0, HW), v("hb", HW, 2 * HW), OP.add)
         for s in (1, 2):
             act(v("bi", s * GW, s * GW + GW), v("kw", PAD, PAD + GW), ID, pc(57 + s))
         for s in range(3):
             tt(v("ot", s, 4 * GW, 4), ind(v("kw"), shifts(s)), v("bi", s * GW, s * GW + GW), OP.is_lt)
-        qz(v("oq", 0, GW), v("osx", 0, GW), v("ot", 0, 4 * GW))
-        mm("b4", "cwq", "cws", 256, "oq", "osx", 0, HW)
+        qz(v("cq", o1, o2), v("cs", o1, o2), v("ot", 0, 4 * GW))
+        const("b4", 2, o1, HW)
+        const("b2", 8, o1 - HO, E)
+        const("b2", 7, o1, HE)
+        const("b1", 8, o2 - 128, 128)
+        edge = v("b1", EDGE - HO - GW + 128, EDGE - HO - GW + 160)
         cp(v("pw", PAD, PAD + HW), v("b4", 0, HW))
-        act(v("ab"), ind(v("pw"), shifts(2)), AF.Abs, pc(2))
+        act(v("ab", 0, AW), ind(v("pw"), shifts(2, 0, AW)), AF.Abs, pc(2))
+        act(v("ot", 4 * GW + 2, 4 * (GW + AW), 4), v("ab", 0, AW), AF.Relu, 1.0, -1.0)
+        ts(v("ot", 4 * (GW + AW) + 2, 8 * GW, 4), ind(v("pw"), shifts(2, AW)), pc(14), OP.is_equal)
         for s in range(2):
             ts(v("ot", 4 * GW + s, 8 * GW, 4), ind(v("pw"), shifts(s)), pc(12 + s), OP.is_equal)
-        act(v("ot", 4 * GW + 2, 8 * GW, 4), v("ab"), AF.Relu, 1.0, -1.0)
-        qz(v("oq", GW, 2 * GW), v("osx", GW, 2 * GW), v("ot", 4 * GW, 8 * GW))
-        mm("b1", "cwq", "cws", 384, "oq", "osx", GW, HE)
-        mm("b4", "cwq", "cws", 512, "oq", "osx", GW + HE - HO, HE)
-        mm("b2", "cwq", "cws", 512, "oq", "osx", GW - HO, E)
-        mm("b2", "cwq", "cws", 384, "oq", "osx", GW, HE)
-        for bk_, w0 in (("b0", 896), ("b3", 640)):
-            mm(bk_, "cwq", "cws", w0 + 128, "oq", "osx", GW - HO, C)
-            mm(bk_, "cwq", "cws", w0, "oq", "osx", GW, HE)
-
-        for k, bk_ in enumerate(("b1", "b4")):
-            scan(v("sc", k * HE, k * HE + HE), v(bk_, 0, HE), v("mw", 0, HE), -2 * P, OP.max, OP.add)
-        tt(v("t26"), v("sc", 15, E, 16), v("co"), OP.add)
-        ts(v("ow"), v("t26"), 1.0 / 1024, OP.mult)
-        act(v("ad2"), v("b0", 0, C), AF.Sign, pc(25), 1.0, v("acc"))
-        act(v("dl"), v("b2", 0, E), ID, 0.0, rl_)
+        qz(v("cq", o2, o2 + GW), v("cs", o2, o2 + GW), v("ot", 4 * GW, 8 * GW))
+        const("b3", 5, o2, HE)
+        const("b7", 6, o2 + HE - HO, 128)
+        tt(v("eg", 0, 32), edge, v("eg", 64, 96), OP.is_lt)
+        tt(v("eg", 32, 64), edge, v("eg", 0, 32), OP.mult)
+        act(v("ad", 0, EDGE), v("b2", 0, EDGE), AF.Abs)
+        act(v("ad", EDGE, EDGE + 32), v("eg", 32, 64), AF.Abs)
+        act(v("ad2"), v("ad"), AF.Sign, pc(25), 1.0, v("acc"))
+        act(v("dl"), v("b2", 0, E), ID, 0.0, pc(24))
         scan(v("xs"), v("irc"), v("dl"), -float(HE), OP.max, OP.add)
         scan(back("mir", 16, 16 + E), v("ones", 0, E), back("xs", 0, E), 500.0, OP.add, OP.min)
+        const("b1", 3, o2, HE)
+        const("b4", 4, o2 + HE - HO, HE)
+        for k, bk_ in enumerate(("b1", "b4")):
+            scan(v("sc", k * HE, k * HE + HE), v(bk_, 0, HE), v("mw", k * HE, k * HE + HE), -2 * P, OP.max, OP.add)
+        ts(v("ow"), v("sc", 15, E, 16), pc(42), OP.add)
         for b in range(4):
             act(plane(b), ind(v("fp", b * E, b * E + E), v("ow")), AF.Copy, 0.0, -0.5)
 
-        scan(v("val"), v("b3", 0, C), v("ones", 0, C), v("acc"), OP.add, OP.mult)
-        tt(v("vm", 16, 16 + C), v("b3", 0, C), v("val"), OP.mult)
+        for bk_, a, b in (("b3", 0, HE), ("b7", HE, C)):
+            scan(v("val", a, b), v(bk_, 0, b - a), v("ones", 0, b - a), col("val", a - 1) if a else v("acc"), OP.add, OP.mult)
+            tt(v("vm", 16 + a, 16 + b), v(bk_, 0, b - a), v("val", a, b), OP.mult)
         tr(v("tb", 0, C), v("vm", 16, 16 + C))
         tr(v("tb", E, E + C + 32), v("vm"))
         scan(v("tbs", 0, C), v("keep", 0, C), v("tb", 0, C), 0.0, OP.mult, OP.add)
         scan(v("tbs", E, E + C + 32), v("keep", 0, C + 32), v("tb", E, E + C + 32), 0.0, OP.mult, OP.add)
-        ts(v("rkw"), ind(v("tbs"), v("cnl", 0, 2)), 0.25, OP.mult, 159.0, OP.add)
+        ts(v("rkw"), ind(v("tbs"), v("cnl", 0, 2)), 0.25, OP.mult, (EDGE + 32) / 2 - 1.0, OP.add)
         cp(ind(v("er", 16, 16 + C), v("rkw", 0, 20)), v("mir", 16, 16 + C))
         ops[-1]["wr"], ops[-1]["rd"] = v("er", 16, 16 + C)[1], v("rkw", 0, 20)[1] + v("mir", 16, 16 + C)[1]
         for k0, k1, o0, wide in ((0, K, 0, 1), (K, C, 16, 2)):
@@ -422,11 +424,14 @@ def rank_program(g, core, T, topo):
             ts(v("mew", o0, o0 + 16 * wide), ind(v("tb"), v("cnl", 0, wide)), float(HE), OP.add)
             e_, m_ = [v(name, o0 + k0 // 16, o0 + k1 // 16) for name in ("ew", "mew")]
             for b in range(4):
-                gb = v("ge", b * C + k0, b * C + k1)
+                gb, wb = v("ge", b * C + k0, b * C + k1), v("zw", b * C + k0, b * C + k1)
                 zb = v("z", b * C + k0, b * C + k1) if k0 else v("at", b, 4 * K, 4)
                 act(gb, ind(plane(b), e_), AF.Copy, 0.0, -2.0)
                 tt(zb, ind(plane(b), m_), gb, OP.add)
-                act(v("zw", b * C + k0, b * C + k1), zb, AF.Copy, 0.0, 32.0)
+                if k0:
+                    act(wb, zb, AF.Copy, 0.0, 32.0)
+                else:
+                    ts(wb, zb, 32.0, OP.mult)
             if k0 == 0:
                 qz(v("aq%d" % t), v("as%d" % t), v("at"))
                 send(far, "al%d" % t, "als%d" % t, 0, "aq%d" % t, "as%d" % t, K, "f%d" % t)
@@ -434,27 +439,31 @@ def rank_program(g, core, T, topo):
             tr(v("tm", 0, E), v("mir", 16, 16 + E))
             tr(v("tm", E, 2 * E + 32), v("mir"))
             ts(v("mrw"), ind(v("tm"), v("cnl", 0, 2)), float(HE), OP.add)
-            tt(v("dsb"), v("b2", 0, E), v("ik"), OP.add)
-            act(v("mr"), ind(v("dsb"), v("mrw", 0, NB)), AF.Copy, 0.0, 1.0 / 1024)
+            act(v("orow"), ind(v("irc"), v("ow")), AF.Copy)
+            act(v("mr"), ind(v("orow"), v("mrw", 0, NB)), ID, float(HE))
             dma("s", T.lm[:], (T.mr[0:128:16, :], v("mr")[1]), "ol")
 
         for b in range(4):
             mm(bank(b), "wq", "wp", 128 * b, "al%d" % t, "als%d" % t, 0, K, ext=[("f%d" % t, n_far)])
             tt(v("zw", b * C, b * C + K), v(bank(b), 0, K), v("zw", b * C, b * C + K), OP.add)
-        for b, lo, hi, on_scalar in ((0, 0, C, 1), (1, 0, C, 1), (2, XS, C, 0), (3, 0, C, 0), (2, 0, XS, 1)):
+        for b, lo, hi, on_scalar in GATHERS:
             src = ind(v("zw", b * C, b * C + C), v("rkw", lo // 16, hi // 16))
             if on_scalar:
                 act(v("xst", 4 * lo + b, 4 * hi, 4), src, AF.Copy, 0.0, 1.0 / 32)
             else:
                 ts(v("xst", 4 * lo + b, 4 * hi, 4), src, 1.0 / 32, OP.mult)
 
-    qz(v("fq"), v("fs"), v("xst"))
-    mm("b1", "vq", "vs", 0, "fq", "fs", 0, C)
-    act(v("ysb"), v("b1", 0, C), AF.Copy)
+    for k, (a, b) in enumerate(PIECES[:2]):
+        qz(v("fq", a, b), v("fs", a, b), v("xst", 4 * a, 4 * b))
+        mm("b%d" % (1 + k), "vq", "vs", 0, "fq", "fs", a, b - a)
+        if k:
+            cp(v("ysb", a, b), v("b2", 0, b - a))
+        else:
+            act(v("ysb", a, b), v("b1", 0, b - a), AF.Copy)
+        dma("s" if k else "a", T.y[:, a:b], v("ysb", a, b), "oy")
     dma("s", T.oc[:], bytes_of(v("fq")), "ocs")
     for k in range(4):
         dma("s", T.osc[4 * k:4 * k + 4, :], v("fs", 0, C, 1, 32 * k, 32 * k + 4), "ocs")
-    dma("a", T.y[:], v("ysb"), "oy")
 
     emit(g, T, arrange(ops), sent[0])
 
@@ -515,7 +524,7 @@ def depends(ops):
 
 
 def arrange(ops):
-    deps = [{j: HOP + (LOAD if ops[j]["dma"] else 0.0) for j in d} for d in depends(ops)]
+    deps = [{j: HOP + (LOAD if ops[j]["dma"] else 60.0 if ops[j]["q"] == "t" else 0.0) for j in d} for d in depends(ops)]
     groups, sends = {}, {}
     for i, o in enumerate(ops):
         if o["acc"] is not None:

@@ -1,25 +1,29 @@
+import numpy as np
 from concourse.mybir import dt, AluOpType as OP, ActivationFunctionType as AF
 
 C, H, E, K, J, R = 320, 96, 416, 128, 2, 2
 HW, GW, HO, PAD = 232, 240, 184, 16
 HE = E // 2
-NB = E // 16
+NB, OWN = E // 16, C // 16
 PIECES = ((0, 128), (128, C), (C, E))
 EDGE = C - 16
 BIG = 2.0 ** 96
 P = 1024.0
 DIG = 6144.0
-ON_VECTOR = (14, 16)
-SHARED = ((25, 24, 23, 22), (25, 24))
-SN = 256
+ON_VECTOR, TOP = (14, 14), 24
+SN = 416
 AW = 160
 GATHERS = [(b, 0, 128, b < 1) for b in range(4)] + [(b, 128, C, b < 3) for b in range(4)]
 NT = 7
+TB = [128, 0] + [u * E for u in range(2, NT)]
 TW = [128, 128, 192, 256, 320, 384, E]
 TP = [128, 128, HO + 128, HO + 128, 320, 384, E]
-CYCLE, HOP, LOAD = 0.9, 170.0, 2000.0
-TRAVEL, FIRST = 1500.0, 2000.0
-PASSES = 2
+O1, O2 = NT * E, NT * E + 256
+CYCLE, HOP, LOAD, TRAVEL, FIRST = 0.85, 160.0, 1300.0, 1000.0, 3600.0
+LOADS = (1100.0, 1550.0, 2100.0)
+PASSES, TRIES, NOISE, SLOW = 2, 8, 300.0, 1.4
+PLANS = [(150.0, 1.0), (170.0, 1.0), (200.0, 1.0), (240.0, 1.0), (170.0, 1.2)]
+ORDER = []
 
 F32, BF, I32, U16, Q4, U8 = "float32", "bfloat16", "int32", "uint16", "float8_e4m3fn_x4", "uint8"
 
@@ -36,25 +40,25 @@ SCRATCH = {
     "fq": _sb(C, Q4), "fs": _sb(C, U8),
     "aq0": _sb(K, Q4), "as0": _sb(K, U8), "aq1": _sb(K, Q4), "as1": _sb(K, U8),
     "al0": _sb(K, Q4), "als0": _sb(K, U8), "al1": _sb(K, Q4), "als1": _sb(K, U8),
-    "pi": _sb(8, I32), "pf": _sb(8, F32), "pc": _sb(64, F32), "ul": _sb(8, U16),
+    "pi": _sb(9, I32), "pf": _sb(9, F32), "pc": _sb(64, F32), "ul": _sb(8, U16), "mk": _sb(256, BF),
     "yrow": _sb(128, BF), "m16": _sb(320, BF), "mrow": _sb(256, BF), "mhi": _sb(256, BF), "c16": _sb(32, F32),
     "irow": _sb(HW, F32), "irc": _sb(E, BF), "ones": _sb(516, BF), "hb": _sb(2 * HW, F32),
-    "pvl": _sb(4, U16), "pm": _sb(32, F32), "ibl": _sb(12, U16), "exl": _sb(NB, U16), "dul": _sb(4, U16), "dm": _sb(64, F32),
+    "pvl": _sb(4, U16), "pm": _sb(32, F32), "ibl": _sb(12, U16), "dul": _sb(6, U16), "exl": _sb(NB, U16), "dm": _sb(64, F32),
     "m0": _sb(16, F32), "m1": _sb(16, F32), "m2": _sb(32, F32), "mw16": _sb(16, F32), "mw": _sb(E, F32),
-    "shl": _sb(48, U16), "cnf": _sb(2, F32), "cnl": _sb(4, U16),
+    "shl": _sb(48, U16), "cnf": _sb(4, F32), "cnl": _sb(4, U16),
     "keep": _sb(E, BF), "ctw": _sb(9 * 512, BF), "cwq": _sb(9 * 128, Q4), "cws": _sb(9 * 128, U8),
     "et": _sb(516, BF), "eq": _sb(512, Q4), "es": _sb(512, U8),
-    "sb": _sb(E, F32), "pt": _sb(96, F32), "pv": _sb(48, F32), "sg": _sb(8 * NB * NB, BF), "jk": _sb(8 * NB * NB, BF),
-    "rs": _sb(32, F32), "sn": _sb(SN * 17, BF), "seg": _sb(E, BF),
+    "sb": _sb(E, F32), "pt": _sb(96, F32), "pv": _sb(48, F32), "sg": _sb(8 * NB * NB, BF),
+    "rs": _sb(32, F32), "sn": _sb(SN * NB, BF), "seg": _sb(E, BF),
     "y0": _sb(32, F32), "y1": _sb(64, F32), "hi": _sb(64, BF), "lo": _sb(64, F32),
-    "ct": _sb(NT * 4 * E, BF), "cq": _sb(NT * E + 2 * GW, Q4), "cs": _sb(NT * E + 2 * GW, U8),
+    "ct": _sb(NT * 4 * E, BF), "cq": _sb(O2 + 256, Q4), "cs": _sb(O2 + 256, U8),
     "kw": _sb(272, BF), "bi": _sb(3 * GW, BF), "pw": _sb(272, BF), "ab": _sb(GW, BF),
-    "ot": _sb(8 * GW, BF), "eg": _sb(96, F32),
+    "ot": _sb(1024 + 4 * GW, BF), "eg": _sb(96, F32),
     "sc": _sb(E, F32), "ow": _sb(NB, U16), "dl": _sb(E, BF),
     "xs": _sb(E, BF), "mir": _sb(E + 32, BF), "tm": _sb(2 * E + 32, BF), "mrw": _sb(32, U16),
     "ad": _sb(EDGE + 32, BF), "ad2": _sb(EDGE + 32, BF), "acc": _sb(1, F32), "val": _sb(C, BF), "vm": _sb(C + 32, BF),
-    "tb": _sb(2 * E + 32, BF), "tbs": _sb(2 * E + 32, BF), "rkw": _sb(32, U16), "er": _sb(C + 32, BF),
-    "ew": _sb(48, U16), "mew": _sb(48, U16),
+    "tb": _sb(2 * E + 32, BF), "tc": _sb(2 * E + 32, BF), "tbs": _sb(2 * E + 32, BF),
+    "rkw": _sb(32, U16), "er": _sb(C + 32, BF), "ew": _sb(64, U16),
     "fp": _sb(4 * E, BF), "gp": _sb(4 * E, BF), "ge": _sb(4 * C, BF),
     "at": _sb(4 * K, BF), "z": _sb(4 * C, BF), "zw": _sb(4 * C, BF),
     "orow": _sb(E, BF), "mr": _sb(E, F32), "ysb": _sb(C, F32),
@@ -62,8 +66,8 @@ SCRATCH = {
 for _b in range(8):
     SCRATCH["b%d" % _b] = ("psum", [128, 512], F32)
 
-SEMAPHORES = ["qv", "qa", "qt", "qg", "h0", "h1", "f0", "f1", "sent",
-              "dx", "dy", "du", "dv", "dw", "ds", "oy", "ol", "ocs"]
+SEMAPHORES = ["qv", "qa", "qt", "qg", "h0", "h1", "f0", "f1", "sent", "dx", "dy", "du", "dv", "dw", "ds",
+              "z20", "z21", "z22", "z30", "z31", "oy", "ol", "ocs"]
 
 
 def rank_program(g, core, T, topo):
@@ -150,10 +154,11 @@ def rank_program(g, core, T, topo):
         src = v("ones", 0, out[1][0][4])
         add("g", lambda: g.affine_select(out[0], src[0], pat, op, 0.0, base, cm), [out], [src])
 
-    def dma(q, out, a, sem):
+    def dma(q, out, a, sem, load=LOAD):
         eng = g.sync if q == "s" else g.scalar
         outs = [out] if isinstance(out, tuple) else []
         add(q, lambda: eng.dma_start(ap(out), ap(a)), outs, [a], (), sem)
+        ops[-1]["load"] = load
 
     def bytes_of(x):
         return (x[0].bitcast(dt.uint8), x[1])
@@ -173,15 +178,12 @@ def rank_program(g, core, T, topo):
     n_halo = 2 * len(topo.engines(T.cores[(rank + 1) % n], core))
     n_far = 2 * len(topo.engines(T.cores[(rank - J) % n], core))
 
-    dma("s", v("xin", 0, 512), T.x[:, 0:512], "dx")
-    dma("a", v("uin"), T.u[:], "du")
-    dma("s", v("xin", 512, 4 * C), T.x[:, 512:4 * C], "dy")
-    for out, src, sem in ((bytes_of(v("wq")), T.wc[:], "dw"), (v("wp"), T.ws[:], "ds"), (v("vin"), T.v[:], "dv")):
-        dma("s", out, src, sem)
-        ops[-1]["rd"] = v("xin")[1]
+    dma("s", v("xin", 0, 512), T.x[:, 0:512], "dx", LOADS[0])
+    dma("s", v("uin"), T.u[:], "du", LOADS[1])
+    dma("s", v("xin", 512, 4 * C), T.x[:, 512:4 * C], "dy", LOADS[2])
 
     ID = AF.Identity
-    r_, a_, par, g_, h_, rh, rl_ = [col("pf", k) for k in range(1, 8)]
+    r_, a_, _, g_, h_, rh, rl_, par = [col("pf", k) for k in range(1, 9)]
 
     def pc(k, p0=0, p1=128):
         return col("pc", k, p0, p1)
@@ -195,16 +197,28 @@ def rank_program(g, core, T, topo):
     iota(v("mhi"), [[1, 16], [0, 16]], 0, 0)
     iota(v("mrow"), [[1, 256]], 0, 0)
     iota(v("eg", 64, 96), [[-1, 32]], C - EDGE, 0)
-    for name, c in (("rs", 0.0), ("y0", 0.0), ("pv", -BIG), ("ones", 1.0)):
+    for name, c in (("y0", 0.0), ("pv", -BIG), ("ones", 1.0)):
         ms(v(name), c)
     ms(col("sn", SN - 1), 0.0)
     for u in range(NT):
-        (ms if u < 4 else fill)(v("ct", 4 * (u * E + 16 * (4 * u + 1)), 4 * (u * E + TP[u])), 0)
+        a0, w = 4 * (TB[u] + 16 * (4 * u + 1)), 4 * (TP[u] - 16 * (4 * u + 1))
+        if u < 2:
+            act(v("ct", a0, a0 + w), v("ones", 0, w), AF.Copy, 0.0, 0.0)
+        elif u < 4:
+            for a in range(0, w, 256):
+                k = min(w - a, 256)
+                dma("s", v("ct", a0 + a, a0 + a + k), v("ct", 4 * TB[0] + 256, 4 * TB[0] + 256 + k), "z%d%d" % (u, a // 256))
+        else:
+            fill(v("ct", a0, a0 + w), 0)
+    for out, src, sem in ((bytes_of(v("wq")), T.wc[:], "dw"), (v("wp"), T.ws[:], "ds"), (v("vin"), T.v[:], "dv")):
+        dma("s", out, src, sem)
+        ops[-1]["rd"] = v("xin")[1]
     select(v("et"), [[1, 516]], OP.is_equal, -3, -4)
     select(v("keep"), [[0, NB], [1, 16]], OP.not_equal, 0, 0)
     fill(v("ctw", 1024 + 3, 1536, 4), 0)
     fill(v("ctw", 1536 + 3, 9 * 512, 4), 0)
-    fill(v("ot", 3, 8 * GW, 4), 0)
+    fill(v("ot", 3, 1024 + 4 * GW, 4), 0)
+    fill(v("ot", 4 * GW, 1024), 0)
     fill(v("bi", HW, GW), 0)
     for name, c in (("kw", 1024), ("pw", 99)):
         fill(v(name, 0, PAD), c)
@@ -212,7 +226,7 @@ def rank_program(g, core, T, topo):
     for name, w in (("vm", C), ("er", C), ("mir", E)):
         fill(v(name, 0, 16), 0)
         fill(v(name, 16 + w, 32 + w), 0)
-    for name in ("tb", "tbs"):
+    for name in ("tb", "tbs", "tc"):
         fill(v(name, C, E), 0)
         fill(v(name, E + C + 32, 2 * E + 32), 0)
     p_ = col("pi", 0)
@@ -223,41 +237,46 @@ def rank_program(g, core, T, topo):
     ts(col("pi", 6), p_, 1, OP.arith_shift_right, 7, OP.bitwise_and)
     ts(col("pi", 7), p_, 1, OP.bitwise_and)
     tt(col("pi", 3), p_, col("pi", 2), OP.add)
-    ts(col("pi", 3), col("pi", 3), 1, OP.bitwise_and)
-    cp(v("pf"), v("pi"))
-    ts(v("ul"), v("rs", 0, 8), g_, OP.add, 16.0, OP.mult)
+    cp(v("pf", 1, 7), v("pi", 1, 7))
+    ts(col("pi", 8), col("pi", 3), 1, OP.bitwise_and)
+    cp(v("pf", 7, 9), v("pi", 7, 9))
+    ts(v("ul"), v("ones", 0, 8), g_, OP.mult, 16.0, OP.mult)
     qz(v("uq"), v("us"), v("uin"))
     cp((v("ur")[0].bitcast(dt.uint32), v("ur")[1]), ind(v("uq"), v("ul"), True))
     act(v("urs"), ind(v("us"), v("ul")), AF.Copy)
     qz(v("vq"), v("vs"), v("vin"))
-    act(pc(45), h_, ID, 0.0, -BIG)
-    act(pc(46), h_, ID, -BIG, BIG)
     act(pc(43), a_, ID, rl_, 2.0)
     act(pc(44), rh, ID, pc(43), 16.0)
-    act(pc(47), h_, ID, -1.0, 1.0)
-    act(pc(48), h_, ID, 0.0, -1.0)
-    for k in range(2):
-        act(v("pm", k, 32, 2), v("c16", 0, 16), ID, pc(45 + k), 0.0)
-        act(v("dm", k, 64, 2), v("c16"), ID, pc(47 + k), 0.0)
+    iota(v("y1"), [[0, 32], [1, 2]], 0, 0)
+    ts(v("dm"), v("y1"), h_, OP.is_equal, -1.0, OP.mult)
+    act(v("pm"), v("dm", 0, 32), ID, -BIG, -BIG)
     ts(v("pvl", 0, 2), v("c16", 0, 16, 8), pc(44), OP.add, C - 129.0, OP.min)
     ts(v("pvl", 2, 3), v("c16", 0, 1), pc(44), OP.add, H - 1.0, OP.min)
     act(pc(50), a_, ID, 0.0, 2.0)
-    act(pc(54), rl_, ID, -8.0 * 63, 8.0)
     ts(pc(51), r_, pc(50), OP.is_le, 1.0 / 16, OP.mult)
     ts(pc(53), rh, a_, OP.is_equal, 1.0 / 8, OP.mult)
     act(pc(52), pc(51), ID, 12.0, -192.0)
-    act(pc(55), pc(53), ID, 63.0, pc(54))
-    ts(v("dul"), v("c16", 0, 4), 0.5, OP.mult, rh, OP.add)
     ts(v("ibl"), v("c16", 0, 12), pc(51), OP.mult, pc(52), OP.add)
-    ts(v("exl"), v("c16", 0, NB), pc(53), OP.mult, pc(55), OP.add)
+    act(pc(60), h_, ID, rh, 100.0)
+    ts(v("dul", 0, 2), v("c16", 0, 2), 0.5, OP.mult, rh, OP.add)
+    ts(v("dul", 2, 3), pc(60), 16.0, OP.add, 31.0, OP.min)
+    ts(v("dul", 4, 5), rh, float(OWN), OP.add)
+    for k, zero, a, b in ((61, 47.0, 0, OWN), (62, 15.0, OWN, NB)):
+        act(pc(k - 16), rl_, ID, -8.0 * zero, 8.0)
+        act(pc(k), pc(53), ID, zero, pc(k - 16))
+        ts(v("exl", a, b), v("c16", 0, b - a), pc(53), OP.mult, pc(k), OP.add)
     for p0, p1, sg_, c in ((0, 64, 1.0, 0.0), (64, 128, -1.0, 11.0)):
         act(pc(9, p0, p1), col("pf", 2, p0, p1), ID, c, 3.0 * sg_)
         act(v("pc", 0, 3, 1, p0, p1), v("c16", 0, 3, 1, p0, p1), ID, pc(9, p0, p1), sg_ / 16)
         act(pc(8, p0, p1), col("pf", 2, p0, p1), ID, sg_, 0.0)
         act(pc(56, p0, p1), col("pf", 5, p0, p1), ID, (192 - 15.5 / 32) * sg_, HO / 32 * sg_)
-        act(v("hb", 0, HW, 1, p0, p1), v("irow", 0, HW, 1, p0, p1), ID, pc(56, p0, p1), sg_ / 32)
     act(v("pc", 4, 7), v("pc", 0, 3), AF.Abs)
     act(v("pc", 57, 60), v("pc", 4, 7), ID, 0.0, -1.0)
+    act(pc(10), pc(8), ID, 0.0, 1.0 / 32)
+    act(pc(16), pc(8), ID, 0.0, -6.0)
+    act(pc(11), h_, ID, pc(56), pc(16))
+    act(v("hb", 0, 16 * TOP - HO), v("irow", 0, 16 * TOP - HO), ID, pc(56), pc(10))
+    act(v("hb", 16 * TOP - HO, HW), v("irow", 16 * TOP - HO, HW), ID, pc(11), pc(10))
     act(v("hb", HW, 2 * HW), v("hb", 0, HW), ID, pc(57))
     act(v("pc", 12, 15), v("pc", 0, 3), ID, 0.0, -1.0)
     act(pc(23), r_, ID, float(PAD))
@@ -268,9 +287,10 @@ def rank_program(g, core, T, topo):
     act(v("pc", 20, 23), v("pc", 0, 3), ID, pc(23))
     act(v("pc", 32, 35), v("pc", 4, 7), ID, pc(28))
     act(pc(31), par, ID, pc(28), E + 16.0)
-    act(v("cnf"), v("c16", 0, 32, 16), ID, pc(31))
-    ts(v("cnl", 0, 2), v("cnf"), 15.0, OP.add, 2 * E + 31.0, OP.min)
-    ts(v("cnl", 2, 4), v("cnf"), 14.0, OP.add, 2 * E + 31.0, OP.min)
+    act(v("cnf", 0, 2), v("c16", 0, 32, 16), ID, pc(31))
+    act(v("cnf", 2, 3), v("cnf", 0, 1), ID, -1.0)
+    act(v("cnf", 3, 4), v("cnf", 0, 1), ID, 0.0)
+    ts(v("cnl"), v("cnf"), 15.0, OP.add, 2 * E + 31.0, OP.min)
     act(pc(30), r_, ID, P)
     ts(v("m0"), v("yrow", 0, 16), r_, OP.is_equal)
     ts(v("m1"), v("yrow", 0, 16), r_, OP.is_equal, pc(30), OP.mult)
@@ -282,9 +302,12 @@ def rank_program(g, core, T, topo):
     for a, b, c in ((0, 64, 1.0), (64, 136, -1.0)):
         ts(v("ctw", 4 * a, 4 * b), v("m16", 0, 4 * (b - a)), pc(49), OP.is_equal, c / 32, OP.mult)
     qz(v("cwq", 0, 136), v("cws", 0, 136), v("ctw", 0, 544))
+    act(pc(26), r_, ID, 0.0, -1.0)
+    act(v("mk", 0, 128), v("yrow"), AF.Abs, pc(26))
+    act(v("mk", 128, 256), v("mk", 0, 128), AF.Relu, 1.0, -1.0)
     for s in range(3):
-        ts(v("ctw", 1024 + s, 1536, 4), v("yrow"), r_, OP.is_equal, pc(8), OP.mult)
         ts(v("shl", 16 * s, 16 * s + 16), v("c16", 0, 16), pc(20 + s), OP.add)
+        act(v("ctw", 1024 + s, 1536, 4), v("mk", 128, 256), ID, 0.0, pc(8))
         ts(v("ctw", 1536 + s, 2560, 4), v("mhi"), r_, OP.is_equal, pc(s), OP.mult)
         ts(v("ctw", 2560 + s, 3584, 4), v("mrow"), pc(32 + s), OP.is_equal, 2.0, OP.mult)
         act(v("ctw", 3584 + s, 4608, 4), v("ctw", 1536 + s, 2560, 4), AF.Sign)
@@ -294,7 +317,7 @@ def rank_program(g, core, T, topo):
         qz(v("eq", 128 * b, 128 * b + 128), v("es", 128 * b, 128 * b + 128), v("et", 3 - b, 515 - b))
 
     def slot(k, a, b):
-        base = (k // 4) * 4 * E + k % 4
+        base = 4 * TB[k // 4] + k % 4
         return v("ct", base + 4 * a, base + 4 * b, 4)
 
     def tri(name, c):
@@ -342,55 +365,63 @@ def rank_program(g, core, T, topo):
         for c in range(1, NB):
             k = max(k for k, (a, b) in enumerate(PIECES) if a <= 16 * c)
             x, below, pivot = slot(c - 1, 0, 16 * c), v("sb", 0, 16 * c), col("pv", 16 * k + c - PIECES[k][0] // 16)
-            if c <= nv or c in SHARED[t]:
+            if c <= nv or c >= TOP:
                 ts(x, below, pivot, OP.is_lt)
-            if c <= nv:
-                scan(v("sn", SN * (c + 1) - 16 * c, SN * (c + 1)), x, x, 0.0, OP.add, OP.max)
-            elif c in SHARED[t]:
-                act(tri("jk", c), x, ID, 0.0, 1.0, col("rs", c))
+                scan(v("sn", SN * (c + 1) - 16 * c, SN * (c + 1)), x, v("ones", 0, 16 * c), -192.0 * (c >= TOP), OP.add, OP.mult)
             else:
                 act(tri("sg", c), below, AF.Sign, pivot, -1.0)
                 act(x, tri("sg", c), AF.Relu, 0.0, 1.0, col("rs", c))
-        scan(v("seg"), v("keep"), slot(NB - 1, 0, E), 0.0, OP.mult, OP.add)
-        tt(v("y0", 0, nv + 1), v("sn", SN - 1, SN * (nv + 1), SN), v("seg", 15, 16 * nv + 16, 16), OP.add)
-        tt(v("y0", nv + 1, NB), v("rs", nv + 1, NB), v("seg", 16 * nv + 31, E, 16), OP.add)
-        tt(v("y1"), ind(v("y0"), v("dul")), v("dm"), OP.mult)
-        ts(v("hi"), v("y1"), DIG, OP.add)
-        tt(v("lo"), v("y1"), v("hi"), OP.subtract)
-        act(slot(NB, 0, 256), ind(v("hi"), v("exl", 0, 16)), ID, -DIG)
-        ts(slot(NB + 1, 0, 256), ind(v("lo"), v("exl", 0, 16)), DIG, OP.add)
-        act(slot(NB, 256, E), ind(v("hi"), v("exl", 16, NB)), ID, -DIG)
-        act(slot(NB + 1, 256, E), ind(v("lo"), v("exl", 16, NB)), ID, DIG)
+        for c0, c1, o, w in ((0, OWN, 0, 48), (OWN, NB, 48, 16)):
+            a0, a1 = 16 * c0, 16 * c1
+            scan(v("seg", a0, a1), v("keep", 0, a1 - a0), slot(NB - 1, a0, a1), 0.0, OP.mult, OP.add)
+            for a, b, run in ((0, nv + 1, True), (nv + 1, TOP, False), (TOP, NB, True)):
+                a, b = max(a, c0), min(b, c1)
+                if a < b:
+                    sums = v("sn", SN * (a + 1) - 1, SN * b, SN) if run else v("rs", a, b)
+                    tt(v("y0", a, b), sums, v("seg", 16 * a + 15, 16 * b, 16), OP.add)
+            y1, hi, lo = [v(name, o, o + w) for name in ("y1", "hi", "lo")]
+            tt(y1, ind(v("y0"), v("dul", c0 // 5, c0 // 5 + w // 16)), v("dm", 0, w), OP.mult)
+            ts(hi, y1, DIG, OP.add)
+            tt(lo, y1, hi, OP.subtract)
+            act(slot(NB, a0, a1), ind(hi, v("exl", c0, c1)), ID, -DIG)
+            if c0 == 0:
+                act(slot(NB + 1, a0, a1), ind(lo, v("exl", c0, c1)), ID, DIG)
+            else:
+                ts(slot(NB + 1, a0, a1), ind(lo, v("exl", c0, c1)), DIG, OP.add)
         for u in (3, 2, 1, 0, 4, 5, 6):
-            w = TP[u] if first else TW[u]
+            w = (TP if first else TW)[u] + ((128 if first else 64) if u == 1 else 0)
             for a, b, hs in ((0, HW, (0,)), (HW, E, (1,))) if u == 6 else ((0, w, (0, 1) if TW[u] > HO else (0,)),):
-                qz(v("cq", u * E + a, u * E + b), v("cs", u * E + a, u * E + b), v("ct", 4 * (u * E + a), 4 * (u * E + b)))
+                if u:
+                    qz(v("cq", TB[u] + a, TB[u] + b), v("cs", TB[u] + a, TB[u] + b), v("ct", 4 * (TB[u] + a), 4 * (TB[u] + b)))
                 for h in hs:
-                    mm("b4", "cwq", "cws", 8 - 8 * h, "cq", "cs", u * E + HO * h, max(128, min(HW, TW[u] - HO * h)),
+                    mm("b4", "cwq", "cws", 8 - 8 * h, "cq", "cs", TB[u] + HO * h, max(128, min(HW, TW[u] - HO * h)),
                        (u, h) == (3, 0), (u, h) == (6, 1), (), ("st", t))
 
-        o1, o2 = NT * E, NT * E + GW
         tt(v("kw", PAD, PAD + HW), v("b4", 0, HW), v("hb", 0, HW), OP.add)
         tt(v("bi", 0, HW), v("b4", 0, HW), v("hb", HW, 2 * HW), OP.add)
         for s in (1, 2):
             act(v("bi", s * GW, s * GW + GW), v("kw", PAD, PAD + GW), ID, pc(57 + s))
-        for s in range(3):
-            tt(v("ot", s, 4 * GW, 4), ind(v("kw"), shifts(s)), v("bi", s * GW, s * GW + GW), OP.is_lt)
-        qz(v("cq", o1, o2), v("cs", o1, o2), v("ot", 0, 4 * GW))
-        const("b4", 2, o1, HW)
-        const("b2", 8, o1 - HO, E)
-        const("b2", 7, o1, HE)
-        const("b1", 8, o2 - 128, 128)
+        for s, a, b in ((0, 0, GW), (1, 0, GW), (2, 0, 128), (2, 128, GW)):
+            tt(v("ot", 4 * a + s, 4 * b, 4), ind(v("kw"), shifts(s, a, b)), v("bi", s * GW + a, s * GW + b), OP.is_lt)
+        for a, bk_ in ((0, "b4"), (128, "b3")):
+            qz(v("cq", O1 + a, O1 + a + 128), v("cs", O1 + a, O1 + a + 128), v("ot", 4 * a, 4 * a + 512))
+            const(bk_, 2, O1 + a, 128)
+            if a:
+                cp(v("pw", PAD + a, PAD + HW), v(bk_, 0, HW - a))
+            else:
+                act(v("pw", PAD, PAD + 128), v(bk_, 0, 128), AF.Copy)
+        const("b2", 8, O1 - HO, E)
+        const("b2", 7, O1, HE)
+        const("b1", 8, O1 + GW - 128, 128)
         edge = v("b1", EDGE - HO - GW + 128, EDGE - HO - GW + 160)
-        cp(v("pw", PAD, PAD + HW), v("b4", 0, HW))
         act(v("ab", 0, AW), ind(v("pw"), shifts(2, 0, AW)), AF.Abs, pc(2))
-        act(v("ot", 4 * GW + 2, 4 * (GW + AW), 4), v("ab", 0, AW), AF.Relu, 1.0, -1.0)
-        ts(v("ot", 4 * (GW + AW) + 2, 8 * GW, 4), ind(v("pw"), shifts(2, AW)), pc(14), OP.is_equal)
+        act(v("ot", 1024 + 2, 1024 + 4 * AW, 4), v("ab", 0, AW), AF.Relu, 1.0, -1.0)
+        ts(v("ot", 1024 + 4 * AW + 2, 1024 + 4 * GW, 4), ind(v("pw"), shifts(2, AW)), pc(14), OP.is_equal)
         for s in range(2):
-            ts(v("ot", 4 * GW + s, 8 * GW, 4), ind(v("pw"), shifts(s)), pc(12 + s), OP.is_equal)
-        qz(v("cq", o2, o2 + GW), v("cs", o2, o2 + GW), v("ot", 4 * GW, 8 * GW))
-        const("b3", 5, o2, HE)
-        const("b7", 6, o2 + HE - HO, 128)
+            ts(v("ot", 1024 + s, 1024 + 4 * GW, 4), ind(v("pw"), shifts(s)), pc(12 + s), OP.is_equal)
+        qz(v("cq", O2, O2 + GW), v("cs", O2, O2 + GW), v("ot", 1024, 1024 + 4 * GW))
+        const("b3", 5, O2, HE)
+        const("b7", 6, O2 + HE - HO, 128)
         tt(v("eg", 0, 32), edge, v("eg", 64, 96), OP.is_lt)
         tt(v("eg", 32, 64), edge, v("eg", 0, 32), OP.mult)
         act(v("ad", 0, EDGE), v("b2", 0, EDGE), AF.Abs)
@@ -399,8 +430,8 @@ def rank_program(g, core, T, topo):
         act(v("dl"), v("b2", 0, E), ID, 0.0, pc(24))
         scan(v("xs"), v("irc"), v("dl"), -float(HE), OP.max, OP.add)
         scan(back("mir", 16, 16 + E), v("ones", 0, E), back("xs", 0, E), 500.0, OP.add, OP.min)
-        const("b1", 3, o2, HE)
-        const("b4", 4, o2 + HE - HO, HE)
+        const("b1", 3, O2, HE)
+        const("b4", 4, O2 + HE - HO, HE)
         for k, bk_ in enumerate(("b1", "b4")):
             scan(v("sc", k * HE, k * HE + HE), v(bk_, 0, HE), v("mw", k * HE, k * HE + HE), -2 * P, OP.max, OP.add)
         ts(v("ow"), v("sc", 15, E, 16), pc(42), OP.add)
@@ -415,14 +446,13 @@ def rank_program(g, core, T, topo):
         scan(v("tbs", 0, C), v("keep", 0, C), v("tb", 0, C), 0.0, OP.mult, OP.add)
         scan(v("tbs", E, E + C + 32), v("keep", 0, C + 32), v("tb", E, E + C + 32), 0.0, OP.mult, OP.add)
         ts(v("rkw"), ind(v("tbs"), v("cnl", 0, 2)), 0.25, OP.mult, (EDGE + 32) / 2 - 1.0, OP.add)
-        cp(ind(v("er", 16, 16 + C), v("rkw", 0, 20)), v("mir", 16, 16 + C))
-        ops[-1]["wr"], ops[-1]["rd"] = v("er", 16, 16 + C)[1], v("rkw", 0, 20)[1] + v("mir", 16, 16 + C)[1]
-        for k0, k1, o0, wide in ((0, K, 0, 1), (K, C, 16, 2)):
-            tr(v("tb", k0, k1), v("er", 16 + k0, 16 + k1))
-            tr(v("tb", E + k0 + (32 if k0 else 0), E + k1 + 32), v("er", k0 + (32 if k0 else 0), k1 + 32))
-            ts(v("ew", o0, o0 + 16 * wide), ind(v("tb"), v("cnl", 2, 2 + wide)), float(HE), OP.add)
-            ts(v("mew", o0, o0 + 16 * wide), ind(v("tb"), v("cnl", 0, wide)), float(HE), OP.add)
-            e_, m_ = [v(name, o0 + k0 // 16, o0 + k1 // 16) for name in ("ew", "mew")]
+        cp(ind(v("er", 16, 16 + C), v("rkw", 0, OWN)), v("mir", 16, 16 + C))
+        ops[-1]["wr"], ops[-1]["rd"] = v("er", 16, 16 + C)[1], v("rkw", 0, OWN)[1] + v("mir", 16, 16 + C)[1]
+        for k0, k1, tb in ((0, K, "tb"), (K, C, "tc")):
+            tr(v(tb, k0, k1), v("er", 16 + k0, 16 + k1))
+            tr(v(tb, E + k0, E + k1 + 32), v("er", k0, k1 + 32))
+            ts(v("ew", k0 // 4, k0 // 4 + 32), ind(v(tb, k0), v("cnl", 2, 4)), float(HE), OP.add)
+            e_, m_ = [v("ew", k0 // 4 + x, k0 // 4 + x + (k1 - k0) // 16) for x in (0, 16)]
             for b in range(4):
                 gb, wb = v("ge", b * C + k0, b * C + k1), v("zw", b * C + k0, b * C + k1)
                 zb = v("z", b * C + k0, b * C + k1) if k0 else v("at", b, 4 * K, 4)
@@ -456,16 +486,18 @@ def rank_program(g, core, T, topo):
     for k, (a, b) in enumerate(PIECES[:2]):
         qz(v("fq", a, b), v("fs", a, b), v("xst", 4 * a, 4 * b))
         mm("b%d" % (1 + k), "vq", "vs", 0, "fq", "fs", a, b - a)
+        dma("s", T.oc[:, 4 * a:4 * b], bytes_of(v("fq", a, b)), "ocs")
         if k:
             cp(v("ysb", a, b), v("b2", 0, b - a))
         else:
             act(v("ysb", a, b), v("b1", 0, b - a), AF.Copy)
         dma("s" if k else "a", T.y[:, a:b], v("ysb", a, b), "oy")
-    dma("s", T.oc[:], bytes_of(v("fq")), "ocs")
     for k in range(4):
         dma("s", T.osc[4 * k:4 * k + 4, :], v("fs", 0, C, 1, 32 * k, 32 * k + 4), "ocs")
 
-    emit(g, T, arrange(ops), sent[0])
+    if not ORDER:
+        ORDER.extend(arrange(ops))
+    emit(g, T, [ops[i] for i in ORDER], sent[0])
 
 
 def bits(cols):
@@ -524,7 +556,8 @@ def depends(ops):
 
 
 def arrange(ops):
-    deps = [{j: HOP + (LOAD if ops[j]["dma"] else 60.0 if ops[j]["q"] == "t" else 0.0) for j in d} for d in depends(ops)]
+    own = depends(ops)
+    deps = [{j: ops[j]["load"] if ops[j]["dma"] else 60.0 if ops[j]["q"] == "t" else 0.0 for j in d} for d in own]
     groups, sends = {}, {}
     for i, o in enumerate(ops):
         if o["acc"] is not None:
@@ -535,46 +568,40 @@ def arrange(ops):
             sends[o["raises"]] = i
         for sem, _ in o["ext"]:
             deps[i][sends[sem]] = TRAVEL
+    loads = [i for i, o in enumerate(ops) if o["q"] == "s" and o["wr"]]
+    for i, j in zip(loads, loads[1:]):
+        deps[j].setdefault(i, 0.0)
     for members in groups.values():
         for i in members[1:]:
             deps[i][members[0]] = 0.0
         for i in members[:-1]:
             deps[members[-1]][i] = 0.0
-    time = [o["time"] for o in ops]
-    time[min(i for i, o in enumerate(ops) if o["dma"] == "remote")] += FIRST
-    back = [{} for _ in ops]
-    for i, d in enumerate(deps):
-        for j, gap in d.items():
-            back[j][i] = gap
-    tail = [LOAD if o["dma"] and o["dma"] != "remote" else 0.0 for o in ops]
-    after, below = list(tail), [set() for _ in ops]
-    for i in reversed(range(len(ops))):
-        for j, gap in back[i].items():
-            after[i] = max(after[i], gap + time[j] + after[j])
-            below[i] |= below[j] | {j}
-        load = {}
-        for j in sorted(below[i], key=lambda k: -after[k]):
-            load[ops[j]["q"]] = load.get(ops[j]["q"], 0.0) + time[j]
-            after[i] = max(after[i], load[ops[j]["q"]] + after[j])
-    free, start, left = {}, {}, [len(d) for d in deps]
-    ready = {i: 0.0 for i, d in enumerate(deps) if not d}
-    while ready:
-        at = {i: max(x, free.get(ops[i]["q"], 0.0)) for i, x in ready.items()}
-        i = min(at, key=lambda k: (at[k], -time[k] - after[k], k))
-        start[i] = at[i]
-        free[ops[i]["q"]] = at[i] + time[i]
-        del ready[i]
-        for j in back[i]:
-            left[j] -= 1
-            if not left[j]:
-                ready[j] = max(start[m] + time[m] + gap for m, gap in deps[j].items())
+    every, queue = range(len(ops)), [o["q"] for o in ops]
+    first = min(i for i in every if ops[i]["dma"] == "remote")
+    tail, zero = [LOAD if o["dma"] and o["dma"] != "remote" else 0.0 for o in ops], [0.0] * len(ops)
 
-    def place(order, before, least):
-        busy, begin = {}, {}
+    def model(hop, slow):
+        time = [o["time"] * (slow if o["q"] in "vag" and not o["dma"] else 1.0) for o in ops]
+        time[first] += FIRST
+        fore = [[(j, gap + (hop if j in own[i] else 0.0)) for j, gap in deps[i].items()] for i in every]
+        back = [[] for _ in ops]
+        for i in every:
+            for j, gap in fore[i]:
+                back[j].append((i, gap))
+        return time, fore, back
+
+    def span(order, time, fore, back):
+        free, fin = {}, [0.0] * len(ops)
         for i in order:
-            at = max([begin[j] + time[j] + gap for j, gap in before[i].items()] + [least[i]])
-            line = busy.setdefault(ops[i]["q"], [])
-            k = 0
+            fin[i] = free[queue[i]] = max([fin[j] + gap for j, gap in fore[i]] + [free.get(queue[i], 0.0)]) + time[i]
+        return max(fin[i] + tail[i] for i in every)
+
+    def place(order, before, least, time):
+        busy, begin = {}, [0.0] * len(ops)
+        for i in order:
+            at = max([begin[j] + time[j] + gap for j, gap in before[i]] + [least[i]])
+            line = busy.setdefault(queue[i], [])
+            k = first_after(line, at)
             while k < len(line) and at + time[i] > line[k][0]:
                 at = max(at, line[k][1])
                 k += 1
@@ -582,11 +609,49 @@ def arrange(ops):
             begin[i] = at
         return begin
 
-    every, zero = range(len(ops)), [0.0] * len(ops)
-    for _ in range(PASSES):
-        late = place(sorted(every, key=lambda k: (-start[k] - time[k], -k)), back, tail)
-        start = place(sorted(every, key=lambda k: (-late[k] - time[k], k)), deps, zero)
-    return [ops[i] for i in sorted(every, key=lambda k: (start[k], k))]
+    def plan(time, fore, back, rank):
+        free, start, left = {}, [0.0] * len(ops), [len(d) for d in fore]
+        ready = {i: 0.0 for i in every if not fore[i]}
+        while ready:
+            i = min(ready, key=lambda k: (max(ready[k], free.get(queue[k], 0.0)), -rank[k], k))
+            start[i] = max(ready.pop(i), free.get(queue[i], 0.0))
+            free[queue[i]] = start[i] + time[i]
+            for j, _ in back[i]:
+                left[j] -= 1
+                if not left[j]:
+                    ready[j] = max(start[m] + time[m] + gap for m, gap in fore[j])
+        for _ in range(PASSES):
+            late = place(sorted(every, key=lambda k: (-start[k] - time[k], -k)), back, tail, time)
+            start = place(sorted(every, key=lambda k: (-late[k] - time[k], k)), fore, zero, time)
+        return sorted(every, key=lambda k: (start[k], k))
+
+    judges = [model(HOP, 1.0), model(HOP, SLOW)]
+    rng, best = np.random.default_rng(0), None
+    for hop, slow in PLANS:
+        time, fore, back = model(hop, slow)
+        after, below = list(tail), [set() for _ in ops]
+        for i in reversed(every):
+            for j, gap in back[i]:
+                after[i] = max(after[i], gap + time[j] + after[j])
+                below[i] |= below[j] | {j}
+            load = {}
+            for j in sorted(below[i], key=lambda k: -after[k]):
+                load[queue[j]] = load.get(queue[j], 0.0) + time[j]
+                after[i] = max(after[i], load[queue[j]] + after[j])
+        for k in range(TRIES):
+            order = plan(time, fore, back, [time[i] + after[i] + (NOISE * rng.random() if k else 0.0) for i in every])
+            x = span(order, *judges[0]) + span(order, *judges[1]) / SLOW / 2
+            if best is None or x < best[0]:
+                best = (x, order)
+    return best[1]
+
+
+def first_after(line, at):
+    lo, hi = 0, len(line)
+    while lo < hi:
+        mid = (lo + hi) // 2
+        lo, hi = (mid + 1, hi) if line[mid][1] <= at else (lo, mid)
+    return lo
 
 
 def emit(g, T, ops, sent):

import numpy as np
from concourse.mybir import dt, AluOpType as OP, ActivationFunctionType as AF

C, H, E, K, J, R = 320, 96, 416, 128, 2, 2
HW, GW, HO, PAD = 232, 240, 184, 16
HE = E // 2
NB, OWN = E // 16, C // 16
PIECES = ((0, 128), (128, C), (C, E))
EDGE = C - 16
BIG = 2.0 ** 96
P = 1024.0
DIG = 6144.0
ON_VECTOR, TOP = (14, 14), 24
SN = 416
AW = 160
GATHERS = [(b, 0, 128, b < 1) for b in range(4)] + [(b, 128, C, b < 3) for b in range(4)]
NT = 7
TB = [128, 0] + [u * E for u in range(2, NT)]
TW = [128, 128, 192, 256, 320, 384, E]
TP = [128, 128, HO + 128, HO + 128, 320, 384, E]
O1, O2 = NT * E, NT * E + 256
CYCLE, HOP, LOAD, TRAVEL, FIRST = 0.85, 160.0, 1300.0, 1000.0, 3600.0
LOADS = (1100.0, 1550.0, 2100.0)
PASSES, TRIES, NOISE, SLOW = 2, 8, 300.0, 1.4
PLANS = [(150.0, 1.0), (170.0, 1.0), (200.0, 1.0), (240.0, 1.0), (170.0, 1.2)]
ORDER = []

F32, BF, I32, U16, Q4, U8 = "float32", "bfloat16", "int32", "uint16", "float8_e4m3fn_x4", "uint8"


def _sb(n, d):
    return ("sbuf", [128, n], d)


SCRATCH = {
    "xin": _sb(4 * C, BF), "xst": _sb(4 * C, BF), "uin": _sb(512, BF), "vin": _sb(512, BF),
    "uq": _sb(128, Q4), "us": _sb(128, U8), "ur": _sb(128, Q4), "urs": _sb(128, U8),
    "vq": _sb(128, Q4), "vs": _sb(128, U8), "wq": _sb(512, Q4), "wp": _sb(512, U8),
    "win0": _sb(E, Q4), "wis0": _sb(E, U8), "win1": _sb(E, Q4), "wis1": _sb(E, U8),
    "fq": _sb(C, Q4), "fs": _sb(C, U8),
    "aq0": _sb(K, Q4), "as0": _sb(K, U8), "aq1": _sb(K, Q4), "as1": _sb(K, U8),
    "al0": _sb(K, Q4), "als0": _sb(K, U8), "al1": _sb(K, Q4), "als1": _sb(K, U8),
    "pi": _sb(9, I32), "pf": _sb(9, F32), "pc": _sb(64, F32), "ul": _sb(8, U16), "mk": _sb(256, BF),
    "yrow": _sb(128, BF), "m16": _sb(320, BF), "mrow": _sb(256, BF), "mhi": _sb(256, BF), "c16": _sb(32, F32),
    "irow": _sb(HW, F32), "irc": _sb(E, BF), "ones": _sb(516, BF), "hb": _sb(2 * HW, F32),
    "pvl": _sb(4, U16), "pm": _sb(32, F32), "ibl": _sb(12, U16), "dul": _sb(6, U16), "exl": _sb(NB, U16), "dm": _sb(64, F32),
    "m0": _sb(16, F32), "m1": _sb(16, F32), "m2": _sb(32, F32), "mw16": _sb(16, F32), "mw": _sb(E, F32),
    "shl": _sb(48, U16), "cnf": _sb(4, F32), "cnl": _sb(4, U16),
    "keep": _sb(E, BF), "ctw": _sb(9 * 512, BF), "cwq": _sb(9 * 128, Q4), "cws": _sb(9 * 128, U8),
    "et": _sb(516, BF), "eq": _sb(512, Q4), "es": _sb(512, U8),
    "sb": _sb(E, F32), "pt": _sb(96, F32), "pv": _sb(48, F32), "sg": _sb(8 * NB * NB, BF),
    "rs": _sb(32, F32), "sn": _sb(SN * NB, BF), "seg": _sb(E, BF),
    "y0": _sb(32, F32), "y1": _sb(64, F32), "hi": _sb(64, BF), "lo": _sb(64, F32),
    "ct": _sb(NT * 4 * E, BF), "cq": _sb(O2 + 256, Q4), "cs": _sb(O2 + 256, U8),
    "kw": _sb(272, BF), "bi": _sb(3 * GW, BF), "pw": _sb(272, BF), "ab": _sb(GW, BF),
    "ot": _sb(1024 + 4 * GW, BF), "eg": _sb(96, F32),
    "sc": _sb(E, F32), "ow": _sb(NB, U16), "dl": _sb(E, BF),
    "xs": _sb(E, BF), "mir": _sb(E + 32, BF), "tm": _sb(2 * E + 32, BF), "mrw": _sb(32, U16),
    "ad": _sb(EDGE + 32, BF), "ad2": _sb(EDGE + 32, BF), "acc": _sb(1, F32), "val": _sb(C, BF), "vm": _sb(C + 32, BF),
    "tb": _sb(2 * E + 32, BF), "tc": _sb(2 * E + 32, BF), "tbs": _sb(2 * E + 32, BF),
    "rkw": _sb(32, U16), "er": _sb(C + 32, BF), "ew": _sb(64, U16),
    "fp": _sb(4 * E, BF), "gp": _sb(4 * E, BF), "ge": _sb(4 * C, BF),
    "at": _sb(4 * K, BF), "z": _sb(4 * C, BF), "zw": _sb(4 * C, BF),
    "orow": _sb(E, BF), "mr": _sb(E, F32), "ysb": _sb(C, F32),
}
for _b in range(8):
    SCRATCH["b%d" % _b] = ("psum", [128, 512], F32)

SEMAPHORES = ["qv", "qa", "qt", "qg", "h0", "h1", "f0", "f1", "sent", "dx", "dy", "du", "dv", "dw", "ds",
              "z20", "z21", "z22", "z30", "z31", "oy", "ol", "ocs"]


def rank_program(g, core, T, topo):
    rank = T.rank_of(core)
    if rank is None:
        return
    n = len(T.cores)
    ops = []

    def v(name, a=0, b=None, s=1, p0=0, p1=128):
        cols = range(a, SCRATCH[name][1][1] if b is None else b, s)
        sl = slice(a, cols[-1] + 1, s) if s > 1 else slice(a, cols[-1] + 1)
        ap = T[name][p0:p1, sl] if (p0, p1) != (0, 128) else T[name][:, sl]
        return (ap, [(name, bits(cols), p0, p1, len(cols))])

    def back(name, a, b):
        return (T[name][:, b - 1:a - 1:-1] if a else T[name][:, b - 1::-1], v(name, a, b)[1])

    def ind(win, off, word=False):
        ap = win[0].bitcast(dt.uint32) if word else win[0]
        return (ap.indirect(off[0]), win[1] + off[1])

    def col(name, c, p0=0, p1=128):
        return v(name, c, c + 1, 1, p0, p1)

    def add(q, fn, outs, ins, ext=(), dma=None, acc=None, rate=None):
        ins = [x for x in ins if isinstance(x, tuple)]
        ops.append({"q": q, "fn": fn, "rd": [r for x in ins for r in x[1]], "wr": [r for x in outs for r in x[1]],
                    "ext": list(ext), "dma": dma, "acc": acc, "time": length(q, outs, ins, dma, rate)})

    def ap(x):
        return x[0] if isinstance(x, tuple) else x

    def ts(out, a, s1, op0, s2=None, op1=None):
        if op1 is None:
            add("v", lambda: g.vector.tensor_scalar(ap(out), ap(a), ap(s1), None, op0), [out], [a, s1])
        else:
            add("v", lambda: g.vector.tensor_scalar(ap(out), ap(a), ap(s1), ap(s2), op0, op1), [out], [a, s1, s2])

    def tt(out, a, b, op):
        add("v", lambda: g.vector.tensor_tensor(ap(out), ap(a), ap(b), op), [out], [a, b], rate=2.0)

    def cp(out, a):
        add("v", lambda: g.vector.tensor_copy(ap(out), ap(a)), [out], [a])

    def scan(out, a, b, init, op0, op1):
        add("v", lambda: g.vector.tensor_tensor_scan(ap(out), ap(a), ap(b), ap(init), op0, op1), [out], [a, b, init])

    def ms(out, c):
        add("v", lambda: g.vector.memset(ap(out), c), [out], [])

    def tr(out, a):
        add("v", lambda: g.vector.transpose(ap(out), ap(a)), [out], [a])

    def qz(q, s, a):
        add("v", lambda: g.vector.quantize_mx(ap(q), ap(s), ap(a)), [q, s], [a], rate=1.0)

    def act(out, a, f, bias=0.0, scale=1.0, accum=None):
        if accum is not None:
            add("a", lambda: g.scalar.activation(ap(out), ap(a), f, bias=ap(bias), scale=scale, accum_out=ap(accum)),
                [out, accum], [a, bias])
        elif f != AF.Copy:
            add("a", lambda: g.scalar.activation(ap(out), ap(a), f, bias=ap(bias), scale=ap(scale)), [out], [a, bias, scale])
        elif scale != 1.0:
            add("a", lambda: g.scalar.activation(ap(out), ap(a), f, scale=scale), [out], [a])
        else:
            add("a", lambda: g.scalar.activation(ap(out), ap(a), f), [out], [a])

    def mm(bank, w, ws_, wc0, x, xs_, xc0, cols, start=True, stop=True, ext=(), acc=None):
        o, a, b = v(bank, 0, cols), v(w, wc0, wc0 + 128), v(ws_, wc0, wc0 + 128)
        c, d = v(x, xc0, xc0 + cols), v(xs_, xc0, xc0 + cols)
        add("t", lambda: g.tensor.matmul_mx(o[0], a[0], b[0], c[0], d[0], start, stop), [o], [a, b, c, d], ext, None, acc)

    def iota(out, pat, base, cm, small=True):
        if small:
            add("g", lambda: g.iota(ap(out), pat, base, cm, allow_small_or_imprecise_dtypes=True), [out], [])
        else:
            add("g", lambda: g.iota(ap(out), pat, base, cm), [out], [])

    def fill(out, c):
        iota(out, [[0, out[1][0][4]]], c, 0)

    def select(out, pat, op, base, cm):
        src = v("ones", 0, out[1][0][4])
        add("g", lambda: g.affine_select(out[0], src[0], pat, op, 0.0, base, cm), [out], [src])

    def dma(q, out, a, sem, load=LOAD):
        eng = g.sync if q == "s" else g.scalar
        outs = [out] if isinstance(out, tuple) else []
        add(q, lambda: eng.dma_start(ap(out), ap(a)), outs, [a], (), sem)
        ops[-1]["load"] = load

    def bytes_of(x):
        return (x[0].bitcast(dt.uint8), x[1])

    sent = [0]

    def send(dst, qd, sd, c0, qs, ss, cols, sem):
        rid, pid, _ = topo.addr(dst)
        m = topo.mask(core, dst)
        for src, land in ((bytes_of(v(qs, 0, cols)), bytes_of(v(qd, c0, c0 + cols))), (v(ss, 0, cols), v(sd, c0, c0 + cols))):
            add("g", lambda src=src, land=land: g.remote_dma(land[0], src[0], T.sem[sem], T.sem.sent, pid, rid, m),
                [], [src], (), "remote")
            ops[-1]["raises"] = sem
            sent[0] += len(topo.engines(core, dst))

    prev, far = T.cores[(rank - 1) % n], T.cores[(rank + J) % n]
    n_halo = 2 * len(topo.engines(T.cores[(rank + 1) % n], core))
    n_far = 2 * len(topo.engines(T.cores[(rank - J) % n], core))

    dma("s", v("xin", 0, 512), T.x[:, 0:512], "dx", LOADS[0])
    dma("s", v("uin"), T.u[:], "du", LOADS[1])
    dma("s", v("xin", 512, 4 * C), T.x[:, 512:4 * C], "dy", LOADS[2])

    ID = AF.Identity
    r_, a_, _, g_, h_, rh, rl_, par = [col("pf", k) for k in range(1, 9)]

    def pc(k, p0=0, p1=128):
        return col("pc", k, p0, p1)

    iota(col("pi", 0), [[0, 1]], 0, 1, False)
    iota(v("c16"), [[16, 32]], 0, 0)
    iota(v("m16"), [[0, 5], [1, 16], [0, 4]], 0, 0)
    iota(v("yrow"), [[0, 8], [1, 16]], 0, 0)
    iota(v("irow"), [[1, HW]], 0, 0)
    iota(v("irc"), [[1, E]], -HE, 0)
    iota(v("mhi"), [[1, 16], [0, 16]], 0, 0)
    iota(v("mrow"), [[1, 256]], 0, 0)
    iota(v("eg", 64, 96), [[-1, 32]], C - EDGE, 0)
    for name, c in (("y0", 0.0), ("pv", -BIG), ("ones", 1.0)):
        ms(v(name), c)
    ms(col("sn", SN - 1), 0.0)
    for u in range(NT):
        a0, w = 4 * (TB[u] + 16 * (4 * u + 1)), 4 * (TP[u] - 16 * (4 * u + 1))
        if u < 2:
            act(v("ct", a0, a0 + w), v("ones", 0, w), AF.Copy, 0.0, 0.0)
        elif u < 4:
            for a in range(0, w, 256):
                k = min(w - a, 256)
                dma("s", v("ct", a0 + a, a0 + a + k), v("ct", 4 * TB[0] + 256, 4 * TB[0] + 256 + k), "z%d%d" % (u, a // 256))
        else:
            fill(v("ct", a0, a0 + w), 0)
    for out, src, sem in ((bytes_of(v("wq")), T.wc[:], "dw"), (v("wp"), T.ws[:], "ds"), (v("vin"), T.v[:], "dv")):
        dma("s", out, src, sem)
        ops[-1]["rd"] = v("xin")[1]
    select(v("et"), [[1, 516]], OP.is_equal, -3, -4)
    select(v("keep"), [[0, NB], [1, 16]], OP.not_equal, 0, 0)
    fill(v("ctw", 1024 + 3, 1536, 4), 0)
    fill(v("ctw", 1536 + 3, 9 * 512, 4), 0)
    fill(v("ot", 3, 1024 + 4 * GW, 4), 0)
    fill(v("ot", 4 * GW, 1024), 0)
    fill(v("bi", HW, GW), 0)
    for name, c in (("kw", 1024), ("pw", 99)):
        fill(v(name, 0, PAD), c)
        fill(v(name, PAD + HW, 272), c)
    for name, w in (("vm", C), ("er", C), ("mir", E)):
        fill(v(name, 0, 16), 0)
        fill(v(name, 16 + w, 32 + w), 0)
    for name in ("tb", "tbs", "tc"):
        fill(v(name, C, E), 0)
        fill(v(name, E + C + 32, 2 * E + 32), 0)
    p_ = col("pi", 0)
    ts(col("pi", 4), p_, 7, OP.bitwise_and)
    ts(col("pi", 1), p_, 15, OP.bitwise_and)
    ts(col("pi", 2), p_, 4, OP.arith_shift_right)
    ts(col("pi", 5), p_, 3, OP.arith_shift_right, 1, OP.bitwise_and)
    ts(col("pi", 6), p_, 1, OP.arith_shift_right, 7, OP.bitwise_and)
    ts(col("pi", 7), p_, 1, OP.bitwise_and)
    tt(col("pi", 3), p_, col("pi", 2), OP.add)
    cp(v("pf", 1, 7), v("pi", 1, 7))
    ts(col("pi", 8), col("pi", 3), 1, OP.bitwise_and)
    cp(v("pf", 7, 9), v("pi", 7, 9))
    ts(v("ul"), v("ones", 0, 8), g_, OP.mult, 16.0, OP.mult)
    qz(v("uq"), v("us"), v("uin"))
    cp((v("ur")[0].bitcast(dt.uint32), v("ur")[1]), ind(v("uq"), v("ul"), True))
    act(v("urs"), ind(v("us"), v("ul")), AF.Copy)
    qz(v("vq"), v("vs"), v("vin"))
    act(pc(43), a_, ID, rl_, 2.0)
    act(pc(44), rh, ID, pc(43), 16.0)
    iota(v("y1"), [[0, 32], [1, 2]], 0, 0)
    ts(v("dm"), v("y1"), h_, OP.is_equal, -1.0, OP.mult)
    act(v("pm"), v("dm", 0, 32), ID, -BIG, -BIG)
    ts(v("pvl", 0, 2), v("c16", 0, 16, 8), pc(44), OP.add, C - 129.0, OP.min)
    ts(v("pvl", 2, 3), v("c16", 0, 1), pc(44), OP.add, H - 1.0, OP.min)
    act(pc(50), a_, ID, 0.0, 2.0)
    ts(pc(51), r_, pc(50), OP.is_le, 1.0 / 16, OP.mult)
    ts(pc(53), rh, a_, OP.is_equal, 1.0 / 8, OP.mult)
    act(pc(52), pc(51), ID, 12.0, -192.0)
    ts(v("ibl"), v("c16", 0, 12), pc(51), OP.mult, pc(52), OP.add)
    act(pc(60), h_, ID, rh, 100.0)
    ts(v("dul", 0, 2), v("c16", 0, 2), 0.5, OP.mult, rh, OP.add)
    ts(v("dul", 2, 3), pc(60), 16.0, OP.add, 31.0, OP.min)
    ts(v("dul", 4, 5), rh, float(OWN), OP.add)
    for k, zero, a, b in ((61, 47.0, 0, OWN), (62, 15.0, OWN, NB)):
        act(pc(k - 16), rl_, ID, -8.0 * zero, 8.0)
        act(pc(k), pc(53), ID, zero, pc(k - 16))
        ts(v("exl", a, b), v("c16", 0, b - a), pc(53), OP.mult, pc(k), OP.add)
    for p0, p1, sg_, c in ((0, 64, 1.0, 0.0), (64, 128, -1.0, 11.0)):
        act(pc(9, p0, p1), col("pf", 2, p0, p1), ID, c, 3.0 * sg_)
        act(v("pc", 0, 3, 1, p0, p1), v("c16", 0, 3, 1, p0, p1), ID, pc(9, p0, p1), sg_ / 16)
        act(pc(8, p0, p1), col("pf", 2, p0, p1), ID, sg_, 0.0)
        act(pc(56, p0, p1), col("pf", 5, p0, p1), ID, (192 - 15.5 / 32) * sg_, HO / 32 * sg_)
    act(v("pc", 4, 7), v("pc", 0, 3), AF.Abs)
    act(v("pc", 57, 60), v("pc", 4, 7), ID, 0.0, -1.0)
    act(pc(10), pc(8), ID, 0.0, 1.0 / 32)
    act(pc(16), pc(8), ID, 0.0, -6.0)
    act(pc(11), h_, ID, pc(56), pc(16))
    act(v("hb", 0, 16 * TOP - HO), v("irow", 0, 16 * TOP - HO), ID, pc(56), pc(10))
    act(v("hb", 16 * TOP - HO, HW), v("irow", 16 * TOP - HO, HW), ID, pc(11), pc(10))
    act(v("hb", HW, 2 * HW), v("hb", 0, HW), ID, pc(57))
    act(v("pc", 12, 15), v("pc", 0, 3), ID, 0.0, -1.0)
    act(pc(23), r_, ID, float(PAD))
    act(pc(25), r_, ID, -0.5, -1.0)
    act(pc(24), rl_, ID, 0.0, 1024.0)
    act(pc(28), r_, ID, 0.0, 16.0)
    act(pc(49), g_, ID, 8.0)
    act(v("pc", 20, 23), v("pc", 0, 3), ID, pc(23))
    act(v("pc", 32, 35), v("pc", 4, 7), ID, pc(28))
    act(pc(31), par, ID, pc(28), E + 16.0)
    act(v("cnf", 0, 2), v("c16", 0, 32, 16), ID, pc(31))
    act(v("cnf", 2, 3), v("cnf", 0, 1), ID, -1.0)
    act(v("cnf", 3, 4), v("cnf", 0, 1), ID, 0.0)
    ts(v("cnl"), v("cnf"), 15.0, OP.add, 2 * E + 31.0, OP.min)
    act(pc(30), r_, ID, P)
    ts(v("m0"), v("yrow", 0, 16), r_, OP.is_equal)
    ts(v("m1"), v("yrow", 0, 16), r_, OP.is_equal, pc(30), OP.mult)
    ts(v("m2", 0, 17), v("yrow", 0, 17), r_, OP.is_equal, -2 * P, OP.mult)
    tt(v("mw16"), v("m1"), v("m2", 1, 17), OP.add)
    act(pc(42), col("m2", 0), ID, -P, -1.0)
    for x in range(16):
        act(v("mw", x, E, 16), v("c16", 0, NB), ID, col("mw16", x), col("m0", x))
    for a, b, c in ((0, 64, 1.0), (64, 136, -1.0)):
        ts(v("ctw", 4 * a, 4 * b), v("m16", 0, 4 * (b - a)), pc(49), OP.is_equal, c / 32, OP.mult)
    qz(v("cwq", 0, 136), v("cws", 0, 136), v("ctw", 0, 544))
    act(pc(26), r_, ID, 0.0, -1.0)
    act(v("mk", 0, 128), v("yrow"), AF.Abs, pc(26))
    act(v("mk", 128, 256), v("mk", 0, 128), AF.Relu, 1.0, -1.0)
    for s in range(3):
        ts(v("shl", 16 * s, 16 * s + 16), v("c16", 0, 16), pc(20 + s), OP.add)
        act(v("ctw", 1024 + s, 1536, 4), v("mk", 128, 256), ID, 0.0, pc(8))
        ts(v("ctw", 1536 + s, 2560, 4), v("mhi"), r_, OP.is_equal, pc(s), OP.mult)
        ts(v("ctw", 2560 + s, 3584, 4), v("mrow"), pc(32 + s), OP.is_equal, 2.0, OP.mult)
        act(v("ctw", 3584 + s, 4608, 4), v("ctw", 1536 + s, 2560, 4), AF.Sign)
    for a, b in ((2, 3), (3, 5), (5, 7), (7, 9)):
        qz(v("cwq", 128 * a, 128 * b), v("cws", 128 * a, 128 * b), v("ctw", 512 * a, 512 * b))
    for b in range(4):
        qz(v("eq", 128 * b, 128 * b + 128), v("es", 128 * b, 128 * b + 128), v("et", 3 - b, 515 - b))

    def slot(k, a, b):
        base = 4 * TB[k // 4] + k % 4
        return v("ct", base + 4 * a, base + 4 * b, 4)

    def tri(name, c):
        return v(name, 8 * c * (c - 1), 8 * c * (c + 1))

    def shifts(s, a=0, b=GW):
        return v("shl", 16 * s + a // 16, 16 * s + b // 16)

    def plane(b):
        return v("gp", b * E, b * E + E)

    def bank(b):
        return "b%d" % ((5 + b) % 8)

    def const(bk_, tile, o, w):
        mm(bk_, "cwq", "cws", 128 * tile, "cq", "cs", o, w)

    for t in range(R):
        first, last = t == 0, t == R - 1
        win, wis, xt = "win%d" % t, "wis%d" % t, "xin" if first else "xst"
        halo = [("h%d" % t, n_halo)]

        for k, (a, b) in enumerate(PIECES):
            w, bk_ = b - a, "b%d" % k
            if b <= C:
                qz(v(win, a, b), v(wis, a, b), v(xt, 4 * a, 4 * b))
                mm(bk_, "ur", "urs", 0, win, wis, a, w)
            else:
                mm(bk_, "ur", "urs", 0, win, wis, b - 128, 128, ext=halo)
            src = v(bk_, max(0, 128 - w), max(128, w))
            if k == 0:
                send(prev, win, wis, C, win, wis, H, "h%d" % t)
                cp(v("sb", a, b), src)
            else:
                act(v("sb", a, b), src, AF.Copy)
            l0, wide = (0, -(-w // 128)) if b <= C else (2, 1)
            tt(v("pt", 32 * k, 32 * k + 16 * wide), ind(v("sb", a, b), v("pvl", l0, l0 + wide)), v("pm", 0, 16 * wide), OP.add)
            tt(v("pv", 16 * k, 16 * k + w // 16), v("pt", 32 * k, 32 * k + w // 8, 2), v("pt", 32 * k + 1, 32 * k + w // 8, 2), OP.max)
            tt(slot(NB - 1, a, b), ind(v("pv", 16 * k, 16 * k + 16), v("ibl", 0, w // 16)), v("sb", a, b), OP.is_gt)
        for b in range(4):
            mm(bank(b), "eq", "es", 128 * b, win, wis, 0, E, ext=halo)
            act(v("fp", b * E, b * E + E), v(bank(b), 0, E), AF.Copy)

        nv = ON_VECTOR[t]
        for c in range(1, NB):
            k = max(k for k, (a, b) in enumerate(PIECES) if a <= 16 * c)
            x, below, pivot = slot(c - 1, 0, 16 * c), v("sb", 0, 16 * c), col("pv", 16 * k + c - PIECES[k][0] // 16)
            if c <= nv or c >= TOP:
                ts(x, below, pivot, OP.is_lt)
                scan(v("sn", SN * (c + 1) - 16 * c, SN * (c + 1)), x, v("ones", 0, 16 * c), -192.0 * (c >= TOP), OP.add, OP.mult)
            else:
                act(tri("sg", c), below, AF.Sign, pivot, -1.0)
                act(x, tri("sg", c), AF.Relu, 0.0, 1.0, col("rs", c))
        for c0, c1, o, w in ((0, OWN, 0, 48), (OWN, NB, 48, 16)):
            a0, a1 = 16 * c0, 16 * c1
            scan(v("seg", a0, a1), v("keep", 0, a1 - a0), slot(NB - 1, a0, a1), 0.0, OP.mult, OP.add)
            for a, b, run in ((0, nv + 1, True), (nv + 1, TOP, False), (TOP, NB, True)):
                a, b = max(a, c0), min(b, c1)
                if a < b:
                    sums = v("sn", SN * (a + 1) - 1, SN * b, SN) if run else v("rs", a, b)
                    tt(v("y0", a, b), sums, v("seg", 16 * a + 15, 16 * b, 16), OP.add)
            y1, hi, lo = [v(name, o, o + w) for name in ("y1", "hi", "lo")]
            tt(y1, ind(v("y0"), v("dul", c0 // 5, c0 // 5 + w // 16)), v("dm", 0, w), OP.mult)
            ts(hi, y1, DIG, OP.add)
            tt(lo, y1, hi, OP.subtract)
            act(slot(NB, a0, a1), ind(hi, v("exl", c0, c1)), ID, -DIG)
            if c0 == 0:
                act(slot(NB + 1, a0, a1), ind(lo, v("exl", c0, c1)), ID, DIG)
            else:
                ts(slot(NB + 1, a0, a1), ind(lo, v("exl", c0, c1)), DIG, OP.add)
        for u in (3, 2, 1, 0, 4, 5, 6):
            w = (TP if first else TW)[u] + ((128 if first else 64) if u == 1 else 0)
            for a, b, hs in ((0, HW, (0,)), (HW, E, (1,))) if u == 6 else ((0, w, (0, 1) if TW[u] > HO else (0,)),):
                if u:
                    qz(v("cq", TB[u] + a, TB[u] + b), v("cs", TB[u] + a, TB[u] + b), v("ct", 4 * (TB[u] + a), 4 * (TB[u] + b)))
                for h in hs:
                    mm("b4", "cwq", "cws", 8 - 8 * h, "cq", "cs", TB[u] + HO * h, max(128, min(HW, TW[u] - HO * h)),
                       (u, h) == (3, 0), (u, h) == (6, 1), (), ("st", t))

        tt(v("kw", PAD, PAD + HW), v("b4", 0, HW), v("hb", 0, HW), OP.add)
        tt(v("bi", 0, HW), v("b4", 0, HW), v("hb", HW, 2 * HW), OP.add)
        for s in (1, 2):
            act(v("bi", s * GW, s * GW + GW), v("kw", PAD, PAD + GW), ID, pc(57 + s))
        for s, a, b in ((0, 0, GW), (1, 0, GW), (2, 0, 128), (2, 128, GW)):
            tt(v("ot", 4 * a + s, 4 * b, 4), ind(v("kw"), shifts(s, a, b)), v("bi", s * GW + a, s * GW + b), OP.is_lt)
        for a, bk_ in ((0, "b4"), (128, "b3")):
            qz(v("cq", O1 + a, O1 + a + 128), v("cs", O1 + a, O1 + a + 128), v("ot", 4 * a, 4 * a + 512))
            const(bk_, 2, O1 + a, 128)
            if a:
                cp(v("pw", PAD + a, PAD + HW), v(bk_, 0, HW - a))
            else:
                act(v("pw", PAD, PAD + 128), v(bk_, 0, 128), AF.Copy)
        const("b2", 8, O1 - HO, E)
        const("b2", 7, O1, HE)
        const("b1", 8, O1 + GW - 128, 128)
        edge = v("b1", EDGE - HO - GW + 128, EDGE - HO - GW + 160)
        act(v("ab", 0, AW), ind(v("pw"), shifts(2, 0, AW)), AF.Abs, pc(2))
        act(v("ot", 1024 + 2, 1024 + 4 * AW, 4), v("ab", 0, AW), AF.Relu, 1.0, -1.0)
        ts(v("ot", 1024 + 4 * AW + 2, 1024 + 4 * GW, 4), ind(v("pw"), shifts(2, AW)), pc(14), OP.is_equal)
        for s in range(2):
            ts(v("ot", 1024 + s, 1024 + 4 * GW, 4), ind(v("pw"), shifts(s)), pc(12 + s), OP.is_equal)
        qz(v("cq", O2, O2 + GW), v("cs", O2, O2 + GW), v("ot", 1024, 1024 + 4 * GW))
        const("b3", 5, O2, HE)
        const("b7", 6, O2 + HE - HO, 128)
        tt(v("eg", 0, 32), edge, v("eg", 64, 96), OP.is_lt)
        tt(v("eg", 32, 64), edge, v("eg", 0, 32), OP.mult)
        act(v("ad", 0, EDGE), v("b2", 0, EDGE), AF.Abs)
        act(v("ad", EDGE, EDGE + 32), v("eg", 32, 64), AF.Abs)
        act(v("ad2"), v("ad"), AF.Sign, pc(25), 1.0, v("acc"))
        act(v("dl"), v("b2", 0, E), ID, 0.0, pc(24))
        scan(v("xs"), v("irc"), v("dl"), -float(HE), OP.max, OP.add)
        scan(back("mir", 16, 16 + E), v("ones", 0, E), back("xs", 0, E), 500.0, OP.add, OP.min)
        const("b1", 3, O2, HE)
        const("b4", 4, O2 + HE - HO, HE)
        for k, bk_ in enumerate(("b1", "b4")):
            scan(v("sc", k * HE, k * HE + HE), v(bk_, 0, HE), v("mw", k * HE, k * HE + HE), -2 * P, OP.max, OP.add)
        ts(v("ow"), v("sc", 15, E, 16), pc(42), OP.add)
        for b in range(4):
            act(plane(b), ind(v("fp", b * E, b * E + E), v("ow")), AF.Copy, 0.0, -0.5)

        for bk_, a, b in (("b3", 0, HE), ("b7", HE, C)):
            scan(v("val", a, b), v(bk_, 0, b - a), v("ones", 0, b - a), col("val", a - 1) if a else v("acc"), OP.add, OP.mult)
            tt(v("vm", 16 + a, 16 + b), v(bk_, 0, b - a), v("val", a, b), OP.mult)
        tr(v("tb", 0, C), v("vm", 16, 16 + C))
        tr(v("tb", E, E + C + 32), v("vm"))
        scan(v("tbs", 0, C), v("keep", 0, C), v("tb", 0, C), 0.0, OP.mult, OP.add)
        scan(v("tbs", E, E + C + 32), v("keep", 0, C + 32), v("tb", E, E + C + 32), 0.0, OP.mult, OP.add)
        ts(v("rkw"), ind(v("tbs"), v("cnl", 0, 2)), 0.25, OP.mult, (EDGE + 32) / 2 - 1.0, OP.add)
        cp(ind(v("er", 16, 16 + C), v("rkw", 0, OWN)), v("mir", 16, 16 + C))
        ops[-1]["wr"], ops[-1]["rd"] = v("er", 16, 16 + C)[1], v("rkw", 0, OWN)[1] + v("mir", 16, 16 + C)[1]
        for k0, k1, tb in ((0, K, "tb"), (K, C, "tc")):
            tr(v(tb, k0, k1), v("er", 16 + k0, 16 + k1))
            tr(v(tb, E + k0, E + k1 + 32), v("er", k0, k1 + 32))
            ts(v("ew", k0 // 4, k0 // 4 + 32), ind(v(tb, k0), v("cnl", 2, 4)), float(HE), OP.add)
            e_, m_ = [v("ew", k0 // 4 + x, k0 // 4 + x + (k1 - k0) // 16) for x in (0, 16)]
            for b in range(4):
                gb, wb = v("ge", b * C + k0, b * C + k1), v("zw", b * C + k0, b * C + k1)
                zb = v("z", b * C + k0, b * C + k1) if k0 else v("at", b, 4 * K, 4)
                act(gb, ind(plane(b), e_), AF.Copy, 0.0, -2.0)
                tt(zb, ind(plane(b), m_), gb, OP.add)
                if k0:
                    act(wb, zb, AF.Copy, 0.0, 32.0)
                else:
                    ts(wb, zb, 32.0, OP.mult)
            if k0 == 0:
                qz(v("aq%d" % t), v("as%d" % t), v("at"))
                send(far, "al%d" % t, "als%d" % t, 0, "aq%d" % t, "as%d" % t, K, "f%d" % t)
        if last:
            tr(v("tm", 0, E), v("mir", 16, 16 + E))
            tr(v("tm", E, 2 * E + 32), v("mir"))
            ts(v("mrw"), ind(v("tm"), v("cnl", 0, 2)), float(HE), OP.add)
            act(v("orow"), ind(v("irc"), v("ow")), AF.Copy)
            act(v("mr"), ind(v("orow"), v("mrw", 0, NB)), ID, float(HE))
            dma("s", T.lm[:], (T.mr[0:128:16, :], v("mr")[1]), "ol")

        for b in range(4):
            mm(bank(b), "wq", "wp", 128 * b, "al%d" % t, "als%d" % t, 0, K, ext=[("f%d" % t, n_far)])
            tt(v("zw", b * C, b * C + K), v(bank(b), 0, K), v("zw", b * C, b * C + K), OP.add)
        for b, lo, hi, on_scalar in GATHERS:
            src = ind(v("zw", b * C, b * C + C), v("rkw", lo // 16, hi // 16))
            if on_scalar:
                act(v("xst", 4 * lo + b, 4 * hi, 4), src, AF.Copy, 0.0, 1.0 / 32)
            else:
                ts(v("xst", 4 * lo + b, 4 * hi, 4), src, 1.0 / 32, OP.mult)

    for k, (a, b) in enumerate(PIECES[:2]):
        qz(v("fq", a, b), v("fs", a, b), v("xst", 4 * a, 4 * b))
        mm("b%d" % (1 + k), "vq", "vs", 0, "fq", "fs", a, b - a)
        dma("s", T.oc[:, 4 * a:4 * b], bytes_of(v("fq", a, b)), "ocs")
        if k:
            cp(v("ysb", a, b), v("b2", 0, b - a))
        else:
            act(v("ysb", a, b), v("b1", 0, b - a), AF.Copy)
        dma("s" if k else "a", T.y[:, a:b], v("ysb", a, b), "oy")
    for k in range(4):
        dma("s", T.osc[4 * k:4 * k + 4, :], v("fs", 0, C, 1, 32 * k, 32 * k + 4), "ocs")

    if not ORDER:
        ORDER.extend(arrange(ops))
    emit(g, T, [ops[i] for i in ORDER], sent[0])


def bits(cols):
    return ((1 << len(cols) * cols.step) - 1) // ((1 << cols.step) - 1) << cols.start


def meets(a, b):
    if a[0] != b[0] or a[3] <= b[2] or b[3] <= a[2]:
        return False
    return SCRATCH[a[0]][0] == "psum" or a[1] & b[1] != 0


def length(q, outs, ins, dma, rate):
    if dma:
        return 300.0 if dma == "remote" else 60.0
    n = outs[0][1][0][4]
    full = [x[1][0][0] for x in outs[:1] + ins if x[1][0][4] == n]
    if q == "t":
        return 0.6 * (n + 16)
    if q == "g":
        return 150 + 2.0 * CYCLE * n
    if len(outs[0][1]) > 1:
        return 50 + 3.8 * CYCLE * n
    if any(len(x[1]) > 1 for x in ins):
        return 60 + 1.56 * CYCLE * n
    if rate == 2.0 and any(SCRATCH[b][0] == "psum" for b in full):
        rate = 1.0
    if rate is None:
        rate = 0.5 if q == "v" and all(SCRATCH[b][2] in (BF, U16) for b in full) else 1.0
    return (30 if q == "v" else 60) + CYCLE * max(32.0, rate * n)


def depends(ops):
    deps = []
    by_buf = {}
    for i, o in enumerate(ops):
        d = set()
        for kind, regs in (("r", o["rd"]), ("w", o["wr"])):
            for reg in regs:
                psum = SCRATCH[reg[0]][0] == "psum"
                for j, k2, r2 in by_buf.get(reg[0], []):
                    if j in d or not meets(reg, r2):
                        continue
                    if kind == "r" and k2 == "r" and not (psum and ops[j]["q"] != o["q"]):
                        continue
                    if o["acc"] is not None and ops[j]["acc"] == o["acc"]:
                        continue
                    if ops[j]["dma"] == "remote":
                        continue
                    d.add(j)
        deps.append(d)
        for kind, regs in (("r", o["rd"]), ("w", o["wr"])):
            for reg in regs:
                by_buf.setdefault(reg[0], []).append((i, kind, reg))
    return deps


def arrange(ops):
    own = depends(ops)
    deps = [{j: ops[j]["load"] if ops[j]["dma"] else 60.0 if ops[j]["q"] == "t" else 0.0 for j in d} for d in own]
    groups, sends = {}, {}
    for i, o in enumerate(ops):
        if o["acc"] is not None:
            groups.setdefault(o["acc"], []).append(i)
        if o["dma"] == "remote":
            if sends:
                deps[i][max(sends.values())] = 0.0
            sends[o["raises"]] = i
        for sem, _ in o["ext"]:
            deps[i][sends[sem]] = TRAVEL
    loads = [i for i, o in enumerate(ops) if o["q"] == "s" and o["wr"]]
    for i, j in zip(loads, loads[1:]):
        deps[j].setdefault(i, 0.0)
    for members in groups.values():
        for i in members[1:]:
            deps[i][members[0]] = 0.0
        for i in members[:-1]:
            deps[members[-1]][i] = 0.0
    every, queue = range(len(ops)), [o["q"] for o in ops]
    first = min(i for i in every if ops[i]["dma"] == "remote")
    tail, zero = [LOAD if o["dma"] and o["dma"] != "remote" else 0.0 for o in ops], [0.0] * len(ops)

    def model(hop, slow):
        time = [o["time"] * (slow if o["q"] in "vag" and not o["dma"] else 1.0) for o in ops]
        time[first] += FIRST
        fore = [[(j, gap + (hop if j in own[i] else 0.0)) for j, gap in deps[i].items()] for i in every]
        back = [[] for _ in ops]
        for i in every:
            for j, gap in fore[i]:
                back[j].append((i, gap))
        return time, fore, back

    def span(order, time, fore, back):
        free, fin = {}, [0.0] * len(ops)
        for i in order:
            fin[i] = free[queue[i]] = max([fin[j] + gap for j, gap in fore[i]] + [free.get(queue[i], 0.0)]) + time[i]
        return max(fin[i] + tail[i] for i in every)

    def place(order, before, least, time):
        busy, begin = {}, [0.0] * len(ops)
        for i in order:
            at = max([begin[j] + time[j] + gap for j, gap in before[i]] + [least[i]])
            line = busy.setdefault(queue[i], [])
            k = first_after(line, at)
            while k < len(line) and at + time[i] > line[k][0]:
                at = max(at, line[k][1])
                k += 1
            line.insert(k, (at, at + time[i]))
            begin[i] = at
        return begin

    def plan(time, fore, back, rank):
        free, start, left = {}, [0.0] * len(ops), [len(d) for d in fore]
        ready = {i: 0.0 for i in every if not fore[i]}
        while ready:
            i = min(ready, key=lambda k: (max(ready[k], free.get(queue[k], 0.0)), -rank[k], k))
            start[i] = max(ready.pop(i), free.get(queue[i], 0.0))
            free[queue[i]] = start[i] + time[i]
            for j, _ in back[i]:
                left[j] -= 1
                if not left[j]:
                    ready[j] = max(start[m] + time[m] + gap for m, gap in fore[j])
        for _ in range(PASSES):
            late = place(sorted(every, key=lambda k: (-start[k] - time[k], -k)), back, tail, time)
            start = place(sorted(every, key=lambda k: (-late[k] - time[k], k)), fore, zero, time)
        return sorted(every, key=lambda k: (start[k], k))

    judges = [model(HOP, 1.0), model(HOP, SLOW)]
    rng, best = np.random.default_rng(0), None
    for hop, slow in PLANS:
        time, fore, back = model(hop, slow)
        after, below = list(tail), [set() for _ in ops]
        for i in reversed(every):
            for j, gap in back[i]:
                after[i] = max(after[i], gap + time[j] + after[j])
                below[i] |= below[j] | {j}
            load = {}
            for j in sorted(below[i], key=lambda k: -after[k]):
                load[queue[j]] = load.get(queue[j], 0.0) + time[j]
                after[i] = max(after[i], load[queue[j]] + after[j])
        for k in range(TRIES):
            order = plan(time, fore, back, [time[i] + after[i] + (NOISE * rng.random() if k else 0.0) for i in every])
            x = span(order, *judges[0]) + span(order, *judges[1]) / SLOW / 2
            if best is None or x < best[0]:
                best = (x, order)
    return best[1]


def first_after(line, at):
    lo, hi = 0, len(line)
    while lo < hi:
        mid = (lo + hi) // 2
        lo, hi = (mid + 1, hi) if line[mid][1] <= at else (lo, mid)
    return lo


def emit(g, T, ops, sent):
    eng = {"v": g.vector, "a": g.scalar, "t": g.tensor, "g": g, "s": g.sync}
    deps = depends(ops)
    known_q = {q: ({}, set()) for q in eng}
    done = []
    waits = []
    needed = set()
    for i, o in enumerate(ops):
        last, dm = known_q[o["q"]]
        last, dm = dict(last), set(dm)
        w = []
        for j in sorted(deps[i], reverse=True):
            oj = ops[j]
            if oj["dma"]:
                if j in dm:
                    continue
            elif last.get(oj["q"], -1) >= j:
                continue
            w.append(j)
            needed.add(j)
            l2, d2 = done[j]
            for q, x in l2.items():
                last[q] = max(last.get(q, -1), x)
            dm |= d2
        waits.append(w)
        known_q[o["q"]] = (last, dm)
        l3, d3 = dict(last), set(dm)
        if o["dma"]:
            d3.add(i)
        else:
            l3[o["q"]] = i
        done.append((l3, d3))
    count, total = {}, {}
    for i, o in enumerate(ops):
        if o["dma"] and o["dma"] != "remote":
            total[o["dma"]] = total.get(o["dma"], 0) + 16
            count[i] = (o["dma"], total[o["dma"]])
        elif i in needed:
            s = "q" + o["q"]
            total[s] = total.get(s, 0) + 1
            count[i] = (s, total[s])
    waited, landed = {}, set()
    for i, o in enumerate(ops):
        e = eng[o["q"]]
        for s, c in [count[j] for j in waits[i]] + [x for x in o["ext"] if x not in landed]:
            e.wait_ge(T.sem[s], c)
            landed.add((s, c))
            waited[s] = max(waited.get(s, 0), c)
        ins = o["fn"]()
        if i in count:
            ins.then_inc(T.sem[count[i][0]], 16 if o["dma"] else 1)
    g.wait_ge(T.sem.sent, sent)
    for s, c in total.items():
        if waited.get(s, 0) < c:
            g.sync.wait_ge(T.sem[s], c)
